import numpy as np
import ml_dtypes


def mxq(x, axis, fmt="e4m3"):
    dtype, down = {"e4m3": (ml_dtypes.float8_e4m3fn, 7), "e5m2": (ml_dtypes.float8_e5m2, 14)}[fmt]
    v = np.moveaxis(np.asarray(x, np.float32).astype(ml_dtypes.bfloat16).astype(np.float64), axis, -1)
    blocks = v.reshape(v.shape[:-1] + (-1, 32))
    amax = np.abs(blocks).max(-1, keepdims=True)
    byte = np.maximum(np.where(amax > 0, np.frexp(amax)[1] - 1 + 127, 0) - down, 1)
    scale = np.exp2(byte - 127.0)
    codes = (blocks / scale).astype(np.float32).astype(dtype).astype(np.float64)
    return np.moveaxis((codes * scale).reshape(v.shape), -1, axis)


WIDE = False


def mx_kscale(k):
    if not WIDE:
        return np.ones(k)
    levels = np.array([10, -10, 5, -5, 0])
    if k % 512:
        return np.exp2(np.random.permutation(np.resize(levels, k // 32))).repeat(32)
    a = np.empty((k // 512, 16))
    for p in range(k // 512):
        a[p, :8] = np.random.permutation(np.resize(levels, 8))
        for g in range(8):
            far = levels[np.abs(levels - a[p, g]) >= 10]
            a[p, g + 8] = far[np.random.randint(len(far))]
    return np.exp2(a.ravel()).repeat(32)


def f64(x):
    return np.asarray(x).astype(np.float64)


def striped(idx):
    return np.tile(idx.reshape(-1, 16).T, (8, 1)).astype(np.uint16)


def unstriped(offs):
    return offs[:16].T.reshape(-1).astype(np.int64)


E2M1 = np.array([0.0, 0.5, 1.0, 1.5, 2.0, 3.0, 4.0, 6.0, -0.0, -0.5, -1.0, -1.5, -2.0, -3.0, -4.0, -6.0])


def pack_weight(w, fmt):
    k, n = w.shape
    w = f64(np.asarray(w, np.float32).astype(ml_dtypes.bfloat16)).reshape(k // 32, 32, n)
    amax = np.abs(w).max(1)
    if fmt == "e4m3":
        byte = np.frexp(amax)[1] - 1 + 127 - 7
    else:
        mant, ex = np.frexp(amax / 6.0)
        byte = np.where(mant > 0.5, ex, ex - 1) + 127
    byte = np.clip(np.where(amax > 0, byte, 1), 1, 254)
    scaled = (w * np.exp2(127.0 - byte)[:, None, :]).reshape(k, n).astype(np.float32)
    by_word = np.ascontiguousarray(scaled.reshape(k // 512, 128, 4, n).transpose(0, 1, 3, 2))
    if fmt == "e4m3":
        words = by_word.astype(ml_dtypes.float8_e4m3fn).view(np.uint8)
    else:
        c = by_word.astype(ml_dtypes.float4_e2m1fn).view(np.uint8) & 0xF
        words = (c[..., 0::2] | (c[..., 1::2] << 4)).reshape(k // 512, 128, 2 * n)
    return np.ascontiguousarray(words), np.ascontiguousarray(byte.astype(np.uint8).reshape(k // 512, 16, n))


def unpack_weight(words, scales, fmt):
    g, _, n = scales.shape
    words = np.ascontiguousarray(words).reshape(g, 128, n, -1)
    if fmt == "e4m3":
        vals = words.view(ml_dtypes.float8_e4m3fn).astype(np.float64)
    else:
        nib = np.empty((g, 128, n, 4), np.uint8)
        nib[..., 0::2] = words & 0xF
        nib[..., 1::2] = words >> 4
        vals = E2M1[nib]
    vals = vals * np.repeat(np.exp2(scales.astype(np.float64) - 127.0), 8, axis=1)[..., None]
    return vals.transpose(0, 1, 3, 2).reshape(g * 512, n)


def gelu(v):
    return 0.5 * v * (1.0 + np.tanh(np.sqrt(2.0 / np.pi) * (v + 0.044715 * v**3)))


K, H, N, T, S = 1024, 1024, 512, 4096, 1024

def setup_inputs():
    n = np.random.standard_normal
    s = mx_kscale(K)[:, None]
    u = mx_kscale(H)[:, None]
    tab_words, tab_scales = pack_weight(n((K, T)) * s, "e4m3")
    wg_words, wg_scales = pack_weight(n((K, N)) / np.sqrt(K) / s, "e2m1")
    w2_words, w2_scales = pack_weight(1.5 * n((H, N)) / np.sqrt(H) / u, "e4m3")
    return {
        "tab_words": tab_words, "tab_scales": tab_scales,
        "offs": striped(np.random.permutation(T)[:S]),
        "w1": (n((K, H)) / np.sqrt(K) / s).astype(np.float32),
        "gain": (np.exp(0.3 * n(H)) * u[:, 0]).astype(np.float32),
        "wg_words": wg_words, "wg_scales": wg_scales,
        "bg": (0.5 * n(N)).astype(np.float32),
        "w2_words": w2_words, "w2_scales": w2_scales,
    }

def reference(tab_words, tab_scales, offs, w1, gain, wg_words, wg_scales, bg, w2_words, w2_scales):
    v = unpack_weight(tab_words, tab_scales, "e4m3")[:, unstriped(offs)]
    wg = unpack_weight(wg_words, wg_scales, "e2m1")
    w2 = unpack_weight(w2_words, w2_scales, "e4m3")
    m = mxq(f64(w1), 0, "e4m3").T @ v
    h = f64(gain)[:, None] * np.tanh(m)
    g = (wg.T @ v) + f64(bg)[:, None]
    gate = 1.0 / (1.0 + np.exp(-g))
    y = w2.T @ mxq(h, 0, "e4m3")
    return y * gate

@@ -1,0 +1,249 @@
+from contextlib import ExitStack
+
+import concourse.mybir as mybir
+
+K, H, N, T, S = 1024, 1024, 512, 4096, 1024
+FLOPS = 2 * S * (K * H + K * N + H * N)
+
+F32 = mybir.dt.float32
+BF16 = mybir.dt.bfloat16
+I32 = mybir.dt.int32
+U32 = mybir.dt.uint32
+U16 = mybir.dt.uint16
+U8 = mybir.dt.uint8
+E4M3X4 = mybir.dt.float8_e4m3fn_x4
+E2M1X4 = mybir.dt.float4_e2m1fn_x4
+ACT = mybir.ActivationFunctionType
+MULT = mybir.AluOpType.mult
+
+P = 128
+PACK = 4
+PASS = P * PACK
+PASSES = 2
+QUADS = 4
+BANK = 512
+CHUNKS = [(0, 256), (256, 256), (512, 256), (768, 128), (896, 128)]
+UNITS = [(0, 0), (0, 1), (0, 2), (1, 0), (1, 1), (0, 3), (0, 4), (1, 2), (1, 3), (1, 4)]
+VECTOR_SHARE = 84
+
+
+def tile_list_gated_edge_messages_kernel(
+    tc, tab_words, tab_scales, offs, w1, gain, wg_words, wg_scales, bg, w2_words, w2_scales, out
+):
+    nc = tc.nc
+    with ExitStack() as ctx:
+        keep = ctx.enter_context(tc.tile_pool(name="keep", bufs=1))
+        ring = ctx.enter_context(tc.tile_pool(name="ring", bufs=4))
+        stage = ctx.enter_context(tc.tile_pool(name="stage", bufs=2))
+        psum = ctx.enter_context(tc.psum_pool(name="psum", bufs=4))
+
+        offsets = keep.tile([P, S // 16], U16, name="offsets")
+        nc.sync.dma_start(offsets[:], offs)
+
+        tab_plane = keep.tile([P, T // 4], I32, name="tab_plane", align_bytes=64)
+        w_planes = keep.tile([P, 2 * PASSES, N // 4], I32, name="w_planes", align_bytes=64)
+        v_scales_low = keep.tile([P, S // 4], I32, name="v_scales_low", align_bytes=64)
+        nc.gpsimd.memset(tab_plane[:], 0)
+        nc.vector.memset(w_planes[:], 0)
+        nc.vector.memset(v_scales_low[:], 0)
+        for q in range(QUADS):
+            nc.gpsimd.dma_start(
+                tab_plane[32 * q : 32 * q + 8, :], tab_scales[:, 4 * q : 4 * q + 4, :].bitcast(I32)
+            )
+
+        table = [keep.tile([P, T], I32, name=f"table{a}", align_bytes=64) for a in range(PASSES)]
+        wg = keep.tile([P, PASSES, 2 * N], U8, name="wg", align_bytes=64)
+        w2 = keep.tile([P, PASSES, N], I32, name="w2", align_bytes=64)
+        raw = {}
+        nc.sync.dma_start(table[0][:], tab_words[0].rearrange("p t i -> p (t i)").bitcast(I32))
+        nc.sync.dma_start(wg[:].bitcast(I32), wg_words.bitcast(I32).rearrange("a p n -> p a n"))
+        bias = keep.tile([P, N // P], F32, name="bias")
+        gains = keep.tile([P, PASSES, PACK], F32, name="gains")
+        for q in range(QUADS):
+            nc.sync.dma_start(
+                w_planes[32 * q : 32 * q + 4, 0:PASSES, :],
+                wg_scales[:, 4 * q : 4 * q + 4, :].bitcast(I32).rearrange("a r n -> r a n"),
+            )
+        with nc.allow_non_contiguous_dma(reason="one bias value a partition"):
+            nc.sync.dma_start(bias[:], bg.rearrange("(i p) -> p i", p=P))
+        nc.sync.dma_start(table[1][:], tab_words[1].rearrange("p t i -> p (t i)").bitcast(I32))
+
+        def load_w1(b, a):
+            raw[b, a] = stage.tile([P, PACK, PASS], F32, name="raw")
+            rows = w1[a * PASS : (a + 1) * PASS, b * PASS : (b + 1) * PASS]
+            nc.sync.dma_start(raw[b, a][:], rows.rearrange("(p j) c -> p j c", j=PACK))
+
+        for a in range(PASSES):
+            load_w1(0, a)
+        nc.sync.dma_start(gains[:], gain.rearrange("(b p t) -> p b t", p=P, t=PACK))
+        nc.sync.dma_start(
+            w2[:], w2_words.rearrange("a p n i -> a p (n i)").bitcast(I32).rearrange("a p n -> p a n")
+        )
+        for q in range(QUADS):
+            nc.sync.dma_start(
+                w_planes[32 * q : 32 * q + 4, PASSES : 2 * PASSES, :],
+                w2_scales[:, 4 * q : 4 * q + 4, :].bitcast(I32).rearrange("a r n -> r a n"),
+            )
+
+        v_words = keep.tile([P, PASSES, S], U32, name="v_words", align_bytes=64)
+        v_scales = keep.tile([P, S], U8, name="v_scales", align_bytes=64)
+        nc.vector.tensor_copy(v_scales[:], tab_plane[:].bitcast(U8).indirect(offsets[:]))
+        nc.gpsimd.dma_start(v_scales_low[0:100, :], v_scales[4:104, :].bitcast(I32))
+        nc.vector.tensor_copy(v_words[:, 0, :], table[0][:].bitcast(U32).indirect(offsets[:]))
+        for half in range(2):
+            nc.vector.tensor_copy(
+                v_words[:, 1, half * BANK : (half + 1) * BANK],
+                table[1][:].bitcast(U32).indirect(offsets[:, half * 32 : (half + 1) * 32]),
+            )
+
+        gate = keep.tile([P, N // P, S], F32, name="gate")
+        gate_planes = [v_scales[:], v_scales_low[:].bitcast(U8)]
+
+        def gate_half(half):
+            edges = slice(half * BANK, (half + 1) * BANK)
+            for i in range(N // P):
+                acc = psum.tile([P, BANK], F32, name="acc_out")
+                for a in range(PASSES):
+                    nc.tensor.matmul_mx(
+                        out=acc[:],
+                        lhsT=wg[:, a, 2 * P * i : 2 * P * (i + 1)].bitcast(E2M1X4),
+                        lhsT_scale=w_planes[:, a, :].bitcast(U8)[:, P * i : P * (i + 1)],
+                        rhs=v_words[:, a, edges].bitcast(E4M3X4),
+                        rhs_scale=gate_planes[a][:, edges],
+                        start=(a == 0),
+                        stop=(a == PASSES - 1),
+                    )
+                nc.scalar.activation(gate[:, i, edges], acc[:], ACT.Sigmoid, bias=bias[:, i : i + 1])
+
+        w1_words = keep.tile([P, PASSES, H], U32, name="w1_words", align_bytes=64)
+        w1_scales = keep.tile([P, PASSES, H], U8, name="w1_scales", align_bytes=64)
+        grouped = {
+            key: keep.tile([P, PACK, P, PACK], BF16, name=f"grouped{key[0]}{key[1]}", align_bytes=64)
+            for key in [(b, a) for b in range(PASSES) for a in range(PASSES)]
+        }
+
+        def cast_views(b, a, m0, m1):
+            dst = grouped[b, a][:, :, m0:m1, :].rearrange("p t m j -> p m j t")
+            src = raw[b, a][:, :, PACK * m0 : PACK * m1].rearrange("p j (m t) -> p m j t", t=PACK)
+            return dst, src
+
+        def cast_on_vector(b, a, m0, m1):
+            nc.vector.tensor_copy(*cast_views(b, a, m0, m1))
+
+        def cast_on_scalar(b, a, m0, m1):
+            nc.scalar.copy(*cast_views(b, a, m0, m1))
+
+        def quantize_w1(b, a):
+            cols = slice(b * PASS, (b + 1) * PASS)
+            nc.vector.quantize_mx(
+                out=w1_words[:, a, cols].bitcast(E4M3X4),
+                scales=w1_scales[:, a, cols],
+                in_=grouped[b, a][:].rearrange("p t m j -> p (t m j)"),
+            )
+
+        h_words = keep.tile([P, PASSES, S], U32, name="h_words", align_bytes=64)
+        h_scales = keep.tile([P, PASSES, S], U8, name="h_scales", align_bytes=64)
+        tanh_of = {}
+        h_of = {}
+        y_of = {}
+
+        def first_layer(b, c):
+            start, width = CHUNKS[c]
+            th = ring.tile([P, width, PACK], F32, name="th")
+            tanh_of[b, c] = th
+            for j0 in range(0, width, P):
+                edges = slice(start + j0, start + j0 + P)
+                acc = psum.tile([P, PACK, P], F32, name="acc_m")
+                for t in range(PACK):
+                    cols = slice(b * PASS + t * P, b * PASS + (t + 1) * P)
+                    for a in range(PASSES):
+                        nc.tensor.matmul_mx(
+                            out=acc[:, t, :],
+                            lhsT=w1_words[:, a, cols].bitcast(E4M3X4),
+                            lhsT_scale=w1_scales[:, a, cols],
+                            rhs=v_words[:, a, edges].bitcast(E4M3X4),
+                            rhs_scale=v_scales[4 * a :, edges],
+                            start=(a == 0),
+                            stop=(a == PASSES - 1),
+                        )
+                nc.scalar.activation(th[:, j0 : j0 + P, :], acc[:].rearrange("p t j -> p j t"), ACT.Tanh)
+
+        def apply_gain(b, c):
+            width = CHUNKS[c][1]
+            hb = ring.tile([P, width, PACK], BF16, name="hb", align_bytes=64)
+            h_of[b, c] = hb
+            factor = gains[:, b : b + 1, :].to_broadcast([P, width, PACK])
+            nc.vector.tensor_tensor(hb[:], tanh_of[b, c][:], factor, MULT)
+
+        def quantize_h(b, c):
+            start, width = CHUNKS[c]
+            edges = slice(start, start + width)
+            nc.vector.quantize_mx(
+                out=h_words[:, b, edges].bitcast(E4M3X4),
+                scales=h_scales[:, b, edges],
+                in_=h_of[b, c][:].rearrange("p j t -> p (j t)"),
+            )
+
+        def second_layer(c):
+            start, width = CHUNKS[c]
+            edges = slice(start, start + width)
+            per_bank = BANK // width
+            y_of[c] = []
+            for i0 in range(0, N // P, per_bank):
+                acc = psum.tile([P, per_bank, width], F32, name="acc_out")
+                y_of[c].append((i0, acc))
+                for i in range(i0, i0 + per_bank):
+                    cols = slice(P * i, P * (i + 1))
+                    for b in range(PASSES):
+                        nc.tensor.matmul_mx(
+                            out=acc[:, i - i0, :],
+                            lhsT=w2[:, b, cols].bitcast(E4M3X4),
+                            lhsT_scale=w_planes[:, PASSES + b, :].bitcast(U8)[:, cols],
+                            rhs=h_words[:, b, edges].bitcast(E4M3X4),
+                            rhs_scale=h_scales[:, b, edges],
+                            start=(b == 0),
+                            stop=(b == PASSES - 1),
+                        )
+
+        out_view = out.rearrange("(i p) j -> p i j", p=P)
+
+        def gate_and_store(c):
+            start, width = CHUNKS[c]
+            edges = slice(start, start + width)
+            per_bank = BANK // width
+            for i0, acc in y_of[c]:
+                result = ring.tile([P, per_bank, width], F32, name="result")
+                nc.vector.tensor_tensor(result[:], acc[:], gate[:, i0 : i0 + per_bank, edges], MULT)
+                nc.sync.dma_start(out_view[:, i0 : i0 + per_bank, edges], result[:])
+
+        def cast_shared(b, a):
+            cast_on_vector(b, a, 0, VECTOR_SHARE)
+            cast_on_scalar(b, a, VECTOR_SHARE, P)
+            quantize_w1(b, a)
+
+        gate_half(0)
+        for a in range(PASSES):
+            cast_on_vector(0, a, 0, P)
+            load_w1(1, a)
+            quantize_w1(0, a)
+
+        for step in range(len(UNITS) + 3):
+            if step < len(UNITS):
+                first_layer(*UNITS[step])
+            if step == 3:
+                gate_half(1)
+            if step < 2:
+                for m0 in range(64 * step, 64 * step + 64, 32):
+                    cast_on_scalar(1, 0, m0, m0 + 32)
+            if 0 <= step - 1 < len(UNITS):
+                apply_gain(*UNITS[step - 1])
+            if step == 1:
+                quantize_w1(1, 0)
+            if step == 2:
+                cast_shared(1, 1)
+            if 0 <= step - 2 < len(UNITS):
+                quantize_h(*UNITS[step - 2])
+                if UNITS[step - 2][0] == PASSES - 1:
+                    second_layer(UNITS[step - 2][1])
+            if 0 <= step - 3 < len(UNITS) and UNITS[step - 3][0] == PASSES - 1:
+                gate_and_store(UNITS[step - 3][1])

@@ -24,7 +24,7 @@ QUADS = 4
 BANK = 512
 CHUNKS = [(0, 256), (256, 256), (512, 256), (768, 128), (896, 128)]
 UNITS = [(0, 0), (0, 1), (0, 2), (1, 0), (1, 1), (0, 3), (0, 4), (1, 2), (1, 3), (1, 4)]
-VECTOR_SHARE = 84
+GAIN_ON_SCALAR = []
 
 
 def tile_list_gated_edge_messages_kernel(
@@ -34,86 +34,49 @@ def tile_list_gated_edge_messages_kernel(
     with ExitStack() as ctx:
         keep = ctx.enter_context(tc.tile_pool(name="keep", bufs=1))
         ring = ctx.enter_context(tc.tile_pool(name="ring", bufs=4))
-        stage = ctx.enter_context(tc.tile_pool(name="stage", bufs=2))
+        stream = ctx.enter_context(tc.tile_pool(name="stream", bufs=3))
         psum = ctx.enter_context(tc.psum_pool(name="psum", bufs=4))
 
         offsets = keep.tile([P, S // 16], U16, name="offsets")
         nc.sync.dma_start(offsets[:], offs)
 
-        tab_plane = keep.tile([P, T // 4], I32, name="tab_plane", align_bytes=64)
+        tab_planes = keep.tile([P, PASSES, T // 4], I32, name="tab_planes", align_bytes=64)
         w_planes = keep.tile([P, 2 * PASSES, N // 4], I32, name="w_planes", align_bytes=64)
-        v_scales_low = keep.tile([P, S // 4], I32, name="v_scales_low", align_bytes=64)
-        nc.gpsimd.memset(tab_plane[:], 0)
+        nc.vector.memset(tab_planes[:], 0)
         nc.vector.memset(w_planes[:], 0)
-        nc.vector.memset(v_scales_low[:], 0)
-        for q in range(QUADS):
-            nc.gpsimd.dma_start(
-                tab_plane[32 * q : 32 * q + 8, :], tab_scales[:, 4 * q : 4 * q + 4, :].bitcast(I32)
-            )
+        warm = keep.tile([P, 2], F32, name="warm")
+        nc.vector.memset(warm[:, 0:1], 0)
+        nc.scalar.activation(warm[:, 1:2], warm[:, 0:1], ACT.Sigmoid)
 
-        table = [keep.tile([P, T], I32, name=f"table{a}", align_bytes=64) for a in range(PASSES)]
-        wg = keep.tile([P, PASSES, 2 * N], U8, name="wg", align_bytes=64)
-        w2 = keep.tile([P, PASSES, N], I32, name="w2", align_bytes=64)
+        def load_planes(planes, scales):
+            rows = scales.bitcast(I32).rearrange("a (q r) n -> r q a n", r=4)
+            for r in range(4):
+                nc.sync.dma_start(planes[r:P:32], rows[r])
+
+        def load_table(a):
+            words = stream.tile([P, T], I32, name="stream", align_bytes=64)
+            nc.sync.dma_start(words[:], tab_words[a].rearrange("p t i -> p (t i)").bitcast(I32))
+            return words
+
         raw = {}
-        nc.sync.dma_start(table[0][:], tab_words[0].rearrange("p t i -> p (t i)").bitcast(I32))
-        nc.sync.dma_start(wg[:].bitcast(I32), wg_words.bitcast(I32).rearrange("a p n -> p a n"))
+
+        def load_w1(b, a, pieces=1):
+            raw[b, a] = stream.tile([P, PACK, PASS], F32, name="stream", align_bytes=64)
+            rows = w1[a * PASS : (a + 1) * PASS, b * PASS : (b + 1) * PASS].rearrange("(p j) c -> p j c", j=PACK)
+            width = PASS // pieces
+            for c0 in range(0, PASS, width):
+                nc.sync.dma_start(raw[b, a][:, :, c0 : c0 + width], rows[:, :, c0 : c0 + width])
+
+        wg = keep.tile([P, PASSES, 2 * N], U8, name="wg", align_bytes=64)
         bias = keep.tile([P, N // P], F32, name="bias")
         gains = keep.tile([P, PASSES, PACK], F32, name="gains")
-        for q in range(QUADS):
-            nc.sync.dma_start(
-                w_planes[32 * q : 32 * q + 4, 0:PASSES, :],
-                wg_scales[:, 4 * q : 4 * q + 4, :].bitcast(I32).rearrange("a r n -> r a n"),
-            )
+        load_w1(0, 0)
+        load_planes(tab_planes, tab_scales)
+        table = [load_table(a) for a in range(PASSES)]
+        nc.sync.dma_start(wg[:].bitcast(I32), wg_words.bitcast(I32).rearrange("a p n -> p a n"))
+        load_planes(w_planes[:, 0:PASSES, :], wg_scales)
         with nc.allow_non_contiguous_dma(reason="one bias value a partition"):
             nc.sync.dma_start(bias[:], bg.rearrange("(i p) -> p i", p=P))
-        nc.sync.dma_start(table[1][:], tab_words[1].rearrange("p t i -> p (t i)").bitcast(I32))
-
-        def load_w1(b, a):
-            raw[b, a] = stage.tile([P, PACK, PASS], F32, name="raw")
-            rows = w1[a * PASS : (a + 1) * PASS, b * PASS : (b + 1) * PASS]
-            nc.sync.dma_start(raw[b, a][:], rows.rearrange("(p j) c -> p j c", j=PACK))
-
-        for a in range(PASSES):
-            load_w1(0, a)
-        nc.sync.dma_start(gains[:], gain.rearrange("(b p t) -> p b t", p=P, t=PACK))
-        nc.sync.dma_start(
-            w2[:], w2_words.rearrange("a p n i -> a p (n i)").bitcast(I32).rearrange("a p n -> p a n")
-        )
-        for q in range(QUADS):
-            nc.sync.dma_start(
-                w_planes[32 * q : 32 * q + 4, PASSES : 2 * PASSES, :],
-                w2_scales[:, 4 * q : 4 * q + 4, :].bitcast(I32).rearrange("a r n -> r a n"),
-            )
-
-        v_words = keep.tile([P, PASSES, S], U32, name="v_words", align_bytes=64)
-        v_scales = keep.tile([P, S], U8, name="v_scales", align_bytes=64)
-        nc.vector.tensor_copy(v_scales[:], tab_plane[:].bitcast(U8).indirect(offsets[:]))
-        nc.gpsimd.dma_start(v_scales_low[0:100, :], v_scales[4:104, :].bitcast(I32))
-        nc.vector.tensor_copy(v_words[:, 0, :], table[0][:].bitcast(U32).indirect(offsets[:]))
-        for half in range(2):
-            nc.vector.tensor_copy(
-                v_words[:, 1, half * BANK : (half + 1) * BANK],
-                table[1][:].bitcast(U32).indirect(offsets[:, half * 32 : (half + 1) * 32]),
-            )
-
-        gate = keep.tile([P, N // P, S], F32, name="gate")
-        gate_planes = [v_scales[:], v_scales_low[:].bitcast(U8)]
-
-        def gate_half(half):
-            edges = slice(half * BANK, (half + 1) * BANK)
-            for i in range(N // P):
-                acc = psum.tile([P, BANK], F32, name="acc_out")
-                for a in range(PASSES):
-                    nc.tensor.matmul_mx(
-                        out=acc[:],
-                        lhsT=wg[:, a, 2 * P * i : 2 * P * (i + 1)].bitcast(E2M1X4),
-                        lhsT_scale=w_planes[:, a, :].bitcast(U8)[:, P * i : P * (i + 1)],
-                        rhs=v_words[:, a, edges].bitcast(E4M3X4),
-                        rhs_scale=gate_planes[a][:, edges],
-                        start=(a == 0),
-                        stop=(a == PASSES - 1),
-                    )
-                nc.scalar.activation(gate[:, i, edges], acc[:], ACT.Sigmoid, bias=bias[:, i : i + 1])
 
         w1_words = keep.tile([P, PASSES, H], U32, name="w1_words", align_bytes=64)
         w1_scales = keep.tile([P, PASSES, H], U8, name="w1_scales", align_bytes=64)
@@ -141,6 +104,42 @@ def tile_list_gated_edge_messages_kernel(
                 in_=grouped[b, a][:].rearrange("p t m j -> p (t m j)"),
             )
 
+        cast_on_vector(0, 0, 0, P)
+        quantize_w1(0, 0)
+        load_w1(0, 1, pieces=2)
+        nc.sync.dma_start(gains[:], gain.rearrange("(b p t) -> p b t", p=P, t=PACK))
+
+        v_words = keep.tile([P, PASSES, S], U32, name="v_words", align_bytes=64)
+        v_scales = keep.tile([P, PASSES, S], U8, name="v_scales", align_bytes=64)
+        for a in range(PASSES):
+            nc.vector.tensor_copy(v_scales[:, a, :], tab_planes[:, a, :].bitcast(U8).indirect(offsets[:]))
+        nc.vector.tensor_copy(v_words[:, 0, :], table[0][:].bitcast(U32).indirect(offsets[:]))
+        load_w1(1, 0)
+        for half in range(2):
+            nc.vector.tensor_copy(
+                v_words[:, 1, half * BANK : (half + 1) * BANK],
+                table[1][:].bitcast(U32).indirect(offsets[:, half * 32 : (half + 1) * 32]),
+            )
+        load_w1(1, 1)
+
+        gate = keep.tile([P, N // P, S], F32, name="gate")
+
+        def gate_half(half):
+            edges = slice(half * BANK, (half + 1) * BANK)
+            for i in range(N // P):
+                acc = psum.tile([P, BANK], F32, name="acc_out")
+                for a in range(PASSES):
+                    nc.tensor.matmul_mx(
+                        out=acc[:],
+                        lhsT=wg[:, a, 2 * P * i : 2 * P * (i + 1)].bitcast(E2M1X4),
+                        lhsT_scale=w_planes[:, a, :].bitcast(U8)[:, P * i : P * (i + 1)],
+                        rhs=v_words[:, a, edges].bitcast(E4M3X4),
+                        rhs_scale=v_scales[:, a, edges],
+                        start=(a == 0),
+                        stop=(a == PASSES - 1),
+                    )
+                nc.scalar.activation(gate[:, i, edges], acc[:], ACT.Sigmoid, bias=bias[:, i : i + 1])
+
         h_words = keep.tile([P, PASSES, S], U32, name="h_words", align_bytes=64)
         h_scales = keep.tile([P, PASSES, S], U8, name="h_scales", align_bytes=64)
         tanh_of = {}
@@ -149,31 +148,42 @@ def tile_list_gated_edge_messages_kernel(
 
         def first_layer(b, c):
             start, width = CHUNKS[c]
-            th = ring.tile([P, width, PACK], F32, name="th")
+            edges = slice(start, start + width)
+            per_bank = BANK // width
+            th = ring.tile([P, PACK, width], F32, name="th")
             tanh_of[b, c] = th
-            for j0 in range(0, width, P):
-                edges = slice(start + j0, start + j0 + P)
-                acc = psum.tile([P, PACK, P], F32, name="acc_m")
-                for t in range(PACK):
+            for t0 in range(0, PACK, per_bank):
+                acc = psum.tile([P, per_bank, width], F32, name="acc_m")
+                for t in range(t0, t0 + per_bank):
                     cols = slice(b * PASS + t * P, b * PASS + (t + 1) * P)
                     for a in range(PASSES):
                         nc.tensor.matmul_mx(
-                            out=acc[:, t, :],
+                            out=acc[:, t - t0, :],
                             lhsT=w1_words[:, a, cols].bitcast(E4M3X4),
                             lhsT_scale=w1_scales[:, a, cols],
                             rhs=v_words[:, a, edges].bitcast(E4M3X4),
-                            rhs_scale=v_scales[4 * a :, edges],
+                            rhs_scale=v_scales[:, a, edges],
                             start=(a == 0),
                             stop=(a == PASSES - 1),
                         )
-                nc.scalar.activation(th[:, j0 : j0 + P, :], acc[:].rearrange("p t j -> p j t"), ACT.Tanh)
+                nc.scalar.activation(th[:, t0 : t0 + per_bank, :], acc[:], ACT.Tanh)
+            if (b, c) in GAIN_ON_SCALAR:
+                rows = ring.tile([P, PACK, width], BF16, name="rows")
+                for t in range(PACK):
+                    nc.scalar.activation(rows[:, t, :], th[:, t, :], ACT.Copy, scale=gains[:, b, t : t + 1])
+                tanh_of[b, c] = rows
 
         def apply_gain(b, c):
             width = CHUNKS[c][1]
             hb = ring.tile([P, width, PACK], BF16, name="hb", align_bytes=64)
             h_of[b, c] = hb
-            factor = gains[:, b : b + 1, :].to_broadcast([P, width, PACK])
-            nc.vector.tensor_tensor(hb[:], tanh_of[b, c][:], factor, MULT)
+            dst = hb[:].rearrange("p (c i) t -> p c t i", i=4)
+            src = tanh_of[b, c][:].rearrange("p t (c i) -> p c t i", i=4)
+            if (b, c) in GAIN_ON_SCALAR:
+                nc.vector.tensor_copy(dst, src)
+            else:
+                factor = gains[:, b : b + 1, :].unsqueeze(3).to_broadcast([P, width // 4, PACK, 4])
+                nc.vector.tensor_tensor(dst, src, factor, MULT)
 
         def quantize_h(b, c):
             start, width = CHUNKS[c]
@@ -216,33 +226,32 @@ def tile_list_gated_edge_messages_kernel(
                 nc.vector.tensor_tensor(result[:], acc[:], gate[:, i0 : i0 + per_bank, edges], MULT)
                 nc.sync.dma_start(out_view[:, i0 : i0 + per_bank, edges], result[:])
 
-        def cast_shared(b, a):
-            cast_on_vector(b, a, 0, VECTOR_SHARE)
-            cast_on_scalar(b, a, VECTOR_SHARE, P)
-            quantize_w1(b, a)
-
         gate_half(0)
-        for a in range(PASSES):
-            cast_on_vector(0, a, 0, P)
-            load_w1(1, a)
-            quantize_w1(0, a)
+        cast_on_vector(0, 1, 0, P // 2)
+        cast_on_vector(0, 1, P // 2, P)
+        w2 = stream.tile([P, PASSES, N], I32, name="stream", align_bytes=64)
+        nc.sync.dma_start(
+            w2[:], w2_words.rearrange("a p n i -> a p (n i)").bitcast(I32).rearrange("a p n -> p a n")
+        )
+        load_planes(w_planes[:, PASSES : 2 * PASSES, :], w2_scales)
+        quantize_w1(0, 1)
+        cast_on_vector(1, 0, 0, P)
+        quantize_w1(1, 0)
 
         for step in range(len(UNITS) + 3):
             if step < len(UNITS):
                 first_layer(*UNITS[step])
-            if step == 3:
+            if step == 7:
                 gate_half(1)
-            if step < 2:
-                for m0 in range(64 * step, 64 * step + 64, 32):
-                    cast_on_scalar(1, 0, m0, m0 + 32)
+            if step == 1:
+                for m0 in range(0, P, 64):
+                    cast_on_scalar(1, 1, m0, m0 + 64)
             if 0 <= step - 1 < len(UNITS):
                 apply_gain(*UNITS[step - 1])
-            if step == 1:
-                quantize_w1(1, 0)
-            if step == 2:
-                cast_shared(1, 1)
             if 0 <= step - 2 < len(UNITS):
                 quantize_h(*UNITS[step - 2])
+                if step == 2:
+                    quantize_w1(1, 1)
                 if UNITS[step - 2][0] == PASSES - 1:
                     second_layer(UNITS[step - 2][1])
             if 0 <= step - 3 < len(UNITS) and UNITS[step - 3][0] == PASSES - 1:

@@ -1,6 +1,7 @@
 from contextlib import ExitStack
 
 import concourse.mybir as mybir
+from concourse.masks import make_identity
 
 K, H, N, T, S = 1024, 1024, 512, 4096, 1024
 FLOPS = 2 * S * (K * H + K * N + H * N)
@@ -24,7 +25,7 @@ QUADS = 4
 BANK = 512
 CHUNKS = [(0, 256), (256, 256), (512, 256), (768, 128), (896, 128)]
 UNITS = [(0, 0), (0, 1), (0, 2), (1, 0), (1, 1), (0, 3), (0, 4), (1, 2), (1, 3), (1, 4)]
-GAIN_ON_SCALAR = []
+GAIN_ON_SCALAR = [(1, 1), (0, 3), (0, 4), (1, 2)]
 
 
 def tile_list_gated_edge_messages_kernel(
@@ -34,49 +35,59 @@ def tile_list_gated_edge_messages_kernel(
     with ExitStack() as ctx:
         keep = ctx.enter_context(tc.tile_pool(name="keep", bufs=1))
         ring = ctx.enter_context(tc.tile_pool(name="ring", bufs=4))
-        stream = ctx.enter_context(tc.tile_pool(name="stream", bufs=3))
+        slots = ctx.enter_context(tc.tile_pool(name="slots", bufs=1))
         psum = ctx.enter_context(tc.psum_pool(name="psum", bufs=4))
 
         offsets = keep.tile([P, S // 16], U16, name="offsets")
         nc.sync.dma_start(offsets[:], offs)
 
-        tab_planes = keep.tile([P, PASSES, T // 4], I32, name="tab_planes", align_bytes=64)
-        w_planes = keep.tile([P, 2 * PASSES, N // 4], I32, name="w_planes", align_bytes=64)
-        nc.vector.memset(tab_planes[:], 0)
-        nc.vector.memset(w_planes[:], 0)
-        warm = keep.tile([P, 2], F32, name="warm")
-        nc.vector.memset(warm[:, 0:1], 0)
-        nc.scalar.activation(warm[:, 1:2], warm[:, 0:1], ACT.Sigmoid)
+        raw = {}
+
+        def load_w1(b, staged, pieces):
+            for a in range(PASSES):
+                raw[b, a] = staged[:, a * PACK * PASS : (a + 1) * PACK * PASS].rearrange("p (j c) -> p j c", j=PACK)
+                rows = w1[a * PASS : (a + 1) * PASS, b * PASS : (b + 1) * PASS].rearrange("(p j) c -> p j c", j=PACK)
+                width = PASS // pieces[a]
+                for c0 in range(0, PASS, width):
+                    nc.sync.dma_start(raw[b, a][:, :, c0 : c0 + width], rows[:, :, c0 : c0 + width])
+
+        def load_table(a, slot):
+            words = slots.tile([P, T], I32, name=slot, align_bytes=64)
+            nc.sync.dma_start(words[:], tab_words[a].rearrange("p t i -> p (t i)").bitcast(I32))
+            return words
 
         def load_planes(planes, scales):
             rows = scales.bitcast(I32).rearrange("a (q r) n -> r q a n", r=4)
             for r in range(4):
                 nc.sync.dma_start(planes[r:P:32], rows[r])
 
-        def load_table(a):
-            words = stream.tile([P, T], I32, name="stream", align_bytes=64)
-            nc.sync.dma_start(words[:], tab_words[a].rearrange("p t i -> p (t i)").bitcast(I32))
-            return words
+        tab_planes = slots.tile([P, T // 4], I32, name="slot_a", align_bytes=64)
+        v_scales_low = keep.tile([P, S // 4], I32, name="v_scales_low", align_bytes=64)
+        nc.vector.memset(tab_planes[:], 0)
+        wg = keep.tile([P, PASSES, N // 2], I32, name="wg", align_bytes=64)
+        wg_plane_words = keep.tile([P, PASSES, N // 4], I32, name="wg_plane_words", align_bytes=64)
+        wg_planes = wg_plane_words[:].bitcast(U8)
+        nc.vector.memset(wg_plane_words[:], 0)
+        nc.vector.memset(v_scales_low[:], 0)
+        warm = keep.tile([P, 2], F32, name="warm")
+        nc.vector.memset(warm[:, 0:1], 0)
+        nc.scalar.activation(warm[:, 1:2], warm[:, 0:1], ACT.Sigmoid)
 
-        raw = {}
-
-        def load_w1(b, a, pieces=1):
-            raw[b, a] = stream.tile([P, PACK, PASS], F32, name="stream", align_bytes=64)
-            rows = w1[a * PASS : (a + 1) * PASS, b * PASS : (b + 1) * PASS].rearrange("(p j) c -> p j c", j=PACK)
-            width = PASS // pieces
-            for c0 in range(0, PASS, width):
-                nc.sync.dma_start(raw[b, a][:, :, c0 : c0 + width], rows[:, :, c0 : c0 + width])
-
-        wg = keep.tile([P, PASSES, 2 * N], U8, name="wg", align_bytes=64)
         bias = keep.tile([P, N // P], F32, name="bias")
-        gains = keep.tile([P, PASSES, PACK], F32, name="gains")
-        load_w1(0, 0)
-        load_planes(tab_planes, tab_scales)
-        table = [load_table(a) for a in range(PASSES)]
-        nc.sync.dma_start(wg[:].bitcast(I32), wg_words.bitcast(I32).rearrange("a p n -> p a n"))
-        load_planes(w_planes[:, 0:PASSES, :], wg_scales)
-        with nc.allow_non_contiguous_dma(reason="one bias value a partition"):
-            nc.sync.dma_start(bias[:], bg.rearrange("(i p) -> p i", p=P))
+        bias_rows = keep.tile([P, P], F32, name="bias_rows")
+        identity = keep.tile([P, P], F32, name="identity")
+        nc.gpsimd.memset(bias_rows[:], 0.0)
+        make_identity(nc, identity[:])
+        nc.sync.dma_start(wg[:], wg_words.bitcast(I32).rearrange("a p n -> p a n"))
+        nc.sync.dma_start(bias_rows[0 : N // P, :], bg.rearrange("(i p) -> i p", p=P))
+        tab_rows = tab_scales.bitcast(I32).rearrange("a (q r) n -> r q a n", r=4)
+        for r in range(4):
+            nc.sync.dma_start(tab_planes[r:P:16, :], tab_rows[r])
+        table = [load_table(0, "table0"), load_table(1, "slot_b")]
+        load_planes(wg_plane_words, wg_scales)
+        bias_turned = psum.tile([P, P], F32, name="acc_m")
+        nc.tensor.transpose(bias_turned[:], bias_rows[:], identity[:])
+        nc.scalar.copy(bias[:], bias_turned[:, 0 : N // P])
 
         w1_words = keep.tile([P, PASSES, H], U32, name="w1_words", align_bytes=64)
         w1_scales = keep.tile([P, PASSES, H], U8, name="w1_scales", align_bytes=64)
@@ -104,25 +115,24 @@ def tile_list_gated_edge_messages_kernel(
                 in_=grouped[b, a][:].rearrange("p t m j -> p (t m j)"),
             )
 
-        cast_on_vector(0, 0, 0, P)
-        quantize_w1(0, 0)
-        load_w1(0, 1, pieces=2)
-        nc.sync.dma_start(gains[:], gain.rearrange("(b p t) -> p b t", p=P, t=PACK))
-
         v_words = keep.tile([P, PASSES, S], U32, name="v_words", align_bytes=64)
-        v_scales = keep.tile([P, PASSES, S], U8, name="v_scales", align_bytes=64)
-        for a in range(PASSES):
-            nc.vector.tensor_copy(v_scales[:, a, :], tab_planes[:, a, :].bitcast(U8).indirect(offsets[:]))
+        v_scales = keep.tile([P, S], U8, name="v_scales", align_bytes=64)
+        nc.vector.tensor_copy(v_scales[:], tab_planes[:].bitcast(U8).indirect(offsets[:]))
+        nc.sync.dma_start(v_scales_low[0:100, :], v_scales[16:116, :].bitcast(I32))
+        load_w1(0, slots.tile([P, PASSES * PACK * PASS], F32, name="slot_a", align_bytes=64), [1, 2])
         nc.vector.tensor_copy(v_words[:, 0, :], table[0][:].bitcast(U32).indirect(offsets[:]))
-        load_w1(1, 0)
         for half in range(2):
             nc.vector.tensor_copy(
                 v_words[:, 1, half * BANK : (half + 1) * BANK],
                 table[1][:].bitcast(U32).indirect(offsets[:, half * 32 : (half + 1) * 32]),
             )
-        load_w1(1, 1)
+        staged = slots.tile([P, PASSES * PACK * (PASS + 1)], F32, name="slot_b", align_bytes=64)
+        gains = staged[:, PASSES * PACK * PASS :].rearrange("p (b t) -> p b t", t=PACK)
+        nc.sync.dma_start(gains, gain.rearrange("(b p t) -> p b t", p=P, t=PACK))
+        load_w1(1, staged, [2, 1])
 
         gate = keep.tile([P, N // P, S], F32, name="gate")
+        gate_planes = [v_scales[:], v_scales_low[:].bitcast(U8)]
 
         def gate_half(half):
             edges = slice(half * BANK, (half + 1) * BANK)
@@ -131,10 +141,10 @@ def tile_list_gated_edge_messages_kernel(
                 for a in range(PASSES):
                     nc.tensor.matmul_mx(
                         out=acc[:],
-                        lhsT=wg[:, a, 2 * P * i : 2 * P * (i + 1)].bitcast(E2M1X4),
-                        lhsT_scale=w_planes[:, a, :].bitcast(U8)[:, P * i : P * (i + 1)],
+                        lhsT=wg[:, a, P * i // 2 : P * (i + 1) // 2].bitcast(E2M1X4),
+                        lhsT_scale=wg_planes[:, a, P * i : P * (i + 1)],
                         rhs=v_words[:, a, edges].bitcast(E4M3X4),
-                        rhs_scale=v_scales[:, a, edges],
+                        rhs_scale=gate_planes[a][:, edges],
                         start=(a == 0),
                         stop=(a == PASSES - 1),
                     )
@@ -146,44 +156,54 @@ def tile_list_gated_edge_messages_kernel(
         h_of = {}
         y_of = {}
 
+        def first_layer_passes(acc, b, t, edges):
+            cols = slice(b * PASS + t * P, b * PASS + (t + 1) * P)
+            for a in range(PASSES):
+                nc.tensor.matmul_mx(
+                    out=acc,
+                    lhsT=w1_words[:, a, cols].bitcast(E4M3X4),
+                    lhsT_scale=w1_scales[:, a, cols],
+                    rhs=v_words[:, a, edges].bitcast(E4M3X4),
+                    rhs_scale=gate_planes[a][:, edges],
+                    start=(a == 0),
+                    stop=(a == PASSES - 1),
+                )
+
         def first_layer(b, c):
             start, width = CHUNKS[c]
-            edges = slice(start, start + width)
-            per_bank = BANK // width
-            th = ring.tile([P, PACK, width], F32, name="th")
-            tanh_of[b, c] = th
-            for t0 in range(0, PACK, per_bank):
-                acc = psum.tile([P, per_bank, width], F32, name="acc_m")
-                for t in range(t0, t0 + per_bank):
-                    cols = slice(b * PASS + t * P, b * PASS + (t + 1) * P)
-                    for a in range(PASSES):
-                        nc.tensor.matmul_mx(
-                            out=acc[:, t - t0, :],
-                            lhsT=w1_words[:, a, cols].bitcast(E4M3X4),
-                            lhsT_scale=w1_scales[:, a, cols],
-                            rhs=v_words[:, a, edges].bitcast(E4M3X4),
-                            rhs_scale=v_scales[:, a, edges],
-                            start=(a == 0),
-                            stop=(a == PASSES - 1),
-                        )
-                nc.scalar.activation(th[:, t0 : t0 + per_bank, :], acc[:], ACT.Tanh)
             if (b, c) in GAIN_ON_SCALAR:
+                per_bank = BANK // width
+                th = ring.tile([P, PACK, width], F32, name="th")
+                for t0 in range(0, PACK, per_bank):
+                    acc = psum.tile([P, per_bank, width], F32, name="acc_m")
+                    for t in range(t0, t0 + per_bank):
+                        first_layer_passes(acc[:, t - t0, :], b, t, slice(start, start + width))
+                    nc.scalar.activation(th[:, t0 : t0 + per_bank, :], acc[:], ACT.Tanh)
                 rows = ring.tile([P, PACK, width], BF16, name="rows")
                 for t in range(PACK):
                     nc.scalar.activation(rows[:, t, :], th[:, t, :], ACT.Copy, scale=gains[:, b, t : t + 1])
                 tanh_of[b, c] = rows
+            else:
+                th = ring.tile([P, width, PACK], F32, name="th")
+                for j0 in range(0, width, P):
+                    acc = psum.tile([P, PACK, P], F32, name="acc_m")
+                    for t in range(PACK):
+                        first_layer_passes(acc[:, t, :], b, t, slice(start + j0, start + j0 + P))
+                    nc.scalar.activation(th[:, j0 : j0 + P, :], acc[:].rearrange("p t j -> p j t"), ACT.Tanh)
+                tanh_of[b, c] = th
 
         def apply_gain(b, c):
             width = CHUNKS[c][1]
             hb = ring.tile([P, width, PACK], BF16, name="hb", align_bytes=64)
             h_of[b, c] = hb
-            dst = hb[:].rearrange("p (c i) t -> p c t i", i=4)
-            src = tanh_of[b, c][:].rearrange("p t (c i) -> p c t i", i=4)
             if (b, c) in GAIN_ON_SCALAR:
-                nc.vector.tensor_copy(dst, src)
+                nc.vector.tensor_copy(
+                    hb[:].rearrange("p (c i) t -> p c t i", i=4),
+                    tanh_of[b, c][:].rearrange("p t (c i) -> p c t i", i=4),
+                )
             else:
-                factor = gains[:, b : b + 1, :].unsqueeze(3).to_broadcast([P, width // 4, PACK, 4])
-                nc.vector.tensor_tensor(dst, src, factor, MULT)
+                factor = gains[:, b : b + 1, :].to_broadcast([P, width, PACK])
+                nc.vector.tensor_tensor(hb[:], tanh_of[b, c][:], factor, MULT)
 
         def quantize_h(b, c):
             start, width = CHUNKS[c]
@@ -208,7 +228,7 @@ def tile_list_gated_edge_messages_kernel(
                         nc.tensor.matmul_mx(
                             out=acc[:, i - i0, :],
                             lhsT=w2[:, b, cols].bitcast(E4M3X4),
-                            lhsT_scale=w_planes[:, PASSES + b, :].bitcast(U8)[:, cols],
+                            lhsT_scale=w2_planes[:, b, cols],
                             rhs=h_words[:, b, edges].bitcast(E4M3X4),
                             rhs_scale=h_scales[:, b, edges],
                             start=(b == 0),
@@ -227,22 +247,26 @@ def tile_list_gated_edge_messages_kernel(
                 nc.sync.dma_start(out_view[:, i0 : i0 + per_bank, edges], result[:])
 
         gate_half(0)
+        gate_half(1)
+        cast_on_vector(0, 0, 0, P)
+        quantize_w1(0, 0)
         cast_on_vector(0, 1, 0, P // 2)
         cast_on_vector(0, 1, P // 2, P)
-        w2 = stream.tile([P, PASSES, N], I32, name="stream", align_bytes=64)
+        w2 = slots.tile([P, PASSES, N + N // 4], I32, name="slot_a", align_bytes=64)
+        w2_planes = w2[:, :, N:].bitcast(U8)
+        nc.gpsimd.memset(w2[:, :, N:], 0)
         nc.sync.dma_start(
-            w2[:], w2_words.rearrange("a p n i -> a p (n i)").bitcast(I32).rearrange("a p n -> p a n")
+            w2[:, :, 0:N], w2_words.rearrange("a p n i -> a p (n i)").bitcast(I32).rearrange("a p n -> p a n")
         )
-        load_planes(w_planes[:, PASSES : 2 * PASSES, :], w2_scales)
+        load_planes(w2[:, :, N:], w2_scales)
         quantize_w1(0, 1)
-        cast_on_vector(1, 0, 0, P)
+        cast_on_vector(1, 0, 0, P // 2)
+        cast_on_vector(1, 0, P // 2, P)
         quantize_w1(1, 0)
 
         for step in range(len(UNITS) + 3):
             if step < len(UNITS):
                 first_layer(*UNITS[step])
-            if step == 7:
-                gate_half(1)
             if step == 1:
                 for m0 in range(0, P, 64):
                     cast_on_scalar(1, 1, m0, m0 + 64)

@@ -23,9 +23,8 @@ PASS = P * PACK
 PASSES = 2
 QUADS = 4
 BANK = 512
-CHUNKS = [(0, 256), (256, 256), (512, 256), (768, 128), (896, 128)]
-UNITS = [(0, 0), (0, 1), (0, 2), (1, 0), (1, 1), (0, 3), (0, 4), (1, 2), (1, 3), (1, 4)]
-GAIN_ON_SCALAR = [(1, 1), (0, 3), (0, 4), (1, 2)]
+UNITS = [(0, j, 256) for j in range(0, S, 256)] + [(1, 0, 256), (1, 256, 256), (1, 512, 256), (1, 768, 128), (1, 896, 128)]
+GAIN_ON_SCALAR = UNITS[-3:-1]
 
 
 def tile_list_gated_edge_messages_kernel(
@@ -83,8 +82,9 @@ def tile_list_gated_edge_messages_kernel(
         tab_rows = tab_scales.bitcast(I32).rearrange("a (q r) n -> r q a n", r=4)
         for r in range(4):
             nc.sync.dma_start(tab_planes[r:P:16, :], tab_rows[r])
-        table = [load_table(0, "table0"), load_table(1, "slot_b")]
+        table = [load_table(0, "table0")]
         load_planes(wg_plane_words, wg_scales)
+        table.append(load_table(1, "slot_b"))
         bias_turned = psum.tile([P, P], F32, name="acc_m")
         nc.tensor.transpose(bias_turned[:], bias_rows[:], identity[:])
         nc.scalar.copy(bias[:], bias_turned[:, 0 : N // P])
@@ -169,9 +169,8 @@ def tile_list_gated_edge_messages_kernel(
                     stop=(a == PASSES - 1),
                 )
 
-        def first_layer(b, c):
-            start, width = CHUNKS[c]
-            if (b, c) in GAIN_ON_SCALAR:
+        def first_layer(b, start, width):
+            if (b, start, width) in GAIN_ON_SCALAR:
                 per_bank = BANK // width
                 th = ring.tile([P, PACK, width], F32, name="th")
                 for t0 in range(0, PACK, per_bank):
@@ -182,7 +181,7 @@ def tile_list_gated_edge_messages_kernel(
                 rows = ring.tile([P, PACK, width], BF16, name="rows")
                 for t in range(PACK):
                     nc.scalar.activation(rows[:, t, :], th[:, t, :], ACT.Copy, scale=gains[:, b, t : t + 1])
-                tanh_of[b, c] = rows
+                tanh_of[b, start] = rows
             else:
                 th = ring.tile([P, width, PACK], F32, name="th")
                 for j0 in range(0, width, P):
@@ -190,38 +189,35 @@ def tile_list_gated_edge_messages_kernel(
                     for t in range(PACK):
                         first_layer_passes(acc[:, t, :], b, t, slice(start + j0, start + j0 + P))
                     nc.scalar.activation(th[:, j0 : j0 + P, :], acc[:].rearrange("p t j -> p j t"), ACT.Tanh)
-                tanh_of[b, c] = th
+                tanh_of[b, start] = th
 
-        def apply_gain(b, c):
-            width = CHUNKS[c][1]
+        def apply_gain(b, start, width):
             hb = ring.tile([P, width, PACK], BF16, name="hb", align_bytes=64)
-            h_of[b, c] = hb
-            if (b, c) in GAIN_ON_SCALAR:
+            h_of[b, start] = hb
+            if (b, start, width) in GAIN_ON_SCALAR:
                 nc.vector.tensor_copy(
                     hb[:].rearrange("p (c i) t -> p c t i", i=4),
-                    tanh_of[b, c][:].rearrange("p t (c i) -> p c t i", i=4),
+                    tanh_of[b, start][:].rearrange("p t (c i) -> p c t i", i=4),
                 )
             else:
                 factor = gains[:, b : b + 1, :].to_broadcast([P, width, PACK])
-                nc.vector.tensor_tensor(hb[:], tanh_of[b, c][:], factor, MULT)
+                nc.vector.tensor_tensor(hb[:], tanh_of[b, start][:], factor, MULT)
 
-        def quantize_h(b, c):
-            start, width = CHUNKS[c]
+        def quantize_h(b, start, width):
             edges = slice(start, start + width)
             nc.vector.quantize_mx(
                 out=h_words[:, b, edges].bitcast(E4M3X4),
                 scales=h_scales[:, b, edges],
-                in_=h_of[b, c][:].rearrange("p j t -> p (j t)"),
+                in_=h_of[b, start][:].rearrange("p j t -> p (j t)"),
             )
 
-        def second_layer(c):
-            start, width = CHUNKS[c]
+        def second_layer(start, width):
             edges = slice(start, start + width)
             per_bank = BANK // width
-            y_of[c] = []
+            y_of[start] = []
             for i0 in range(0, N // P, per_bank):
                 acc = psum.tile([P, per_bank, width], F32, name="acc_out")
-                y_of[c].append((i0, acc))
+                y_of[start].append((i0, acc))
                 for i in range(i0, i0 + per_bank):
                     cols = slice(P * i, P * (i + 1))
                     for b in range(PASSES):
@@ -237,11 +233,10 @@ def tile_list_gated_edge_messages_kernel(
 
         out_view = out.rearrange("(i p) j -> p i j", p=P)
 
-        def gate_and_store(c):
-            start, width = CHUNKS[c]
+        def gate_and_store(start, width):
             edges = slice(start, start + width)
             per_bank = BANK // width
-            for i0, acc in y_of[c]:
+            for i0, acc in y_of[start]:
                 result = ring.tile([P, per_bank, width], F32, name="result")
                 nc.vector.tensor_tensor(result[:], acc[:], gate[:, i0 : i0 + per_bank, edges], MULT)
                 nc.sync.dma_start(out_view[:, i0 : i0 + per_bank, edges], result[:])
@@ -267,16 +262,16 @@ def tile_list_gated_edge_messages_kernel(
         for step in range(len(UNITS) + 3):
             if step < len(UNITS):
                 first_layer(*UNITS[step])
-            if step == 1:
+            if step == 2:
                 for m0 in range(0, P, 64):
                     cast_on_scalar(1, 1, m0, m0 + 64)
             if 0 <= step - 1 < len(UNITS):
                 apply_gain(*UNITS[step - 1])
             if 0 <= step - 2 < len(UNITS):
                 quantize_h(*UNITS[step - 2])
-                if step == 2:
+                if step == 3:
                     quantize_w1(1, 1)
                 if UNITS[step - 2][0] == PASSES - 1:
-                    second_layer(UNITS[step - 2][1])
+                    second_layer(*UNITS[step - 2][1:])
             if 0 <= step - 3 < len(UNITS) and UNITS[step - 3][0] == PASSES - 1:
-                gate_and_store(UNITS[step - 3][1])
+                gate_and_store(*UNITS[step - 3][1:])

@@ -21,10 +21,9 @@ P = 128
 PACK = 4
 PASS = P * PACK
 PASSES = 2
-QUADS = 4
 BANK = 512
-UNITS = [(0, j, 256) for j in range(0, S, 256)] + [(1, 0, 256), (1, 256, 256), (1, 512, 256), (1, 768, 128), (1, 896, 128)]
-GAIN_ON_SCALAR = UNITS[-3:-1]
+UNITS = [(0, 0, 128, 128), (0, 128, 128, 128), (0, 256, 256, 256), (0, 512, 256, 256), (0, 768, 256, 256), (1, 0, 256, 256), (1, 256, 256, 256), (1, 512, 256, -1), (1, 768, 128, -1), (1, 896, 128, 128)]
+CAST_ON_SCALAR = {2: (0, 64), 3: (64, 128)}
 
 
 def tile_list_gated_edge_messages_kernel(
@@ -73,21 +72,30 @@ def tile_list_gated_edge_messages_kernel(
         nc.scalar.activation(warm[:, 1:2], warm[:, 0:1], ACT.Sigmoid)
 
         bias = keep.tile([P, N // P], F32, name="bias")
-        bias_rows = keep.tile([P, P], F32, name="bias_rows")
+        gains = keep.tile([P, PASSES, PACK], F32, name="gains")
+        vec_rows = keep.tile([P, PASS], F32, name="vec_rows")
         identity = keep.tile([P, P], F32, name="identity")
-        nc.gpsimd.memset(bias_rows[:], 0.0)
+        nc.gpsimd.memset(vec_rows[:], 0.0)
         make_identity(nc, identity[:])
+        w2_plane_words = keep.tile([P, PASSES, N // 4], I32, name="w2_plane_words", align_bytes=64)
+        w2_planes = w2_plane_words[:].bitcast(U8)
+        nc.gpsimd.memset(w2_plane_words[:], 0)
         nc.sync.dma_start(wg[:], wg_words.bitcast(I32).rearrange("a p n -> p a n"))
-        nc.sync.dma_start(bias_rows[0 : N // P, :], bg.rearrange("(i p) -> i p", p=P))
+        nc.sync.dma_start(vec_rows[4 : 4 + N // P, 0:P], bg.rearrange("(i p) -> i p", p=P))
         tab_rows = tab_scales.bitcast(I32).rearrange("a (q r) n -> r q a n", r=4)
         for r in range(4):
             nc.sync.dma_start(tab_planes[r:P:16, :], tab_rows[r])
         table = [load_table(0, "table0")]
         load_planes(wg_plane_words, wg_scales)
         table.append(load_table(1, "slot_b"))
-        bias_turned = psum.tile([P, P], F32, name="acc_m")
-        nc.tensor.transpose(bias_turned[:], bias_rows[:], identity[:])
-        nc.scalar.copy(bias[:], bias_turned[:, 0 : N // P])
+        nc.sync.dma_start(vec_rows[0:PASSES, :], gain.rearrange("(b c) -> b c", b=PASSES))
+        bias_turned = psum.tile([P, P], F32, name="acc_m", bufs=4)
+        nc.tensor.transpose(bias_turned[:], vec_rows[:, 0:P], identity[:])
+        gains_turned = psum.tile([P, PACK, P], F32, name="acc_m", bufs=4)
+        for t in range(PACK):
+            nc.tensor.transpose(gains_turned[:, t, :], vec_rows[:, t:PASS:PACK], identity[:])
+        nc.scalar.copy(bias[:], bias_turned[:, 4 : 4 + N // P])
+        nc.scalar.copy(gains[:], gains_turned[:, :, 0:PASSES].rearrange("p t b -> p b t"))
 
         w1_words = keep.tile([P, PASSES, H], U32, name="w1_words", align_bytes=64)
         w1_scales = keep.tile([P, PASSES, H], U8, name="w1_scales", align_bytes=64)
@@ -126,10 +134,7 @@ def tile_list_gated_edge_messages_kernel(
                 v_words[:, 1, half * BANK : (half + 1) * BANK],
                 table[1][:].bitcast(U32).indirect(offsets[:, half * 32 : (half + 1) * 32]),
             )
-        staged = slots.tile([P, PASSES * PACK * (PASS + 1)], F32, name="slot_b", align_bytes=64)
-        gains = staged[:, PASSES * PACK * PASS :].rearrange("p (b t) -> p b t", t=PACK)
-        nc.sync.dma_start(gains, gain.rearrange("(b p t) -> p b t", p=P, t=PACK))
-        load_w1(1, staged, [2, 1])
+        load_w1(1, slots.tile([P, PASSES * PACK * PASS], F32, name="slot_b", align_bytes=64), [1, 1])
 
         gate = keep.tile([P, N // P, S], F32, name="gate")
         gate_planes = [v_scales[:], v_scales_low[:].bitcast(U8)]
@@ -169,41 +174,52 @@ def tile_list_gated_edge_messages_kernel(
                     stop=(a == PASSES - 1),
                 )
 
-        def first_layer(b, start, width):
-            if (b, start, width) in GAIN_ON_SCALAR:
-                per_bank = BANK // width
-                th = ring.tile([P, PACK, width], F32, name="th")
-                for t0 in range(0, PACK, per_bank):
-                    acc = psum.tile([P, per_bank, width], F32, name="acc_m")
-                    for t in range(t0, t0 + per_bank):
-                        first_layer_passes(acc[:, t - t0, :], b, t, slice(start, start + width))
-                    nc.scalar.activation(th[:, t0 : t0 + per_bank, :], acc[:], ACT.Tanh)
+        def first_layer(b, start, width, share):
+            block = min(width, 256 if share >= 0 else 256)
+            per_bank = BANK // block
+            groups = PACK // per_bank
+            th = ring.tile([P, groups, width * per_bank], F32, name="th", bufs=4)
+            for j0 in range(0, width, block):
+                for g in range(groups):
+                    acc = psum.tile([P, per_bank, block], F32, name="acc_m", bufs=4)
+                    for e in range(per_bank):
+                        first_layer_passes(acc[:, e, :], b, g * per_bank + e, slice(start + j0, start + j0 + block))
+                    if share < 0:
+                        dst = th[:, g, :].rearrange("p (e j) -> p e j", e=per_bank)[:, :, j0 : j0 + block]
+                        nc.scalar.activation(dst, acc[:], ACT.Tanh)
+                    else:
+                        dst = th[:, g, :].rearrange("p (j e) -> p j e", e=per_bank)[:, j0 : j0 + block, :]
+                        nc.scalar.activation(dst, acc[:].rearrange("p e j -> p j e"), ACT.Tanh)
+            if share < 0:
                 rows = ring.tile([P, PACK, width], BF16, name="rows")
+                by_t = th[:].rearrange("p g (e j) -> p (g e) j", e=per_bank)
                 for t in range(PACK):
-                    nc.scalar.activation(rows[:, t, :], th[:, t, :], ACT.Copy, scale=gains[:, b, t : t + 1])
+                    nc.scalar.activation(rows[:, t, :], by_t[:, t, :], ACT.Copy, scale=gains[:, b, t : t + 1])
                 tanh_of[b, start] = rows
             else:
-                th = ring.tile([P, width, PACK], F32, name="th")
-                for j0 in range(0, width, P):
-                    acc = psum.tile([P, PACK, P], F32, name="acc_m")
-                    for t in range(PACK):
-                        first_layer_passes(acc[:, t, :], b, t, slice(start + j0, start + j0 + P))
-                    nc.scalar.activation(th[:, j0 : j0 + P, :], acc[:].rearrange("p t j -> p j t"), ACT.Tanh)
                 tanh_of[b, start] = th
 
-        def apply_gain(b, start, width):
-            hb = ring.tile([P, width, PACK], BF16, name="hb", align_bytes=64)
+        def apply_gain(b, start, width, share):
+            hb = ring.tile([P, width, PACK], BF16, name="hb", align_bytes=64, bufs=4)
             h_of[b, start] = hb
-            if (b, start, width) in GAIN_ON_SCALAR:
+            if share < 0:
                 nc.vector.tensor_copy(
                     hb[:].rearrange("p (c i) t -> p c t i", i=4),
                     tanh_of[b, start][:].rearrange("p t (c i) -> p c t i", i=4),
                 )
-            else:
-                factor = gains[:, b : b + 1, :].to_broadcast([P, width, PACK])
-                nc.vector.tensor_tensor(hb[:], tanh_of[b, start][:], factor, MULT)
+                return
+            per_bank = BANK // min(width, 256 if share >= 0 else 256)
+            src = tanh_of[b, start][:].rearrange("p g (j e) -> p j g e", e=per_bank)
+            dst = hb[:].rearrange("p j (g e) -> p j g e", e=per_bank)
+            for engine, j0, j1, factor in (
+                (nc.vector, 0, share, gains[:, b, :]),
+            ) + tuple((nc.gpsimd, j, min(j + 64, width), gains[:, b, :]) for j in range(share, width, 64)):
+                if j1 > j0:
+                    factor = factor.rearrange("p (g e) -> p g e", e=per_bank).unsqueeze(1)
+                    factor = factor.to_broadcast([P, j1 - j0, PACK // per_bank, per_bank])
+                    engine.tensor_tensor(dst[:, j0:j1], src[:, j0:j1], factor, MULT)
 
-        def quantize_h(b, start, width):
+        def quantize_h(b, start, width, share):
             edges = slice(start, start + width)
             nc.vector.quantize_mx(
                 out=h_words[:, b, edges].bitcast(E4M3X4),
@@ -211,32 +227,36 @@ def tile_list_gated_edge_messages_kernel(
                 in_=h_of[b, start][:].rearrange("p j t -> p (j t)"),
             )
 
-        def second_layer(start, width):
+        def second_layer_pass(acc, i, b, edges):
+            cols = slice(P * i, P * (i + 1))
+            nc.tensor.matmul_mx(
+                out=acc,
+                lhsT=w2[:, b, cols].bitcast(E4M3X4),
+                lhsT_scale=w2_planes[:, b, cols],
+                rhs=h_words[:, b, edges].bitcast(E4M3X4),
+                rhs_scale=h_scales[:, b, edges],
+                start=(b == 0),
+                stop=(b == PASSES - 1),
+            )
+
+        def second_layer(start, width, passes):
             edges = slice(start, start + width)
             per_bank = BANK // width
-            y_of[start] = []
-            for i0 in range(0, N // P, per_bank):
-                acc = psum.tile([P, per_bank, width], F32, name="acc_out")
-                y_of[start].append((i0, acc))
+            if start not in y_of:
+                y_of[start] = [
+                    (i0, psum.tile([P, per_bank, width], F32, name="acc_out")) for i0 in range(0, N // P, per_bank)
+                ]
+            for i0, acc in y_of[start]:
                 for i in range(i0, i0 + per_bank):
-                    cols = slice(P * i, P * (i + 1))
-                    for b in range(PASSES):
-                        nc.tensor.matmul_mx(
-                            out=acc[:, i - i0, :],
-                            lhsT=w2[:, b, cols].bitcast(E4M3X4),
-                            lhsT_scale=w2_planes[:, b, cols],
-                            rhs=h_words[:, b, edges].bitcast(E4M3X4),
-                            rhs_scale=h_scales[:, b, edges],
-                            start=(b == 0),
-                            stop=(b == PASSES - 1),
-                        )
+                    for b in passes:
+                        second_layer_pass(acc[:, i - i0, :], i, b, edges)
 
         out_view = out.rearrange("(i p) j -> p i j", p=P)
 
-        def gate_and_store(start, width):
+        def gate_and_store(start, width, banks):
             edges = slice(start, start + width)
             per_bank = BANK // width
-            for i0, acc in y_of[start]:
+            for i0, acc in y_of[start][banks]:
                 result = ring.tile([P, per_bank, width], F32, name="result")
                 nc.vector.tensor_tensor(result[:], acc[:], gate[:, i0 : i0 + per_bank, edges], MULT)
                 nc.sync.dma_start(out_view[:, i0 : i0 + per_bank, edges], result[:])
@@ -245,33 +265,42 @@ def tile_list_gated_edge_messages_kernel(
         gate_half(1)
         cast_on_vector(0, 0, 0, P)
         quantize_w1(0, 0)
-        cast_on_vector(0, 1, 0, P // 2)
-        cast_on_vector(0, 1, P // 2, P)
-        w2 = slots.tile([P, PASSES, N + N // 4], I32, name="slot_a", align_bytes=64)
-        w2_planes = w2[:, :, N:].bitcast(U8)
-        nc.gpsimd.memset(w2[:, :, N:], 0)
+        for m0 in range(0, P, P // 2):
+            cast_on_vector(0, 1, m0, m0 + P // 2)
+        w2 = slots.tile([P, PASSES, N], I32, name="slot_a", align_bytes=64)
         nc.sync.dma_start(
-            w2[:, :, 0:N], w2_words.rearrange("a p n i -> a p (n i)").bitcast(I32).rearrange("a p n -> p a n")
+            w2[:], w2_words.rearrange("a p n i -> a p (n i)").bitcast(I32).rearrange("a p n -> p a n")
         )
-        load_planes(w2[:, :, N:], w2_scales)
+        load_planes(w2_plane_words, w2_scales)
         quantize_w1(0, 1)
-        cast_on_vector(1, 0, 0, P // 2)
-        cast_on_vector(1, 0, P // 2, P)
+        for m0 in range(0, P, P // 1):
+            cast_on_vector(1, 0, m0, m0 + P // 1)
         quantize_w1(1, 0)
 
-        for step in range(len(UNITS) + 3):
-            if step < len(UNITS):
-                first_layer(*UNITS[step])
-            if step == 2:
-                for m0 in range(0, P, 64):
-                    cast_on_scalar(1, 1, m0, m0 + 64)
+        todo = []
+        for unit in UNITS[:0]:
+            first_layer(*unit)
+        for step in range(len(UNITS) + 5):
+            if step + 0 < len(UNITS):
+                first_layer(*UNITS[step + 0])
+            if step in CAST_ON_SCALAR:
+                cast_on_scalar(1, 1, *CAST_ON_SCALAR[step])
             if 0 <= step - 1 < len(UNITS):
                 apply_gain(*UNITS[step - 1])
+            if step == 4:
+                quantize_w1(1, 1)
+            for job in todo[:2]:
+                gate_and_store(*job)
+            todo = todo[2:]
             if 0 <= step - 2 < len(UNITS):
                 quantize_h(*UNITS[step - 2])
-                if step == 3:
-                    quantize_w1(1, 1)
-                if UNITS[step - 2][0] == PASSES - 1:
-                    second_layer(*UNITS[step - 2][1:])
-            if 0 <= step - 3 < len(UNITS) and UNITS[step - 3][0] == PASSES - 1:
-                gate_and_store(*UNITS[step - 3][1:])
+                b, start, width, share = UNITS[step - 2]
+                if b == 0 and start + width == S:
+                    second_layer(0, BANK, [0])
+                if b == 1 and start + width == BANK:
+                    second_layer(0, BANK, [1])
+                    todo += [(0, BANK, slice(i, i + 1)) for i in range(N // P)]
+                if b == 1 and start >= BANK:
+                    second_layer(start, width, [0, 1])
+                    todo += [(start, width, slice(i, i + 1)) for i in range(len(y_of[start]))]
+        assert not todo

@@ -22,8 +22,16 @@ PACK = 4
 PASS = P * PACK
 PASSES = 2
 BANK = 512
-UNITS = [(0, 0, 128, 128), (0, 128, 128, 128), (0, 256, 256, 256), (0, 512, 256, 256), (0, 768, 256, 256), (1, 0, 256, 256), (1, 256, 256, 256), (1, 512, 256, -1), (1, 768, 128, -1), (1, 896, 128, 128)]
-CAST_ON_SCALAR = {2: (0, 64), 3: (64, 128)}
+UNITS = [(0, 0, 128, 128), (0, 128, 128, 128), (0, 256, 256, 256), (0, 512, 256, 256), (0, 768, 256, 256), (1, 0, 256, 256), (1, 256, 256, 256), (1, 512, 256, -1), (1, 768, 256, -1)]
+H_SPANS = {(0, 0): 512, (0, 512): 512, (1, 0): 512, (1, 512): 512}
+
+GATE_BANKS = [[0, 1, 2, 3], [4, 5, 6, 7]]
+FIRST_BANKS = {(0, 0): [0], (0, 128): [1], (0, 256): [2,3], (0, 512): [4,5], (0, 768): [6,7], (1, 0): [0,1], (1, 256): [2,3], (1, 512): [0,1], (1, 768): [2,3]}
+SECOND_BANKS = {0: [4, 5], 256: [6, 7], 512: [0, 1], 768: [2, 3]}
+
+HB_TAGS = {(1, 768): "pin_e"}
+
+RESULT_TAGS = {(512, 2): "pin_e"}
 
 
 def tile_list_gated_edge_messages_kernel(
@@ -34,7 +42,7 @@ def tile_list_gated_edge_messages_kernel(
         keep = ctx.enter_context(tc.tile_pool(name="keep", bufs=1))
         ring = ctx.enter_context(tc.tile_pool(name="ring", bufs=4))
         slots = ctx.enter_context(tc.tile_pool(name="slots", bufs=1))
-        psum = ctx.enter_context(tc.psum_pool(name="psum", bufs=4))
+        psum = ctx.enter_context(tc.psum_pool(name="psum", bufs=1))
 
         offsets = keep.tile([P, S // 16], U16, name="offsets")
         nc.sync.dma_start(offsets[:], offs)
@@ -77,21 +85,18 @@ def tile_list_gated_edge_messages_kernel(
         identity = keep.tile([P, P], F32, name="identity")
         nc.gpsimd.memset(vec_rows[:], 0.0)
         make_identity(nc, identity[:])
-        w2_plane_words = keep.tile([P, PASSES, N // 4], I32, name="w2_plane_words", align_bytes=64)
-        w2_planes = w2_plane_words[:].bitcast(U8)
-        nc.gpsimd.memset(w2_plane_words[:], 0)
         nc.sync.dma_start(wg[:], wg_words.bitcast(I32).rearrange("a p n -> p a n"))
         nc.sync.dma_start(vec_rows[4 : 4 + N // P, 0:P], bg.rearrange("(i p) -> i p", p=P))
         tab_rows = tab_scales.bitcast(I32).rearrange("a (q r) n -> r q a n", r=4)
         for r in range(4):
             nc.sync.dma_start(tab_planes[r:P:16, :], tab_rows[r])
         table = [load_table(0, "table0")]
+        nc.sync.dma_start(vec_rows[0:PASSES, :], gain.rearrange("(b c) -> b c", b=PASSES))
         load_planes(wg_plane_words, wg_scales)
         table.append(load_table(1, "slot_b"))
-        nc.sync.dma_start(vec_rows[0:PASSES, :], gain.rearrange("(b c) -> b c", b=PASSES))
-        bias_turned = psum.tile([P, P], F32, name="acc_m", bufs=4)
+        bias_turned = psum.tile([P, P], F32, name="bank6")
         nc.tensor.transpose(bias_turned[:], vec_rows[:, 0:P], identity[:])
-        gains_turned = psum.tile([P, PACK, P], F32, name="acc_m", bufs=4)
+        gains_turned = psum.tile([P, PACK, P], F32, name="bank7")
         for t in range(PACK):
             nc.tensor.transpose(gains_turned[:, t, :], vec_rows[:, t:PASS:PACK], identity[:])
         nc.scalar.copy(bias[:], bias_turned[:, 4 : 4 + N // P])
@@ -99,12 +104,13 @@ def tile_list_gated_edge_messages_kernel(
 
         w1_words = keep.tile([P, PASSES, H], U32, name="w1_words", align_bytes=64)
         w1_scales = keep.tile([P, PASSES, H], U8, name="w1_scales", align_bytes=64)
-        grouped = {
-            key: keep.tile([P, PACK, P, PACK], BF16, name=f"grouped{key[0]}{key[1]}", align_bytes=64)
-            for key in [(b, a) for b in range(PASSES) for a in range(PASSES)]
-        }
+        grouped = {}
+        GROUPED_TAGS = {(1, 1): "pin_a"}
 
         def cast_views(b, a, m0, m1):
+            if (b, a) not in grouped:
+                tag = GROUPED_TAGS.get((b, a), f"grouped{b}{a}")
+                grouped[b, a] = keep.tile([P, PACK, P, PACK], BF16, name=tag, align_bytes=64)
             dst = grouped[b, a][:, :, m0:m1, :].rearrange("p t m j -> p m j t")
             src = raw[b, a][:, :, PACK * m0 : PACK * m1].rearrange("p j (m t) -> p m j t", t=PACK)
             return dst, src
@@ -126,7 +132,8 @@ def tile_list_gated_edge_messages_kernel(
         v_words = keep.tile([P, PASSES, S], U32, name="v_words", align_bytes=64)
         v_scales = keep.tile([P, S], U8, name="v_scales", align_bytes=64)
         nc.vector.tensor_copy(v_scales[:], tab_planes[:].bitcast(U8).indirect(offsets[:]))
-        nc.sync.dma_start(v_scales_low[0:100, :], v_scales[16:116, :].bitcast(I32))
+        for r in range(4):
+            nc.sync.dma_start(v_scales_low[r:P:32, :], v_scales[16 + r : P : 32, :].bitcast(I32))
         load_w1(0, slots.tile([P, PASSES * PACK * PASS], F32, name="slot_a", align_bytes=64), [1, 2])
         nc.vector.tensor_copy(v_words[:, 0, :], table[0][:].bitcast(U32).indirect(offsets[:]))
         for half in range(2):
@@ -134,73 +141,115 @@ def tile_list_gated_edge_messages_kernel(
                 v_words[:, 1, half * BANK : (half + 1) * BANK],
                 table[1][:].bitcast(U32).indirect(offsets[:, half * 32 : (half + 1) * 32]),
             )
-        load_w1(1, slots.tile([P, PASSES * PACK * PASS], F32, name="slot_b", align_bytes=64), [1, 1])
+        load_w1(1, slots.tile([P, PASSES * PACK * PASS], F32, name="slot_b", align_bytes=64), [2, 1])
 
-        gate = keep.tile([P, N // P, S], F32, name="gate")
+        gate_low = [keep.tile([P, 2, BANK], F32, name=f"gate{i}", align_bytes=64) for i in range(N // P // 2)]
+        gate_high = keep.tile([P, N // P, BANK], F32, name="gate_high")
         gate_planes = [v_scales[:], v_scales_low[:].bitcast(U8)]
 
-        def gate_half(half):
+        gate_acc = {}
+
+        def gate_pass(half, a):
             edges = slice(half * BANK, (half + 1) * BANK)
             for i in range(N // P):
-                acc = psum.tile([P, BANK], F32, name="acc_out")
-                for a in range(PASSES):
-                    nc.tensor.matmul_mx(
-                        out=acc[:],
-                        lhsT=wg[:, a, P * i // 2 : P * (i + 1) // 2].bitcast(E2M1X4),
-                        lhsT_scale=wg_planes[:, a, P * i : P * (i + 1)],
-                        rhs=v_words[:, a, edges].bitcast(E4M3X4),
-                        rhs_scale=gate_planes[a][:, edges],
-                        start=(a == 0),
-                        stop=(a == PASSES - 1),
-                    )
-                nc.scalar.activation(gate[:, i, edges], acc[:], ACT.Sigmoid, bias=bias[:, i : i + 1])
-
-        h_words = keep.tile([P, PASSES, S], U32, name="h_words", align_bytes=64)
-        h_scales = keep.tile([P, PASSES, S], U8, name="h_scales", align_bytes=64)
-        tanh_of = {}
-        h_of = {}
-        y_of = {}
-
-        def first_layer_passes(acc, b, t, edges):
-            cols = slice(b * PASS + t * P, b * PASS + (t + 1) * P)
-            for a in range(PASSES):
+                if a == 0:
+                    gate_acc[half, i] = psum.tile([P, BANK], F32, name=f"bank{GATE_BANKS[half][i]}")
+                acc = gate_acc[half, i]
                 nc.tensor.matmul_mx(
-                    out=acc,
-                    lhsT=w1_words[:, a, cols].bitcast(E4M3X4),
-                    lhsT_scale=w1_scales[:, a, cols],
+                    out=acc[:],
+                    lhsT=wg[:, a, P * i // 2 : P * (i + 1) // 2].bitcast(E2M1X4),
+                    lhsT_scale=wg_planes[:, a, P * i : P * (i + 1)],
                     rhs=v_words[:, a, edges].bitcast(E4M3X4),
                     rhs_scale=gate_planes[a][:, edges],
                     start=(a == 0),
                     stop=(a == PASSES - 1),
                 )
+                if a == PASSES - 1:
+                    dst = gate_high[:, i, :] if half else gate_low[i // 2][:, i % 2, :]
+                    nc.scalar.activation(dst, acc[:], ACT.Sigmoid, bias=bias[:, i : i + 1])
+
+        h_tiles = {}
+        H_TAGS = {}
+        TH_TAGS = {(0, 128): "pin_a", (0, 768): "slot_b"}
+
+        def h_views(b, start, width):
+            first = max(s0 for (b0, s0) in H_SPANS if b0 == b and s0 <= start)
+            if (b, first) not in h_tiles:
+                span = H_SPANS[b, first]
+                words = keep.tile([P, span], U32, name=f"h_words{b}_{first}", align_bytes=64)
+                scales = keep.tile([P, span], U8, name=H_TAGS.get((b, first), f"h_scales{b}_{first}"), align_bytes=64)
+                h_tiles[b, first] = (words, scales)
+            words, scales = h_tiles[b, first]
+            cols = slice(start - first, start - first + width)
+            return words[:, cols].bitcast(E4M3X4), scales[:, cols]
+        tanh_of = {}
+        h_of = {}
+        y_of = {}
+
+        m_acc = {}
+
+        def first_layer_pass(acc, b, t, a, edges, start, stop):
+            cols = slice(b * PASS + t * P, b * PASS + (t + 1) * P)
+            nc.tensor.matmul_mx(
+                out=acc,
+                lhsT=w1_words[:, a, cols].bitcast(E4M3X4),
+                lhsT_scale=w1_scales[:, a, cols],
+                rhs=v_words[:, a, edges].bitcast(E4M3X4),
+                rhs_scale=gate_planes[a][:, edges],
+                start=start,
+                stop=stop,
+            )
+
+        def first_pass_ahead(b, start, width, share):
+            per_bank = BANK // width
+            for g in range(PACK // per_bank):
+                acc = psum.tile([P, per_bank, width], F32, name=f"bank{FIRST_BANKS[b, start][g]}")
+                m_acc[b, start, g] = acc
+                for e in range(per_bank):
+                    first_layer_pass(acc[:, e, :], b, g * per_bank + e, 0, slice(start, start + width), e == 0, False)
 
         def first_layer(b, start, width, share):
-            block = min(width, 256 if share >= 0 else 256)
+            block = min(width, 128 if 0 <= share < width else 256)
             per_bank = BANK // block
             groups = PACK // per_bank
-            th = ring.tile([P, groups, width * per_bank], F32, name="th", bufs=4)
+            banks = FIRST_BANKS[b, start]
+            if (b, start) in TH_TAGS:
+                pool = slots if TH_TAGS[b, start] == "slot_b" else keep
+                th = pool.tile([P, groups, width * per_bank], F32, name=TH_TAGS[b, start], align_bytes=64)
+            else:
+                th = ring.tile([P, groups, width * per_bank], F32, name="th", bufs=4)
             for j0 in range(0, width, block):
                 for g in range(groups):
-                    acc = psum.tile([P, per_bank, block], F32, name="acc_m", bufs=4)
-                    for e in range(per_bank):
-                        first_layer_passes(acc[:, e, :], b, g * per_bank + e, slice(start + j0, start + j0 + block))
+                    edges = slice(start + j0, start + j0 + block)
+                    if (b, start, g) in m_acc:
+                        acc = m_acc[b, start, g]
+                        for e in range(per_bank):
+                            first_layer_pass(acc[:, e, :], b, g * per_bank + e, 1, edges, False, e == per_bank - 1)
+                    else:
+                        acc = psum.tile([P, per_bank, block], F32, name=f"bank{banks[j0 // block * groups + g]}")
+                        for e in range(per_bank):
+                            for a in range(PASSES):
+                                first_layer_pass(acc[:, e, :], b, g * per_bank + e, a, edges, a == 0, a == PASSES - 1)
                     if share < 0:
                         dst = th[:, g, :].rearrange("p (e j) -> p e j", e=per_bank)[:, :, j0 : j0 + block]
                         nc.scalar.activation(dst, acc[:], ACT.Tanh)
                     else:
                         dst = th[:, g, :].rearrange("p (j e) -> p j e", e=per_bank)[:, j0 : j0 + block, :]
                         nc.scalar.activation(dst, acc[:].rearrange("p e j -> p j e"), ACT.Tanh)
-            if share < 0:
-                rows = ring.tile([P, PACK, width], BF16, name="rows")
-                by_t = th[:].rearrange("p g (e j) -> p (g e) j", e=per_bank)
-                for t in range(PACK):
-                    nc.scalar.activation(rows[:, t, :], by_t[:, t, :], ACT.Copy, scale=gains[:, b, t : t + 1])
-                tanh_of[b, start] = rows
-            else:
-                tanh_of[b, start] = th
+            tanh_of[b, start] = th
+
+        def gain_on_scalar(b, start, width, share):
+            rows = ring.tile([P, PACK, width], BF16, name="rows")
+            by_t = tanh_of[b, start][:].rearrange("p g (e j) -> p (g e) j", j=width)
+            for t in range(PACK):
+                nc.scalar.activation(rows[:, t, :], by_t[:, t, :], ACT.Copy, scale=gains[:, b, t : t + 1])
+            tanh_of[b, start] = rows
 
         def apply_gain(b, start, width, share):
-            hb = ring.tile([P, width, PACK], BF16, name="hb", align_bytes=64, bufs=4)
+            if (b, start) in HB_TAGS:
+                hb = slots.tile([P, width, PACK], BF16, name=HB_TAGS[b, start], align_bytes=64)
+            else:
+                hb = ring.tile([P, width, PACK], BF16, name="hb", align_bytes=64, bufs=4)
             h_of[b, start] = hb
             if share < 0:
                 nc.vector.tensor_copy(
@@ -208,7 +257,7 @@ def tile_list_gated_edge_messages_kernel(
                     tanh_of[b, start][:].rearrange("p t (c i) -> p c t i", i=4),
                 )
                 return
-            per_bank = BANK // min(width, 256 if share >= 0 else 256)
+            per_bank = BANK // min(width, 128 if 0 <= share < width else 256)
             src = tanh_of[b, start][:].rearrange("p g (j e) -> p j g e", e=per_bank)
             dst = hb[:].rearrange("p j (g e) -> p j g e", e=per_bank)
             for engine, j0, j1, factor in (
@@ -220,23 +269,24 @@ def tile_list_gated_edge_messages_kernel(
                     engine.tensor_tensor(dst[:, j0:j1], src[:, j0:j1], factor, MULT)
 
         def quantize_h(b, start, width, share):
-            edges = slice(start, start + width)
+            words, scales = h_views(b, start, width)
             nc.vector.quantize_mx(
-                out=h_words[:, b, edges].bitcast(E4M3X4),
-                scales=h_scales[:, b, edges],
+                out=words,
+                scales=scales,
                 in_=h_of[b, start][:].rearrange("p j t -> p (j t)"),
             )
 
-        def second_layer_pass(acc, i, b, edges):
+        def second_layer_pass(acc, i, b, edges, start, stop):
             cols = slice(P * i, P * (i + 1))
+            words, scales = h_views(b, edges.start, edges.stop - edges.start)
             nc.tensor.matmul_mx(
                 out=acc,
                 lhsT=w2[:, b, cols].bitcast(E4M3X4),
                 lhsT_scale=w2_planes[:, b, cols],
-                rhs=h_words[:, b, edges].bitcast(E4M3X4),
-                rhs_scale=h_scales[:, b, edges],
-                start=(b == 0),
-                stop=(b == PASSES - 1),
+                rhs=words,
+                rhs_scale=scales,
+                start=start,
+                stop=stop,
             )
 
         def second_layer(start, width, passes):
@@ -244,12 +294,16 @@ def tile_list_gated_edge_messages_kernel(
             per_bank = BANK // width
             if start not in y_of:
                 y_of[start] = [
-                    (i0, psum.tile([P, per_bank, width], F32, name="acc_out")) for i0 in range(0, N // P, per_bank)
+                    (i0, psum.tile([P, per_bank, width], F32, name=f"bank{SECOND_BANKS[start][i0 // per_bank]}"))
+                    for i0 in range(0, N // P, per_bank)
                 ]
             for i0, acc in y_of[start]:
                 for i in range(i0, i0 + per_bank):
                     for b in passes:
-                        second_layer_pass(acc[:, i - i0, :], i, b, edges)
+                        alone = len(passes) == PASSES
+                        opens = b == 0 and (alone or i == i0)
+                        closes = b == PASSES - 1 and (alone or i == i0 + per_bank - 1)
+                        second_layer_pass(acc[:, i - i0, :], i, b, edges, opens, closes)
 
         out_view = out.rearrange("(i p) j -> p i j", p=P)
 
@@ -257,50 +311,86 @@ def tile_list_gated_edge_messages_kernel(
             edges = slice(start, start + width)
             per_bank = BANK // width
             for i0, acc in y_of[start][banks]:
-                result = ring.tile([P, per_bank, width], F32, name="result")
-                nc.vector.tensor_tensor(result[:], acc[:], gate[:, i0 : i0 + per_bank, edges], MULT)
+                if (start, i0) in RESULT_TAGS:
+                    result = slots.tile([P, per_bank, width], F32, name=RESULT_TAGS[start, i0], align_bytes=64)
+                else:
+                    result = ring.tile([P, per_bank, width], F32, name="result", bufs=8)
+                if start < BANK:
+                    factor = gate_low[i0 // 2][:, :, start : start + width]
+                else:
+                    factor = gate_high[:, i0 : i0 + per_bank, start - BANK : start - BANK + width]
+                nc.vector.tensor_tensor(result[:], acc[:], factor, MULT)
                 nc.sync.dma_start(out_view[:, i0 : i0 + per_bank, edges], result[:])
 
-        gate_half(0)
-        gate_half(1)
+        for a in range(PASSES):
+            for half in range(2):
+                gate_pass(half, a)
         cast_on_vector(0, 0, 0, P)
         quantize_w1(0, 0)
+        first_pass_ahead(*UNITS[0])
+        first_pass_ahead(*UNITS[1])
+        first_pass_ahead(*UNITS[2])
         for m0 in range(0, P, P // 2):
             cast_on_vector(0, 1, m0, m0 + P // 2)
-        w2 = slots.tile([P, PASSES, N], I32, name="slot_a", align_bytes=64)
+        w2 = slots.tile([P, PASSES, N + N // 4], I32, name="slot_a", align_bytes=64)
+        w2_planes = w2[:, :, N:].bitcast(U8)
+        nc.gpsimd.memset(w2[:, :, N:], 0)
         nc.sync.dma_start(
-            w2[:], w2_words.rearrange("a p n i -> a p (n i)").bitcast(I32).rearrange("a p n -> p a n")
+            w2[:, :, 0:N], w2_words.rearrange("a p n i -> a p (n i)").bitcast(I32).rearrange("a p n -> p a n")
         )
-        load_planes(w2_plane_words, w2_scales)
+        load_planes(w2[:, :, N:], w2_scales)
         quantize_w1(0, 1)
-        for m0 in range(0, P, P // 1):
-            cast_on_vector(1, 0, m0, m0 + P // 1)
-        quantize_w1(1, 0)
 
-        todo = []
-        for unit in UNITS[:0]:
-            first_layer(*unit)
-        for step in range(len(UNITS) + 5):
-            if step + 0 < len(UNITS):
-                first_layer(*UNITS[step + 0])
-            if step in CAST_ON_SCALAR:
-                cast_on_scalar(1, 1, *CAST_ON_SCALAR[step])
-            if 0 <= step - 1 < len(UNITS):
-                apply_gain(*UNITS[step - 1])
-            if step == 4:
-                quantize_w1(1, 1)
-            for job in todo[:2]:
-                gate_and_store(*job)
-            todo = todo[2:]
-            if 0 <= step - 2 < len(UNITS):
-                quantize_h(*UNITS[step - 2])
-                b, start, width, share = UNITS[step - 2]
-                if b == 0 and start + width == S:
-                    second_layer(0, BANK, [0])
-                if b == 1 and start + width == BANK:
-                    second_layer(0, BANK, [1])
-                    todo += [(0, BANK, slice(i, i + 1)) for i in range(N // P)]
-                if b == 1 and start >= BANK:
-                    second_layer(start, width, [0, 1])
-                    todo += [(start, width, slice(i, i + 1)) for i in range(len(y_of[start]))]
-        assert not todo
+        cast_on_vector(1, 0, 0, 64)
+        cast_on_vector(1, 0, 64, 128)
+        quantize_w1(1, 0)
+        first_layer(*UNITS[0])
+        first_layer(*UNITS[1])
+        apply_gain(*UNITS[0])
+        first_layer(*UNITS[2])
+        apply_gain(*UNITS[1])
+        quantize_h(*UNITS[0])
+        first_layer(*UNITS[3])
+        cast_on_scalar(1, 1, 0, 64)
+        cast_on_scalar(1, 1, 64, 128)
+        apply_gain(*UNITS[2])
+        quantize_h(*UNITS[1])
+        quantize_w1(1, 1)
+        first_layer(*UNITS[4])
+        first_pass_ahead(*UNITS[5])
+        first_pass_ahead(*UNITS[6])
+        apply_gain(*UNITS[3])
+        quantize_h(*UNITS[2])
+        first_layer(*UNITS[5])
+        second_layer(0, 256, [0])
+        apply_gain(*UNITS[4])
+        quantize_h(*UNITS[3])
+        first_layer(*UNITS[6])
+        second_layer(256, 256, [0])
+        apply_gain(*UNITS[5])
+        quantize_h(*UNITS[4])
+        quantize_h(*UNITS[5])
+        first_layer(*UNITS[7])
+        second_layer(0, 256, [1])
+        apply_gain(*UNITS[6])
+        second_layer(512, 256, [0])
+        gain_on_scalar(*UNITS[7])
+        gate_and_store(0, 256, slice(0, 1))
+        quantize_h(*UNITS[6])
+        first_layer(*UNITS[8])
+        second_layer(256, 256, [1])
+        gate_and_store(0, 256, slice(1, 2))
+        second_layer(768, 256, [0])
+        gain_on_scalar(*UNITS[8])
+        apply_gain(*UNITS[7])
+        gate_and_store(256, 256, slice(0, 1))
+        quantize_h(*UNITS[7])
+        second_layer(512, 256, [1])
+        gate_and_store(256, 256, slice(1, 2))
+        apply_gain(*UNITS[8])
+        quantize_h(*UNITS[8])
+        second_layer(768, 256, [1])
+        gate_and_store(512, 256, slice(0, 1))
+        gate_and_store(512, 256, slice(1, 2))
+        gate_and_store(768, 256, slice(0, 1))
+        gate_and_store(768, 256, slice(1, 2))

@@ -26,8 +26,8 @@ UNITS = [(0, 0, 128, 128), (0, 128, 128, 128), (0, 256, 256, 256), (0, 512, 256,
 H_SPANS = {(0, 0): 512, (0, 512): 512, (1, 0): 512, (1, 512): 512}
 
 GATE_BANKS = [[0, 1, 2, 3], [4, 5, 6, 7]]
-FIRST_BANKS = {(0, 0): [0], (0, 128): [1], (0, 256): [2,3], (0, 512): [4,5], (0, 768): [6,7], (1, 0): [0,1], (1, 256): [2,3], (1, 512): [0,1], (1, 768): [2,3]}
-SECOND_BANKS = {0: [4, 5], 256: [6, 7], 512: [0, 1], 768: [2, 3]}
+FIRST_BANKS = {(0, 0): [0], (0, 128): [1], (0, 256): [2,3], (0, 512): [4,5], (0, 768): [4,5], (1, 0): [0,1], (1, 256): [2,3], (1, 512): [0,1], (1, 768): [2,3]}
+SECOND_BANKS = {0: [6, 7], 256: [4, 5], 512: [0, 1], 768: [2, 3]}
 
 HB_TAGS = {(1, 768): "pin_e"}
 
@@ -201,15 +201,14 @@ def tile_list_gated_edge_messages_kernel(
             )
 
         def first_pass_ahead(b, start, width, share):
-            per_bank = BANK // width
-            for g in range(PACK // per_bank):
-                acc = psum.tile([P, per_bank, width], F32, name=f"bank{FIRST_BANKS[b, start][g]}")
-                m_acc[b, start, g] = acc
-                for e in range(per_bank):
-                    first_layer_pass(acc[:, e, :], b, g * per_bank + e, 0, slice(start, start + width), e == 0, False)
+            for n, j0 in enumerate(range(start, start + width, P)):
+                acc = psum.tile([P, PACK, P], F32, name=f"bank{FIRST_BANKS[b, start][n]}")
+                m_acc[b, j0] = acc
+                for t in range(PACK):
+                    first_layer_pass(acc[:, t, :], b, t, 0, slice(j0, j0 + P), t == 0, False)
 
         def first_layer(b, start, width, share):
-            block = min(width, 128 if 0 <= share < width else 256)
+            block = min(width, 128 if share >= 0 else 256)
             per_bank = BANK // block
             groups = PACK // per_bank
             banks = FIRST_BANKS[b, start]
@@ -221,8 +220,8 @@ def tile_list_gated_edge_messages_kernel(
             for j0 in range(0, width, block):
                 for g in range(groups):
                     edges = slice(start + j0, start + j0 + block)
-                    if (b, start, g) in m_acc:
-                        acc = m_acc[b, start, g]
+                    if (b, start + j0) in m_acc:
+                        acc = m_acc[b, start + j0]
                         for e in range(per_bank):
                             first_layer_pass(acc[:, e, :], b, g * per_bank + e, 1, edges, False, e == per_bank - 1)
                     else:
@@ -257,7 +256,7 @@ def tile_list_gated_edge_messages_kernel(
                     tanh_of[b, start][:].rearrange("p t (c i) -> p c t i", i=4),
                 )
                 return
-            per_bank = BANK // min(width, 128 if 0 <= share < width else 256)
+            per_bank = BANK // min(width, 128 if share >= 0 else 256)
             src = tanh_of[b, start][:].rearrange("p g (j e) -> p j g e", e=per_bank)
             dst = hb[:].rearrange("p j (g e) -> p j g e", e=per_bank)
             for engine, j0, j1, factor in (

@@ -22,7 +22,7 @@ PACK = 4
 PASS = P * PACK
 PASSES = 2
 BANK = 512
-UNITS = [(0, 0, 128, 128), (0, 128, 128, 128), (0, 256, 256, 256), (0, 512, 256, 256), (0, 768, 256, 256), (1, 0, 256, 256), (1, 256, 256, 256), (1, 512, 256, -1), (1, 768, 256, -1)]
+UNITS = [(0, 0, 128, 128), (0, 128, 128, 128), (0, 256, 256, 256), (0, 512, 256, 256), (0, 768, 256, 256), (1, 0, 256, 256), (1, 256, 256, -1), (1, 512, 256, -1), (1, 768, 256, -1)]
 H_SPANS = {(0, 0): 512, (0, 512): 512, (1, 0): 512, (1, 512): 512}
 
 GATE_BANKS = [[0, 1, 2, 3], [4, 5, 6, 7]]
@@ -306,7 +306,7 @@ def tile_list_gated_edge_messages_kernel(
 
         out_view = out.rearrange("(i p) j -> p i j", p=P)
 
-        def gate_and_store(start, width, banks):
+        def gate_and_store(start, width, banks, parts=1):
             edges = slice(start, start + width)
             per_bank = BANK // width
             for i0, acc in y_of[start][banks]:
@@ -318,8 +318,10 @@ def tile_list_gated_edge_messages_kernel(
                     factor = gate_low[i0 // 2][:, :, start : start + width]
                 else:
                     factor = gate_high[:, i0 : i0 + per_bank, start - BANK : start - BANK + width]
-                nc.vector.tensor_tensor(result[:], acc[:], factor, MULT)
-                nc.sync.dma_start(out_view[:, i0 : i0 + per_bank, edges], result[:])
+                step = per_bank // parts
+                for n in range(0, per_bank, step):
+                    nc.vector.tensor_tensor(result[:, n : n + step], acc[:, n : n + step], factor[:, n : n + step], MULT)
+                    nc.sync.dma_start(out_view[:, i0 + n : i0 + n + step, edges], result[:, n : n + step])
 
         for a in range(PASSES):
             for half in range(2):
@@ -331,33 +333,31 @@ def tile_list_gated_edge_messages_kernel(
         first_pass_ahead(*UNITS[2])
         for m0 in range(0, P, P // 2):
             cast_on_vector(0, 1, m0, m0 + P // 2)
-        w2 = slots.tile([P, PASSES, N + N // 4], I32, name="slot_a", align_bytes=64)
-        w2_planes = w2[:, :, N:].bitcast(U8)
-        nc.gpsimd.memset(w2[:, :, N:], 0)
+        w2 = slots.tile([P, PASSES, N], I32, name="slot_a", align_bytes=64)
+        w2_planes = wg_planes
         nc.sync.dma_start(
-            w2[:, :, 0:N], w2_words.rearrange("a p n i -> a p (n i)").bitcast(I32).rearrange("a p n -> p a n")
+            w2[:], w2_words.rearrange("a p n i -> a p (n i)").bitcast(I32).rearrange("a p n -> p a n")
         )
-        load_planes(w2[:, :, N:], w2_scales)
+        load_planes(wg_plane_words, w2_scales)
         quantize_w1(0, 1)
 
         cast_on_vector(1, 0, 0, 64)
         cast_on_vector(1, 0, 64, 128)
-        quantize_w1(1, 0)
         first_layer(*UNITS[0])
         first_layer(*UNITS[1])
         apply_gain(*UNITS[0])
+        quantize_w1(1, 0)
         first_layer(*UNITS[2])
         apply_gain(*UNITS[1])
         quantize_h(*UNITS[0])
         first_layer(*UNITS[3])
-        cast_on_scalar(1, 1, 0, 64)
-        cast_on_scalar(1, 1, 64, 128)
+        cast_on_scalar(1, 1, 40, 128)
         apply_gain(*UNITS[2])
+        cast_on_vector(1, 1, 0, 40)
         quantize_h(*UNITS[1])
         quantize_w1(1, 1)
         first_layer(*UNITS[4])
         first_pass_ahead(*UNITS[5])
-        first_pass_ahead(*UNITS[6])
         apply_gain(*UNITS[3])
         quantize_h(*UNITS[2])
         first_layer(*UNITS[5])
@@ -366,6 +366,7 @@ def tile_list_gated_edge_messages_kernel(
         quantize_h(*UNITS[3])
         first_layer(*UNITS[6])
         second_layer(256, 256, [0])
+        gain_on_scalar(*UNITS[6])
         apply_gain(*UNITS[5])
         quantize_h(*UNITS[4])
         quantize_h(*UNITS[5])
@@ -387,9 +388,9 @@ def tile_list_gated_edge_messages_kernel(
         second_layer(512, 256, [1])
         gate_and_store(256, 256, slice(1, 2))
         apply_gain(*UNITS[8])
+        gate_and_store(512, 256, slice(0, 1))
         quantize_h(*UNITS[8])
         second_layer(768, 256, [1])
-        gate_and_store(512, 256, slice(0, 1))
         gate_and_store(512, 256, slice(1, 2))
         gate_and_store(768, 256, slice(0, 1))
-        gate_and_store(768, 256, slice(1, 2))
+        gate_and_store(768, 256, slice(1, 2), 2)

@@ -22,16 +22,19 @@ PACK = 4
 PASS = P * PACK
 PASSES = 2
 BANK = 512
-UNITS = [(0, 0, 128, 128), (0, 128, 128, 128), (0, 256, 256, 256), (0, 512, 256, 256), (0, 768, 256, 256), (1, 0, 256, 256), (1, 256, 256, -1), (1, 512, 256, -1), (1, 768, 256, -1)]
-H_SPANS = {(0, 0): 512, (0, 512): 512, (1, 0): 512, (1, 512): 512}
+HALF = S // 2
+CHUNK = 256
+PLANE_ROWS = 4
+PASS1_DROP = 16
+BIAS_ROW = 4
+RING = 4
+STORES = N // P * S // BANK
+LAST_PIECE_ON_VECTOR = 40
 
-GATE_BANKS = [[0, 1, 2, 3], [4, 5, 6, 7]]
-FIRST_BANKS = {(0, 0): [0], (0, 128): [1], (0, 256): [2,3], (0, 512): [4,5], (0, 768): [4,5], (1, 0): [0,1], (1, 256): [2,3], (1, 512): [0,1], (1, 768): [2,3]}
-SECOND_BANKS = {0: [6, 7], 256: [4, 5], 512: [0, 1], 768: [2, 3]}
-
-HB_TAGS = {(1, 768): "pin_e"}
-
-RESULT_TAGS = {(512, 2): "pin_e"}
+PASS0 = [(0, 0, 128, (0,)), (0, 128, 128, (1,)), (0, 256, 256, (2, 3)), (0, 512, 256, (4, 5)), (0, 768, 256, (4, 5))]
+PASS1 = [(1, 0, 256, (0, 1)), (1, 256, 256, (2, 3)), (1, 512, 256, (0, 1)), (1, 768, 256, (2, 3))]
+GAIN_ON_SCALAR = PASS1[1:]
+SECOND_BANKS = [(6, 7), (4, 5), (0, 1), (2, 3)]
 
 
 def tile_list_gated_edge_messages_kernel(
@@ -40,7 +43,7 @@ def tile_list_gated_edge_messages_kernel(
     nc = tc.nc
     with ExitStack() as ctx:
         keep = ctx.enter_context(tc.tile_pool(name="keep", bufs=1))
-        ring = ctx.enter_context(tc.tile_pool(name="ring", bufs=4))
+        ring = ctx.enter_context(tc.tile_pool(name="ring", bufs=RING))
         slots = ctx.enter_context(tc.tile_pool(name="slots", bufs=1))
         psum = ctx.enter_context(tc.psum_pool(name="psum", bufs=1))
 
@@ -49,7 +52,8 @@ def tile_list_gated_edge_messages_kernel(
 
         raw = {}
 
-        def load_w1(b, staged, pieces):
+        def load_w1(b, slot, pieces):
+            staged = slots.tile([P, PASSES * PACK * PASS], F32, name=slot, align_bytes=64)
             for a in range(PASSES):
                 raw[b, a] = staged[:, a * PACK * PASS : (a + 1) * PACK * PASS].rearrange("p (j c) -> p j c", j=PACK)
                 rows = w1[a * PASS : (a + 1) * PASS, b * PASS : (b + 1) * PASS].rearrange("(p j) c -> p j c", j=PACK)
@@ -62,22 +66,19 @@ def tile_list_gated_edge_messages_kernel(
             nc.sync.dma_start(words[:], tab_words[a].rearrange("p t i -> p (t i)").bitcast(I32))
             return words
 
-        def load_planes(planes, scales):
-            rows = scales.bitcast(I32).rearrange("a (q r) n -> r q a n", r=4)
-            for r in range(4):
-                nc.sync.dma_start(planes[r:P:32], rows[r])
+        def load_weight_planes(scales):
+            rows = scales.bitcast(I32).rearrange("a (q r) n -> r q a n", r=PLANE_ROWS)
+            for r in range(PLANE_ROWS):
+                nc.sync.dma_start(weight_plane_words[r:P:32], rows[r])
 
         tab_planes = slots.tile([P, T // 4], I32, name="slot_a", align_bytes=64)
-        v_scales_low = keep.tile([P, S // 4], I32, name="v_scales_low", align_bytes=64)
+        v_scales_lifted = keep.tile([P, S // 4], I32, name="v_scales_lifted", align_bytes=64)
         nc.vector.memset(tab_planes[:], 0)
         wg = keep.tile([P, PASSES, N // 2], I32, name="wg", align_bytes=64)
-        wg_plane_words = keep.tile([P, PASSES, N // 4], I32, name="wg_plane_words", align_bytes=64)
-        wg_planes = wg_plane_words[:].bitcast(U8)
-        nc.vector.memset(wg_plane_words[:], 0)
-        nc.vector.memset(v_scales_low[:], 0)
-        warm = keep.tile([P, 2], F32, name="warm")
-        nc.vector.memset(warm[:, 0:1], 0)
-        nc.scalar.activation(warm[:, 1:2], warm[:, 0:1], ACT.Sigmoid)
+        weight_plane_words = keep.tile([P, PASSES, N // 4], I32, name="weight_plane_words", align_bytes=64)
+        weight_planes = weight_plane_words[:].bitcast(U8)
+        nc.vector.memset(weight_plane_words[:], 0)
+        nc.vector.memset(v_scales_lifted[:], 0)
 
         bias = keep.tile([P, N // P], F32, name="bias")
         gains = keep.tile([P, PASSES, PACK], F32, name="gains")
@@ -85,41 +86,37 @@ def tile_list_gated_edge_messages_kernel(
         identity = keep.tile([P, P], F32, name="identity")
         nc.gpsimd.memset(vec_rows[:], 0.0)
         make_identity(nc, identity[:])
+
         nc.sync.dma_start(wg[:], wg_words.bitcast(I32).rearrange("a p n -> p a n"))
-        nc.sync.dma_start(vec_rows[4 : 4 + N // P, 0:P], bg.rearrange("(i p) -> i p", p=P))
-        tab_rows = tab_scales.bitcast(I32).rearrange("a (q r) n -> r q a n", r=4)
-        for r in range(4):
-            nc.sync.dma_start(tab_planes[r:P:16, :], tab_rows[r])
+        nc.sync.dma_start(vec_rows[BIAS_ROW : BIAS_ROW + N // P, 0:P], bg.rearrange("(i p) -> i p", p=P))
+        tab_rows = tab_scales.bitcast(I32).rearrange("a (q r) n -> r q a n", r=PLANE_ROWS)
+        for r in range(PLANE_ROWS):
+            nc.sync.dma_start(tab_planes[r:P:PASS1_DROP, :], tab_rows[r])
         table = [load_table(0, "table0")]
         nc.sync.dma_start(vec_rows[0:PASSES, :], gain.rearrange("(b c) -> b c", b=PASSES))
-        load_planes(wg_plane_words, wg_scales)
+        load_weight_planes(wg_scales)
         table.append(load_table(1, "slot_b"))
+
         bias_turned = psum.tile([P, P], F32, name="bank6")
         nc.tensor.transpose(bias_turned[:], vec_rows[:, 0:P], identity[:])
         gains_turned = psum.tile([P, PACK, P], F32, name="bank7")
         for t in range(PACK):
             nc.tensor.transpose(gains_turned[:, t, :], vec_rows[:, t:PASS:PACK], identity[:])
-        nc.scalar.copy(bias[:], bias_turned[:, 4 : 4 + N // P])
+        nc.scalar.copy(bias[:], bias_turned[:, BIAS_ROW : BIAS_ROW + N // P])
         nc.scalar.copy(gains[:], gains_turned[:, :, 0:PASSES].rearrange("p t b -> p b t"))
 
         w1_words = keep.tile([P, PASSES, H], U32, name="w1_words", align_bytes=64)
         w1_scales = keep.tile([P, PASSES, H], U8, name="w1_scales", align_bytes=64)
         grouped = {}
-        GROUPED_TAGS = {(1, 1): "pin_a"}
 
-        def cast_views(b, a, m0, m1):
+        def round_w1(copy, b, a, m0, m1):
             if (b, a) not in grouped:
-                tag = GROUPED_TAGS.get((b, a), f"grouped{b}{a}")
+                tag = "second_tanh" if (b, a) == (1, 1) else f"grouped{b}{a}"
                 grouped[b, a] = keep.tile([P, PACK, P, PACK], BF16, name=tag, align_bytes=64)
-            dst = grouped[b, a][:, :, m0:m1, :].rearrange("p t m j -> p m j t")
-            src = raw[b, a][:, :, PACK * m0 : PACK * m1].rearrange("p j (m t) -> p m j t", t=PACK)
-            return dst, src
-
-        def cast_on_vector(b, a, m0, m1):
-            nc.vector.tensor_copy(*cast_views(b, a, m0, m1))
-
-        def cast_on_scalar(b, a, m0, m1):
-            nc.scalar.copy(*cast_views(b, a, m0, m1))
+            copy(
+                grouped[b, a][:, :, m0:m1, :].rearrange("p t m j -> p m j t"),
+                raw[b, a][:, :, PACK * m0 : PACK * m1].rearrange("p j (m t) -> p m j t", t=PACK),
+            )
 
         def quantize_w1(b, a):
             cols = slice(b * PASS, (b + 1) * PASS)
@@ -132,61 +129,45 @@ def tile_list_gated_edge_messages_kernel(
         v_words = keep.tile([P, PASSES, S], U32, name="v_words", align_bytes=64)
         v_scales = keep.tile([P, S], U8, name="v_scales", align_bytes=64)
         nc.vector.tensor_copy(v_scales[:], tab_planes[:].bitcast(U8).indirect(offsets[:]))
-        for r in range(4):
-            nc.sync.dma_start(v_scales_low[r:P:32, :], v_scales[16 + r : P : 32, :].bitcast(I32))
-        load_w1(0, slots.tile([P, PASSES * PACK * PASS], F32, name="slot_a", align_bytes=64), [1, 2])
+        for r in range(PLANE_ROWS):
+            nc.sync.dma_start(v_scales_lifted[r:P:32, :], v_scales[PASS1_DROP + r : P : 32, :].bitcast(I32))
+        load_w1(0, "slot_a", [1, 2])
         nc.vector.tensor_copy(v_words[:, 0, :], table[0][:].bitcast(U32).indirect(offsets[:]))
         for half in range(2):
             nc.vector.tensor_copy(
-                v_words[:, 1, half * BANK : (half + 1) * BANK],
-                table[1][:].bitcast(U32).indirect(offsets[:, half * 32 : (half + 1) * 32]),
+                v_words[:, 1, half * HALF : (half + 1) * HALF],
+                table[1][:].bitcast(U32).indirect(offsets[:, half * HALF // 16 : (half + 1) * HALF // 16]),
             )
-        load_w1(1, slots.tile([P, PASSES * PACK * PASS], F32, name="slot_b", align_bytes=64), [2, 1])
+        load_w1(1, "slot_b", [2, 1])
+        v_planes = [v_scales[:], v_scales_lifted[:].bitcast(U8)]
 
-        gate_low = [keep.tile([P, 2, BANK], F32, name=f"gate{i}", align_bytes=64) for i in range(N // P // 2)]
-        gate_high = keep.tile([P, N // P, BANK], F32, name="gate_high")
-        gate_planes = [v_scales[:], v_scales_low[:].bitcast(U8)]
-
+        gate = [keep.tile([P, N // P, HALF], F32, name=f"gate{half}", align_bytes=64) for half in range(2)]
         gate_acc = {}
 
         def gate_pass(half, a):
-            edges = slice(half * BANK, (half + 1) * BANK)
+            edges = slice(half * HALF, (half + 1) * HALF)
             for i in range(N // P):
                 if a == 0:
-                    gate_acc[half, i] = psum.tile([P, BANK], F32, name=f"bank{GATE_BANKS[half][i]}")
+                    gate_acc[half, i] = psum.tile([P, HALF], F32, name=f"bank{half * (N // P) + i}")
                 acc = gate_acc[half, i]
                 nc.tensor.matmul_mx(
                     out=acc[:],
                     lhsT=wg[:, a, P * i // 2 : P * (i + 1) // 2].bitcast(E2M1X4),
-                    lhsT_scale=wg_planes[:, a, P * i : P * (i + 1)],
+                    lhsT_scale=weight_planes[:, a, P * i : P * (i + 1)],
                     rhs=v_words[:, a, edges].bitcast(E4M3X4),
-                    rhs_scale=gate_planes[a][:, edges],
+                    rhs_scale=v_planes[a][:, edges],
                     start=(a == 0),
                     stop=(a == PASSES - 1),
                 )
                 if a == PASSES - 1:
-                    dst = gate_high[:, i, :] if half else gate_low[i // 2][:, i % 2, :]
-                    nc.scalar.activation(dst, acc[:], ACT.Sigmoid, bias=bias[:, i : i + 1])
+                    nc.scalar.activation(gate[half][:, i, :], acc[:], ACT.Sigmoid, bias=bias[:, i : i + 1])
 
-        h_tiles = {}
-        H_TAGS = {}
-        TH_TAGS = {(0, 128): "pin_a", (0, 768): "slot_b"}
-
-        def h_views(b, start, width):
-            first = max(s0 for (b0, s0) in H_SPANS if b0 == b and s0 <= start)
-            if (b, first) not in h_tiles:
-                span = H_SPANS[b, first]
-                words = keep.tile([P, span], U32, name=f"h_words{b}_{first}", align_bytes=64)
-                scales = keep.tile([P, span], U8, name=H_TAGS.get((b, first), f"h_scales{b}_{first}"), align_bytes=64)
-                h_tiles[b, first] = (words, scales)
-            words, scales = h_tiles[b, first]
-            cols = slice(start - first, start - first + width)
-            return words[:, cols].bitcast(E4M3X4), scales[:, cols]
+        opened = {}
         tanh_of = {}
-        h_of = {}
+        rows_of = {}
+        rounded_of = {}
+        h_tiles = {}
         y_of = {}
-
-        m_acc = {}
 
         def first_layer_pass(acc, b, t, a, edges, start, stop):
             cols = slice(b * PASS + t * P, b * PASS + (t + 1) * P)
@@ -195,202 +176,194 @@ def tile_list_gated_edge_messages_kernel(
                 lhsT=w1_words[:, a, cols].bitcast(E4M3X4),
                 lhsT_scale=w1_scales[:, a, cols],
                 rhs=v_words[:, a, edges].bitcast(E4M3X4),
-                rhs_scale=gate_planes[a][:, edges],
+                rhs_scale=v_planes[a][:, edges],
                 start=start,
                 stop=stop,
             )
 
-        def first_pass_ahead(b, start, width, share):
-            for n, j0 in enumerate(range(start, start + width, P)):
-                acc = psum.tile([P, PACK, P], F32, name=f"bank{FIRST_BANKS[b, start][n]}")
-                m_acc[b, j0] = acc
+        def open_first_layer(unit):
+            b, first, width, banks = unit
+            for j0, bank in zip(range(first, first + width, P), banks):
+                acc = psum.tile([P, PACK, P], F32, name=f"bank{bank}")
+                opened[b, j0] = acc
                 for t in range(PACK):
                     first_layer_pass(acc[:, t, :], b, t, 0, slice(j0, j0 + P), t == 0, False)
 
-        def first_layer(b, start, width, share):
-            block = min(width, 128 if share >= 0 else 256)
-            per_bank = BANK // block
-            groups = PACK // per_bank
-            banks = FIRST_BANKS[b, start]
-            if (b, start) in TH_TAGS:
-                pool = slots if TH_TAGS[b, start] == "slot_b" else keep
-                th = pool.tile([P, groups, width * per_bank], F32, name=TH_TAGS[b, start], align_bytes=64)
-            else:
-                th = ring.tile([P, groups, width * per_bank], F32, name="th", bufs=4)
-            for j0 in range(0, width, block):
-                for g in range(groups):
-                    edges = slice(start + j0, start + j0 + block)
-                    if (b, start + j0) in m_acc:
-                        acc = m_acc[b, start + j0]
-                        for e in range(per_bank):
-                            first_layer_pass(acc[:, e, :], b, g * per_bank + e, 1, edges, False, e == per_bank - 1)
-                    else:
-                        acc = psum.tile([P, per_bank, block], F32, name=f"bank{banks[j0 // block * groups + g]}")
-                        for e in range(per_bank):
-                            for a in range(PASSES):
-                                first_layer_pass(acc[:, e, :], b, g * per_bank + e, a, edges, a == 0, a == PASSES - 1)
-                    if share < 0:
-                        dst = th[:, g, :].rearrange("p (e j) -> p e j", e=per_bank)[:, :, j0 : j0 + block]
-                        nc.scalar.activation(dst, acc[:], ACT.Tanh)
-                    else:
-                        dst = th[:, g, :].rearrange("p (j e) -> p j e", e=per_bank)[:, j0 : j0 + block, :]
-                        nc.scalar.activation(dst, acc[:].rearrange("p e j -> p j e"), ACT.Tanh)
-            tanh_of[b, start] = th
+        def tanh_tile(unit):
+            if unit == PASS0[1]:
+                return keep.tile([P, unit[2] * PACK], F32, name="second_tanh", align_bytes=64)
+            if unit == PASS0[-1]:
+                return slots.tile([P, unit[2] * PACK], F32, name="slot_b", align_bytes=64)
+            return ring.tile([P, unit[2] * PACK], F32, name="th")
 
-        def gain_on_scalar(b, start, width, share):
+        def first_layer(unit):
+            b, first, width, banks = unit
+            th = tanh_tile(unit)
+            tanh_of[unit] = th
+            if unit in GAIN_ON_SCALAR:
+                per_bank = BANK // width
+                for g, bank in enumerate(banks):
+                    acc = psum.tile([P, per_bank, width], F32, name=f"bank{bank}")
+                    for e in range(per_bank):
+                        for a in range(PASSES):
+                            edges = slice(first, first + width)
+                            first_layer_pass(acc[:, e, :], b, g * per_bank + e, a, edges, a == 0, a == PASSES - 1)
+                    dst = th[:, g * BANK : (g + 1) * BANK].rearrange("p (e j) -> p e j", e=per_bank)
+                    nc.scalar.activation(dst, acc[:], ACT.Tanh)
+                return
+            for n, bank in enumerate(banks):
+                edges = slice(first + n * P, first + (n + 1) * P)
+                if (b, edges.start) in opened:
+                    acc = opened[b, edges.start]
+                    for t in range(PACK):
+                        first_layer_pass(acc[:, t, :], b, t, 1, edges, False, t == PACK - 1)
+                else:
+                    acc = psum.tile([P, PACK, P], F32, name=f"bank{bank}")
+                    for t in range(PACK):
+                        for a in range(PASSES):
+                            first_layer_pass(acc[:, t, :], b, t, a, edges, a == 0, a == PASSES - 1)
+                dst = th[:, n * BANK : (n + 1) * BANK].rearrange("p (j t) -> p j t", t=PACK)
+                nc.scalar.activation(dst, acc[:].rearrange("p t j -> p j t"), ACT.Tanh)
+
+        def gain_on_scalar(unit):
+            b, first, width, banks = unit
             rows = ring.tile([P, PACK, width], BF16, name="rows")
-            by_t = tanh_of[b, start][:].rearrange("p g (e j) -> p (g e) j", j=width)
+            rows_of[unit] = rows
+            by_t = tanh_of[unit][:].rearrange("p (t j) -> p t j", t=PACK)
             for t in range(PACK):
                 nc.scalar.activation(rows[:, t, :], by_t[:, t, :], ACT.Copy, scale=gains[:, b, t : t + 1])
-            tanh_of[b, start] = rows
 
-        def apply_gain(b, start, width, share):
-            if (b, start) in HB_TAGS:
-                hb = slots.tile([P, width, PACK], BF16, name=HB_TAGS[b, start], align_bytes=64)
+        def make_h(unit):
+            b, first, width, banks = unit
+            if unit == PASS1[-1]:
+                hb = slots.tile([P, width, PACK], BF16, name="last_h", align_bytes=64)
             else:
-                hb = ring.tile([P, width, PACK], BF16, name="hb", align_bytes=64, bufs=4)
-            h_of[b, start] = hb
-            if share < 0:
+                hb = ring.tile([P, width, PACK], BF16, name="hb", align_bytes=64)
+            rounded_of[unit] = hb
+            if unit in GAIN_ON_SCALAR:
                 nc.vector.tensor_copy(
                     hb[:].rearrange("p (c i) t -> p c t i", i=4),
-                    tanh_of[b, start][:].rearrange("p t (c i) -> p c t i", i=4),
+                    rows_of[unit][:].rearrange("p t (c i) -> p c t i", i=4),
                 )
-                return
-            per_bank = BANK // min(width, 128 if share >= 0 else 256)
-            src = tanh_of[b, start][:].rearrange("p g (j e) -> p j g e", e=per_bank)
-            dst = hb[:].rearrange("p j (g e) -> p j g e", e=per_bank)
-            for engine, j0, j1, factor in (
-                (nc.vector, 0, share, gains[:, b, :]),
-            ) + tuple((nc.gpsimd, j, min(j + 64, width), gains[:, b, :]) for j in range(share, width, 64)):
-                if j1 > j0:
-                    factor = factor.rearrange("p (g e) -> p g e", e=per_bank).unsqueeze(1)
-                    factor = factor.to_broadcast([P, j1 - j0, PACK // per_bank, per_bank])
-                    engine.tensor_tensor(dst[:, j0:j1], src[:, j0:j1], factor, MULT)
+            else:
+                factor = gains[:, b : b + 1, :].to_broadcast([P, width, PACK])
+                nc.vector.tensor_tensor(hb[:], tanh_of[unit][:].rearrange("p (j t) -> p j t", t=PACK), factor, MULT)
 
-        def quantize_h(b, start, width, share):
-            words, scales = h_views(b, start, width)
-            nc.vector.quantize_mx(
-                out=words,
-                scales=scales,
-                in_=h_of[b, start][:].rearrange("p j t -> p (j t)"),
-            )
+        def h_views(b, first, width):
+            half = first // HALF
+            if (b, half) not in h_tiles:
+                words = keep.tile([P, HALF], U32, name=f"h_words{b}{half}", align_bytes=64)
+                scales = keep.tile([P, HALF], U8, name=f"h_scales{b}{half}", align_bytes=64)
+                h_tiles[b, half] = (words, scales)
+            words, scales = h_tiles[b, half]
+            cols = slice(first % HALF, first % HALF + width)
+            return words[:, cols].bitcast(E4M3X4), scales[:, cols]
 
-        def second_layer_pass(acc, i, b, edges, start, stop):
-            cols = slice(P * i, P * (i + 1))
-            words, scales = h_views(b, edges.start, edges.stop - edges.start)
-            nc.tensor.matmul_mx(
-                out=acc,
-                lhsT=w2[:, b, cols].bitcast(E4M3X4),
-                lhsT_scale=w2_planes[:, b, cols],
-                rhs=words,
-                rhs_scale=scales,
-                start=start,
-                stop=stop,
-            )
+        def quantize_h(unit):
+            b, first, width, banks = unit
+            words, scales = h_views(b, first, width)
+            nc.vector.quantize_mx(out=words, scales=scales, in_=rounded_of[unit][:].rearrange("p j t -> p (j t)"))
 
-        def second_layer(start, width, passes):
-            edges = slice(start, start + width)
-            per_bank = BANK // width
-            if start not in y_of:
-                y_of[start] = [
-                    (i0, psum.tile([P, per_bank, width], F32, name=f"bank{SECOND_BANKS[start][i0 // per_bank]}"))
-                    for i0 in range(0, N // P, per_bank)
-                ]
-            for i0, acc in y_of[start]:
-                for i in range(i0, i0 + per_bank):
-                    for b in passes:
-                        alone = len(passes) == PASSES
-                        opens = b == 0 and (alone or i == i0)
-                        closes = b == PASSES - 1 and (alone or i == i0 + per_bank - 1)
-                        second_layer_pass(acc[:, i - i0, :], i, b, edges, opens, closes)
+        pair = BANK // CHUNK
+
+        def second_layer(chunk, b):
+            if b == 0:
+                y_of[chunk] = [psum.tile([P, pair, CHUNK], F32, name=f"bank{bank}") for bank in SECOND_BANKS[chunk]]
+            for i in range(N // P):
+                cols = slice(P * i, P * (i + 1))
+                words, scales = h_views(b, chunk * CHUNK, CHUNK)
+                nc.tensor.matmul_mx(
+                    out=y_of[chunk][i // pair][:, i % pair, :],
+                    lhsT=w2[:, b, cols].bitcast(E4M3X4),
+                    lhsT_scale=weight_planes[:, b, cols],
+                    rhs=words,
+                    rhs_scale=scales,
+                    start=(b == 0 and i % pair == 0),
+                    stop=(b == PASSES - 1 and i % pair == pair - 1),
+                )
 
         out_view = out.rearrange("(i p) j -> p i j", p=P)
+        last_chunk = S // CHUNK - 1
 
-        def gate_and_store(start, width, banks, parts=1):
-            edges = slice(start, start + width)
-            per_bank = BANK // width
-            for i0, acc in y_of[start][banks]:
-                if (start, i0) in RESULT_TAGS:
-                    result = slots.tile([P, per_bank, width], F32, name=RESULT_TAGS[start, i0], align_bytes=64)
-                else:
-                    result = ring.tile([P, per_bank, width], F32, name="result", bufs=8)
-                if start < BANK:
-                    factor = gate_low[i0 // 2][:, :, start : start + width]
-                else:
-                    factor = gate_high[:, i0 : i0 + per_bank, start - BANK : start - BANK + width]
-                step = per_bank // parts
-                for n in range(0, per_bank, step):
-                    nc.vector.tensor_tensor(result[:, n : n + step], acc[:, n : n + step], factor[:, n : n + step], MULT)
-                    nc.sync.dma_start(out_view[:, i0 + n : i0 + n + step, edges], result[:, n : n + step])
+        def gate_and_store(chunk, n):
+            first = chunk * CHUNK
+            if (chunk, n) == (last_chunk - 1, 1):
+                result = slots.tile([P, pair, CHUNK], F32, name="last_h", align_bytes=64)
+            else:
+                result = ring.tile([P, pair, CHUNK], F32, name="result", bufs=STORES)
+            factor = gate[first // HALF][:, n * pair : (n + 1) * pair, first % HALF : first % HALF + CHUNK]
+            step = 1 if (chunk, n) == (last_chunk, 1) else pair
+            for e in range(0, pair, step):
+                part = slice(e, e + step)
+                nc.vector.tensor_tensor(result[:, part], y_of[chunk][n][:, part], factor[:, part], MULT)
+                channels = slice(n * pair + e, n * pair + e + step)
+                nc.sync.dma_start(out_view[:, channels, first : first + CHUNK], result[:, part])
 
         for a in range(PASSES):
             for half in range(2):
                 gate_pass(half, a)
-        cast_on_vector(0, 0, 0, P)
+
+        round_w1(nc.vector.tensor_copy, 0, 0, 0, P)
         quantize_w1(0, 0)
-        first_pass_ahead(*UNITS[0])
-        first_pass_ahead(*UNITS[1])
-        first_pass_ahead(*UNITS[2])
+        for unit in PASS0[:3]:
+            open_first_layer(unit)
         for m0 in range(0, P, P // 2):
-            cast_on_vector(0, 1, m0, m0 + P // 2)
+            round_w1(nc.vector.tensor_copy, 0, 1, m0, m0 + P // 2)
         w2 = slots.tile([P, PASSES, N], I32, name="slot_a", align_bytes=64)
-        w2_planes = wg_planes
         nc.sync.dma_start(
             w2[:], w2_words.rearrange("a p n i -> a p (n i)").bitcast(I32).rearrange("a p n -> p a n")
         )
-        load_planes(wg_plane_words, w2_scales)
+        load_weight_planes(w2_scales)
         quantize_w1(0, 1)
 
-        cast_on_vector(1, 0, 0, 64)
-        cast_on_vector(1, 0, 64, 128)
-        first_layer(*UNITS[0])
-        first_layer(*UNITS[1])
-        apply_gain(*UNITS[0])
+        for m0 in range(0, P, P // 2):
+            round_w1(nc.vector.tensor_copy, 1, 0, m0, m0 + P // 2)
+        first_layer(PASS0[0])
+        first_layer(PASS0[1])
+        make_h(PASS0[0])
         quantize_w1(1, 0)
-        first_layer(*UNITS[2])
-        apply_gain(*UNITS[1])
-        quantize_h(*UNITS[0])
-        first_layer(*UNITS[3])
-        cast_on_scalar(1, 1, 40, 128)
-        apply_gain(*UNITS[2])
-        cast_on_vector(1, 1, 0, 40)
-        quantize_h(*UNITS[1])
+        first_layer(PASS0[2])
+        make_h(PASS0[1])
+        quantize_h(PASS0[0])
+        first_layer(PASS0[3])
+        round_w1(nc.scalar.copy, 1, 1, LAST_PIECE_ON_VECTOR, P)
+        make_h(PASS0[2])
+        round_w1(nc.vector.tensor_copy, 1, 1, 0, LAST_PIECE_ON_VECTOR)
+        quantize_h(PASS0[1])
         quantize_w1(1, 1)
-        first_layer(*UNITS[4])
-        first_pass_ahead(*UNITS[5])
-        apply_gain(*UNITS[3])
-        quantize_h(*UNITS[2])
-        first_layer(*UNITS[5])
-        second_layer(0, 256, [0])
-        apply_gain(*UNITS[4])
-        quantize_h(*UNITS[3])
-        first_layer(*UNITS[6])
-        second_layer(256, 256, [0])
-        gain_on_scalar(*UNITS[6])
-        apply_gain(*UNITS[5])
-        quantize_h(*UNITS[4])
-        quantize_h(*UNITS[5])
-        first_layer(*UNITS[7])
-        second_layer(0, 256, [1])
-        apply_gain(*UNITS[6])
-        second_layer(512, 256, [0])
-        gain_on_scalar(*UNITS[7])
-        gate_and_store(0, 256, slice(0, 1))
-        quantize_h(*UNITS[6])
-        first_layer(*UNITS[8])
-        second_layer(256, 256, [1])
-        gate_and_store(0, 256, slice(1, 2))
-        second_layer(768, 256, [0])
-        gain_on_scalar(*UNITS[8])
-        apply_gain(*UNITS[7])
-        gate_and_store(256, 256, slice(0, 1))
-        quantize_h(*UNITS[7])
-        second_layer(512, 256, [1])
-        gate_and_store(256, 256, slice(1, 2))
-        apply_gain(*UNITS[8])
-        gate_and_store(512, 256, slice(0, 1))
-        quantize_h(*UNITS[8])
-        second_layer(768, 256, [1])
-        gate_and_store(512, 256, slice(1, 2))
-        gate_and_store(768, 256, slice(0, 1))
-        gate_and_store(768, 256, slice(1, 2), 2)
+        first_layer(PASS0[4])
+        open_first_layer(PASS1[0])
+        make_h(PASS0[3])
+        quantize_h(PASS0[2])
+
+        first_layer(PASS1[0])
+        second_layer(0, 0)
+        make_h(PASS0[4])
+        quantize_h(PASS0[3])
+        first_layer(PASS1[1])
+        second_layer(1, 0)
+        gain_on_scalar(PASS1[1])
+        make_h(PASS1[0])
+        quantize_h(PASS0[4])
+        quantize_h(PASS1[0])
+        first_layer(PASS1[2])
+        second_layer(0, 1)
+        make_h(PASS1[1])
+        second_layer(2, 0)
+        gain_on_scalar(PASS1[2])
+        gate_and_store(0, 0)
+        quantize_h(PASS1[1])
+        first_layer(PASS1[3])
+        second_layer(1, 1)
+        gate_and_store(0, 1)
+        second_layer(3, 0)
+        gain_on_scalar(PASS1[3])
+
+        for chunk in (last_chunk - 1, last_chunk):
+            make_h(PASS1[chunk])
+            gate_and_store(chunk - 1, 0)
+            quantize_h(PASS1[chunk])
+            second_layer(chunk, 1)
+            gate_and_store(chunk - 1, 1)
+        gate_and_store(last_chunk, 0)
+        gate_and_store(last_chunk, 1)

@@ -114,8 +114,8 @@ def tile_list_gated_edge_messages_kernel(
                 tag = "second_tanh" if (b, a) == (1, 1) else f"grouped{b}{a}"
                 grouped[b, a] = keep.tile([P, PACK, P, PACK], BF16, name=tag, align_bytes=64)
             copy(
-                grouped[b, a][:, :, m0:m1, :].rearrange("p t m j -> p m j t"),
-                raw[b, a][:, :, PACK * m0 : PACK * m1].rearrange("p j (m t) -> p m j t", t=PACK),
+                grouped[b, a][:, :, m0:m1, :].rearrange("p (u e) m j -> p u m j e", e=2),
+                raw[b, a][:, :, PACK * m0 : PACK * m1].rearrange("p j (m u e) -> p u m j e", u=2, e=2),
             )
 
         def quantize_w1(b, a):

@@ -29,12 +29,13 @@ PASS1_DROP = 16
 BIAS_ROW = 4
 RING = 4
 STORES = N // P * S // BANK
-LAST_PIECE_ON_VECTOR = 40
-
-PASS0 = [(0, 0, 128, (0,)), (0, 128, 128, (1,)), (0, 256, 256, (2, 3)), (0, 512, 256, (4, 5)), (0, 768, 256, (4, 5))]
-PASS1 = [(1, 0, 256, (0, 1)), (1, 256, 256, (2, 3)), (1, 512, 256, (0, 1)), (1, 768, 256, (2, 3))]
-GAIN_ON_SCALAR = PASS1[1:]
-SECOND_BANKS = [(6, 7), (4, 5), (0, 1), (2, 3)]
+LAST_PIECE_ON_VECTOR = 48
+GAIN_BANK = 7
+FIRST_BANKS = [[1, 2, 3, 4, 5, 6, 5, 6], [2, 3, 4, 2, 3, 4, 2, 3]]
+SECOND_BANKS = [(0, 1), (5, 6), (0, 1), (5, 6)]
+SHARES = [128,64,192,144,96]
+LONGEST_SHARE = max(SHARES)
+OVERLAP = 8
 
 
 def tile_list_gated_edge_messages_kernel(
@@ -81,7 +82,6 @@ def tile_list_gated_edge_messages_kernel(
         nc.vector.memset(v_scales_lifted[:], 0)
 
         bias = keep.tile([P, N // P], F32, name="bias")
-        gains = keep.tile([P, PASSES, PACK], F32, name="gains")
         vec_rows = keep.tile([P, PASS], F32, name="vec_rows")
         identity = keep.tile([P, P], F32, name="identity")
         nc.gpsimd.memset(vec_rows[:], 0.0)
@@ -92,18 +92,24 @@ def tile_list_gated_edge_messages_kernel(
         tab_rows = tab_scales.bitcast(I32).rearrange("a (q r) n -> r q a n", r=PLANE_ROWS)
         for r in range(PLANE_ROWS):
             nc.sync.dma_start(tab_planes[r:P:PASS1_DROP, :], tab_rows[r])
-        table = [load_table(0, "table0")]
+        table = [load_table(0, "slot_c")]
         nc.sync.dma_start(vec_rows[0:PASSES, :], gain.rearrange("(b c) -> b c", b=PASSES))
         load_weight_planes(wg_scales)
         table.append(load_table(1, "slot_b"))
 
         bias_turned = psum.tile([P, P], F32, name="bank6")
         nc.tensor.transpose(bias_turned[:], vec_rows[:, 0:P], identity[:])
-        gains_turned = psum.tile([P, PACK, P], F32, name="bank7")
+        gains_turned = psum.tile([P, PACK, P], F32, name=f"bank{GAIN_BANK}")
         for t in range(PACK):
             nc.tensor.transpose(gains_turned[:, t, :], vec_rows[:, t:PASS:PACK], identity[:])
         nc.scalar.copy(bias[:], bias_turned[:, BIAS_ROW : BIAS_ROW + N // P])
-        nc.scalar.copy(gains[:], gains_turned[:, :, 0:PASSES].rearrange("p t b -> p b t"))
+
+        gain_runs = keep.tile([P, PASSES, LONGEST_SHARE * PACK], F32, name="gain_runs", align_bytes=64)
+        for b in range(PASSES):
+            nc.scalar.copy(
+                gain_runs[:, b, :].rearrange("p (j t) -> p j t", t=PACK),
+                gains_turned[:, :, b].unsqueeze(1).to_broadcast([P, LONGEST_SHARE, PACK]),
+            )
 
         w1_words = keep.tile([P, PASSES, H], U32, name="w1_words", align_bytes=64)
         w1_scales = keep.tile([P, PASSES, H], U8, name="w1_scales", align_bytes=64)
@@ -114,8 +120,8 @@ def tile_list_gated_edge_messages_kernel(
                 tag = "second_tanh" if (b, a) == (1, 1) else f"grouped{b}{a}"
                 grouped[b, a] = keep.tile([P, PACK, P, PACK], BF16, name=tag, align_bytes=64)
             copy(
-                grouped[b, a][:, :, m0:m1, :].rearrange("p (u e) m j -> p u m j e", e=2),
-                raw[b, a][:, :, PACK * m0 : PACK * m1].rearrange("p j (m u e) -> p u m j e", u=2, e=2),
+                grouped[b, a][:, :, m0:m1, :].rearrange("p t m j -> p m j t"),
+                raw[b, a][:, :, PACK * m0 : PACK * m1].rearrange("p j (m t) -> p m j t", t=PACK),
             )
 
         def quantize_w1(b, a):
@@ -138,116 +144,83 @@ def tile_list_gated_edge_messages_kernel(
                 v_words[:, 1, half * HALF : (half + 1) * HALF],
                 table[1][:].bitcast(U32).indirect(offsets[:, half * HALF // 16 : (half + 1) * HALF // 16]),
             )
-        load_w1(1, "slot_b", [2, 1])
+        load_w1(1, "slot_c", [2, 1])
         v_planes = [v_scales[:], v_scales_lifted[:].bitcast(U8)]
 
         gate = [keep.tile([P, N // P, HALF], F32, name=f"gate{half}", align_bytes=64) for half in range(2)]
         gate_acc = {}
 
-        def gate_pass(half, a):
+        def gate_pass(half, i, a):
             edges = slice(half * HALF, (half + 1) * HALF)
-            for i in range(N // P):
-                if a == 0:
-                    gate_acc[half, i] = psum.tile([P, HALF], F32, name=f"bank{half * (N // P) + i}")
-                acc = gate_acc[half, i]
-                nc.tensor.matmul_mx(
-                    out=acc[:],
-                    lhsT=wg[:, a, P * i // 2 : P * (i + 1) // 2].bitcast(E2M1X4),
-                    lhsT_scale=weight_planes[:, a, P * i : P * (i + 1)],
-                    rhs=v_words[:, a, edges].bitcast(E4M3X4),
-                    rhs_scale=v_planes[a][:, edges],
-                    start=(a == 0),
-                    stop=(a == PASSES - 1),
-                )
-                if a == PASSES - 1:
-                    nc.scalar.activation(gate[half][:, i, :], acc[:], ACT.Sigmoid, bias=bias[:, i : i + 1])
+            if a == 0:
+                gate_acc[half, i] = psum.tile([P, HALF], F32, name=f"bank{(half * (N // P) + i) % GAIN_BANK}")
+            acc = gate_acc[half, i]
+            nc.tensor.matmul_mx(
+                out=acc[:],
+                lhsT=wg[:, a, P * i // 2 : P * (i + 1) // 2].bitcast(E2M1X4),
+                lhsT_scale=weight_planes[:, a, P * i : P * (i + 1)],
+                rhs=v_words[:, a, edges].bitcast(E4M3X4),
+                rhs_scale=v_planes[a][:, edges],
+                start=(a == 0),
+                stop=(a == PASSES - 1),
+            )
+            if a == PASSES - 1:
+                nc.scalar.activation(gate[half][:, i, :], acc[:], ACT.Sigmoid, bias=bias[:, i : i + 1])
 
-        opened = {}
+        first_acc = {}
         tanh_of = {}
-        rows_of = {}
-        rounded_of = {}
         h_tiles = {}
         y_of = {}
 
-        def first_layer_pass(acc, b, t, a, edges, start, stop):
-            cols = slice(b * PASS + t * P, b * PASS + (t + 1) * P)
-            nc.tensor.matmul_mx(
-                out=acc,
-                lhsT=w1_words[:, a, cols].bitcast(E4M3X4),
-                lhsT_scale=w1_scales[:, a, cols],
-                rhs=v_words[:, a, edges].bitcast(E4M3X4),
-                rhs_scale=v_planes[a][:, edges],
-                start=start,
-                stop=stop,
-            )
-
-        def open_first_layer(unit):
-            b, first, width, banks = unit
-            for j0, bank in zip(range(first, first + width, P), banks):
-                acc = psum.tile([P, PACK, P], F32, name=f"bank{bank}")
-                opened[b, j0] = acc
-                for t in range(PACK):
-                    first_layer_pass(acc[:, t, :], b, t, 0, slice(j0, j0 + P), t == 0, False)
-
-        def tanh_tile(unit):
-            if unit == PASS0[1]:
-                return keep.tile([P, unit[2] * PACK], F32, name="second_tanh", align_bytes=64)
-            if unit == PASS0[-1]:
-                return slots.tile([P, unit[2] * PACK], F32, name="slot_b", align_bytes=64)
-            return ring.tile([P, unit[2] * PACK], F32, name="th")
-
-        def first_layer(unit):
-            b, first, width, banks = unit
-            th = tanh_tile(unit)
-            tanh_of[unit] = th
-            if unit in GAIN_ON_SCALAR:
-                per_bank = BANK // width
-                for g, bank in enumerate(banks):
-                    acc = psum.tile([P, per_bank, width], F32, name=f"bank{bank}")
-                    for e in range(per_bank):
-                        for a in range(PASSES):
-                            edges = slice(first, first + width)
-                            first_layer_pass(acc[:, e, :], b, g * per_bank + e, a, edges, a == 0, a == PASSES - 1)
-                    dst = th[:, g * BANK : (g + 1) * BANK].rearrange("p (e j) -> p e j", e=per_bank)
-                    nc.scalar.activation(dst, acc[:], ACT.Tanh)
-                return
-            for n, bank in enumerate(banks):
-                edges = slice(first + n * P, first + (n + 1) * P)
-                if (b, edges.start) in opened:
-                    acc = opened[b, edges.start]
-                    for t in range(PACK):
-                        first_layer_pass(acc[:, t, :], b, t, 1, edges, False, t == PACK - 1)
-                else:
-                    acc = psum.tile([P, PACK, P], F32, name=f"bank{bank}")
-                    for t in range(PACK):
-                        for a in range(PASSES):
-                            first_layer_pass(acc[:, t, :], b, t, a, edges, a == 0, a == PASSES - 1)
-                dst = th[:, n * BANK : (n + 1) * BANK].rearrange("p (j t) -> p j t", t=PACK)
-                nc.scalar.activation(dst, acc[:].rearrange("p t j -> p j t"), ACT.Tanh)
-
-        def gain_on_scalar(unit):
-            b, first, width, banks = unit
-            rows = ring.tile([P, PACK, width], BF16, name="rows")
-            rows_of[unit] = rows
-            by_t = tanh_of[unit][:].rearrange("p (t j) -> p t j", t=PACK)
+        def first_layer_pass(b, n, a):
+            if a == 0:
+                first_acc[b, n] = psum.tile([P, PACK, P], F32, name=f"bank{FIRST_BANKS[b][n]}")
+            edges = slice(n * P, (n + 1) * P)
             for t in range(PACK):
-                nc.scalar.activation(rows[:, t, :], by_t[:, t, :], ACT.Copy, scale=gains[:, b, t : t + 1])
-
-        def make_h(unit):
-            b, first, width, banks = unit
-            if unit == PASS1[-1]:
-                hb = slots.tile([P, width, PACK], BF16, name="last_h", align_bytes=64)
-            else:
-                hb = ring.tile([P, width, PACK], BF16, name="hb", align_bytes=64)
-            rounded_of[unit] = hb
-            if unit in GAIN_ON_SCALAR:
-                nc.vector.tensor_copy(
-                    hb[:].rearrange("p (c i) t -> p c t i", i=4),
-                    rows_of[unit][:].rearrange("p t (c i) -> p c t i", i=4),
+                cols = slice(b * PASS + t * P, b * PASS + (t + 1) * P)
+                nc.tensor.matmul_mx(
+                    out=first_acc[b, n][:, t, :],
+                    lhsT=w1_words[:, a, cols].bitcast(E4M3X4),
+                    lhsT_scale=w1_scales[:, a, cols],
+                    rhs=v_words[:, a, edges].bitcast(E4M3X4),
+                    rhs_scale=v_planes[a][:, edges],
+                    start=(a == 0 and t == 0),
+                    stop=(a == PASSES - 1 and t == PACK - 1),
                 )
+
+        def tanh(b, n):
+            if (b, n) == (0, 1):
+                th = keep.tile([P, P, PACK], F32, name="second_tanh", align_bytes=64)[:]
+            elif (b, n) == (0, 0):
+                th = keep.tile([P, P, PACK], F32, name="first_tanh", align_bytes=64)[:]
             else:
-                factor = gains[:, b : b + 1, :].to_broadcast([P, width, PACK])
-                nc.vector.tensor_tensor(hb[:], tanh_of[unit][:].rearrange("p (j t) -> p j t", t=PACK), factor, MULT)
+                if n % 2 == 0:
+                    if (b, n) == (0, 6):
+                        both = slots.tile([P, CHUNK, PACK], F32, name="slot_c", align_bytes=64)
+                    else:
+                        both = ring.tile([P, CHUNK, PACK], F32, name="th")
+                    tanh_of[b, n // 2] = both
+                th = tanh_of[b, n // 2][:, n % 2 * P : (n % 2 + 1) * P, :]
+            tanh_of[b, n, P] = th
+            nc.scalar.activation(th, first_acc[b, n][:].rearrange("p t j -> p j t"), ACT.Tanh)
+
+        def first_layer(b, n, passes):
+            for a in passes:
+                first_layer_pass(b, n, a)
+            tanh(b, n)
+
+        rounded = keep.tile([P, S * PACK], BF16, name="rounded", align_bytes=64)
+
+        def rounded_view(place, width):
+            return rounded[:, place * PACK : (place + width) * PACK]
+
+        def gain_on_vector(b, values, place, width):
+            factor = gains_turned[:, :, b].unsqueeze(1).to_broadcast([P, width, PACK])
+            nc.vector.tensor_tensor(rounded_view(place, width).rearrange("p (j t) -> p j t", t=PACK), values, factor, MULT)
+
+        def gain_on_gpsimd(b, values, place, width):
+            flat = values.rearrange("p j t -> p (j t)")
+            nc.gpsimd.tensor_tensor(rounded_view(place, width), flat, gain_runs[:, b, 0 : width * PACK], MULT)
 
         def h_views(b, first, width):
             half = first // HALF
@@ -259,54 +232,60 @@ def tile_list_gated_edge_messages_kernel(
             cols = slice(first % HALF, first % HALF + width)
             return words[:, cols].bitcast(E4M3X4), scales[:, cols]
 
-        def quantize_h(unit):
-            b, first, width, banks = unit
+        def quantize_h(b, first, width, place):
             words, scales = h_views(b, first, width)
-            nc.vector.quantize_mx(out=words, scales=scales, in_=rounded_of[unit][:].rearrange("p j t -> p (j t)"))
+            nc.vector.quantize_mx(out=words, scales=scales, in_=rounded_view(place, width))
+
+        high, low, top = HALF - OVERLAP, CHUNK, HALF + CHUNK
+
+        def gain_part(apply, b, chunk, place, e0, e1):
+            apply(b, tanh_of[b, chunk][:, e0:e1, :], place + e0, e1 - e0)
 
         pair = BANK // CHUNK
 
-        def second_layer(chunk, b):
-            if b == 0:
-                y_of[chunk] = [psum.tile([P, pair, CHUNK], F32, name=f"bank{bank}") for bank in SECOND_BANKS[chunk]]
-            for i in range(N // P):
-                cols = slice(P * i, P * (i + 1))
-                words, scales = h_views(b, chunk * CHUNK, CHUNK)
-                nc.tensor.matmul_mx(
-                    out=y_of[chunk][i // pair][:, i % pair, :],
-                    lhsT=w2[:, b, cols].bitcast(E4M3X4),
-                    lhsT_scale=weight_planes[:, b, cols],
-                    rhs=words,
-                    rhs_scale=scales,
-                    start=(b == 0 and i % pair == 0),
-                    stop=(b == PASSES - 1 and i % pair == pair - 1),
-                )
+        def second_layer(chunk, b, banks=(0, 1)):
+            for n in banks:
+                if b == 0:
+                    y_of[chunk, n] = psum.tile([P, pair, CHUNK], F32, name=f"bank{SECOND_BANKS[chunk][n]}")
+                for e in range(pair):
+                    cols = slice(P * (n * pair + e), P * (n * pair + e + 1))
+                    words, scales = h_views(b, chunk * CHUNK, CHUNK)
+                    nc.tensor.matmul_mx(
+                        out=y_of[chunk, n][:, e, :],
+                        lhsT=w2[:, b, cols].bitcast(E4M3X4),
+                        lhsT_scale=weight_planes[:, b, cols],
+                        rhs=words,
+                        rhs_scale=scales,
+                        start=(b == 0 and e == 0),
+                        stop=(b == PASSES - 1 and e == pair - 1),
+                    )
 
         out_view = out.rearrange("(i p) j -> p i j", p=P)
         last_chunk = S // CHUNK - 1
 
         def gate_and_store(chunk, n):
             first = chunk * CHUNK
-            if (chunk, n) == (last_chunk - 1, 1):
-                result = slots.tile([P, pair, CHUNK], F32, name="last_h", align_bytes=64)
-            else:
-                result = ring.tile([P, pair, CHUNK], F32, name="result", bufs=STORES)
+            result = ring.tile([P, pair, CHUNK], F32, name="result", bufs=STORES)
             factor = gate[first // HALF][:, n * pair : (n + 1) * pair, first % HALF : first % HALF + CHUNK]
             step = 1 if (chunk, n) == (last_chunk, 1) else pair
             for e in range(0, pair, step):
                 part = slice(e, e + step)
-                nc.vector.tensor_tensor(result[:, part], y_of[chunk][n][:, part], factor[:, part], MULT)
+                nc.vector.tensor_tensor(result[:, part], y_of[chunk, n][:, part], factor[:, part], MULT)
                 channels = slice(n * pair + e, n * pair + e + step)
                 nc.sync.dma_start(out_view[:, channels, first : first + CHUNK], result[:, part])
 
+        outputs = [(half, i) for half in range(2) for i in range(N // P)]
+        for half, i in outputs[:GAIN_BANK]:
+            gate_pass(half, i, 0)
+        for half, i in outputs[:GAIN_BANK]:
+            gate_pass(half, i, 1)
         for a in range(PASSES):
-            for half in range(2):
-                gate_pass(half, a)
+            gate_pass(*outputs[GAIN_BANK], a)
 
         round_w1(nc.vector.tensor_copy, 0, 0, 0, P)
         quantize_w1(0, 0)
-        for unit in PASS0[:3]:
-            open_first_layer(unit)
+        for n in range(6):
+            first_layer_pass(0, n, 0)
         for m0 in range(0, P, P // 2):
             round_w1(nc.vector.tensor_copy, 0, 1, m0, m0 + P // 2)
         w2 = slots.tile([P, PASSES, N], I32, name="slot_a", align_bytes=64)
@@ -318,52 +297,64 @@ def tile_list_gated_edge_messages_kernel(
 
         for m0 in range(0, P, P // 2):
             round_w1(nc.vector.tensor_copy, 1, 0, m0, m0 + P // 2)
-        first_layer(PASS0[0])
-        first_layer(PASS0[1])
-        make_h(PASS0[0])
+        first_layer(0, 0, [1])
+        first_layer(0, 1, [1])
+        gain_on_vector(0, tanh_of[0, 0, P], 0, P)
         quantize_w1(1, 0)
-        first_layer(PASS0[2])
-        make_h(PASS0[1])
-        quantize_h(PASS0[0])
-        first_layer(PASS0[3])
+        first_layer(0, 2, [1])
+        first_layer(0, 3, [1])
+        gain_on_vector(0, tanh_of[0, 1, P], P, P)
+        first_layer(0, 4, [1])
+        first_layer(0, 5, [1])
+        gain_on_vector(0, tanh_of[0, 1][:], CHUNK, CHUNK)
         round_w1(nc.scalar.copy, 1, 1, LAST_PIECE_ON_VECTOR, P)
-        make_h(PASS0[2])
         round_w1(nc.vector.tensor_copy, 1, 1, 0, LAST_PIECE_ON_VECTOR)
-        quantize_h(PASS0[1])
+        first_layer(0, 6, [0, 1])
+        first_layer(0, 7, [0, 1])
+        for n in range(3):
+            first_layer_pass(1, n, 0)
+        quantize_h(0, 0, HALF, 0)
         quantize_w1(1, 1)
-        first_layer(PASS0[4])
-        open_first_layer(PASS1[0])
-        make_h(PASS0[3])
-        quantize_h(PASS0[2])
 
-        first_layer(PASS1[0])
+        gain_part(gain_on_gpsimd, 0, 2, high, 0, SHARES[0])
+        gain_part(gain_on_vector, 0, 2, high, SHARES[0], CHUNK)
+        gain_part(gain_on_vector, 0, 3, top, 0, P)
+        for n in range(3):
+            first_layer(1, n, [1])
         second_layer(0, 0)
-        make_h(PASS0[4])
-        quantize_h(PASS0[3])
-        first_layer(PASS1[1])
-        second_layer(1, 0)
-        gain_on_scalar(PASS1[1])
-        make_h(PASS1[0])
-        quantize_h(PASS0[4])
-        quantize_h(PASS1[0])
-        first_layer(PASS1[2])
+        quantize_h(0, 2 * CHUNK, CHUNK, high)
+        first_layer(1, 3, [0, 1])
+        gain_part(gain_on_vector, 1, 0, low, 0, CHUNK - SHARES[1])
+        gain_part(gain_on_gpsimd, 1, 0, low, CHUNK - SHARES[1], CHUNK)
+        first_layer(1, 4, [0, 1])
+        quantize_h(1, 0, CHUNK, low)
         second_layer(0, 1)
-        make_h(PASS1[1])
-        second_layer(2, 0)
-        gain_on_scalar(PASS1[2])
-        gate_and_store(0, 0)
-        quantize_h(PASS1[1])
-        first_layer(PASS1[3])
-        second_layer(1, 1)
-        gate_and_store(0, 1)
-        second_layer(3, 0)
-        gain_on_scalar(PASS1[3])
+        second_layer(1, 0)
+        first_layer(1, 5, [0, 1])
 
-        for chunk in (last_chunk - 1, last_chunk):
-            make_h(PASS1[chunk])
-            gate_and_store(chunk - 1, 0)
-            quantize_h(PASS1[chunk])
-            second_layer(chunk, 1)
-            gate_and_store(chunk - 1, 1)
-        gate_and_store(last_chunk, 0)
-        gate_and_store(last_chunk, 1)
+        gain_part(gain_on_gpsimd, 1, 1, high, 0, SHARES[2])
+        gain_part(gain_on_vector, 0, 3, top, P, CHUNK)
+        gain_part(gain_on_vector, 1, 1, high, SHARES[2], CHUNK)
+        gate_and_store(0, 0)
+        gate_and_store(0, 1)
+        first_layer(1, 6, [0, 1])
+        quantize_h(0, 3 * CHUNK, CHUNK, top)
+        quantize_h(1, CHUNK, CHUNK, high)
+        second_layer(1, 1)
+        first_layer(1, 7, [0, 1])
+        second_layer(2, 0)
+        gain_part(gain_on_vector, 1, 2, low, 0, CHUNK - SHARES[3])
+        gain_part(gain_on_gpsimd, 1, 2, low, CHUNK - SHARES[3], CHUNK)
+        gate_and_store(1, 0)
+        gate_and_store(1, 1)
+        quantize_h(1, 2 * CHUNK, CHUNK, low)
+        second_layer(2, 1)
+        second_layer(3, 0)
+        gain_part(gain_on_gpsimd, 1, 3, high, 0, SHARES[4])
+        gain_part(gain_on_vector, 1, 3, high, SHARES[4], CHUNK)
+        gate_and_store(2, 0)
+        quantize_h(1, 3 * CHUNK, CHUNK, high)
+        second_layer(3, 1)
+        gate_and_store(2, 1)
+        gate_and_store(3, 0)
+        gate_and_store(3, 1)

@@ -33,8 +33,9 @@ LAST_PIECE_ON_VECTOR = 48
 GAIN_BANK = 7
 FIRST_BANKS = [[1, 2, 3, 4, 5, 6, 5, 6], [2, 3, 4, 2, 3, 4, 2, 3]]
 SECOND_BANKS = [(0, 1), (5, 6), (0, 1), (5, 6)]
-SHARES = [128,64,192,144,96]
+SHARES = [128,64,160,128,80]
 LONGEST_SHARE = max(SHARES)
+H_ORDER = [(0, 0), (0, 1), (0, 2), (1, 0), (1, 1), (0, 3), (1, 2), (1, 3)]
 OVERLAP = 8
 
 
@@ -209,10 +210,11 @@ def tile_list_gated_edge_messages_kernel(
                 first_layer_pass(b, n, a)
             tanh(b, n)
 
-        rounded = keep.tile([P, S * PACK], BF16, name="rounded", align_bytes=64)
+        rounded = [keep.tile([P, HALF * PACK], BF16, name="rounded_first", align_bytes=64)]
 
         def rounded_view(place, width):
-            return rounded[:, place * PACK : (place + width) * PACK]
+            tile, start = (rounded[0], place) if place < HALF else (rounded[1], place - HALF)
+            return tile[:, start * PACK : (start + width) * PACK]
 
         def gain_on_vector(b, values, place, width):
             factor = gains_turned[:, :, b].unsqueeze(1).to_broadcast([P, width, PACK])
@@ -222,21 +224,21 @@ def tile_list_gated_edge_messages_kernel(
             flat = values.rearrange("p j t -> p (j t)")
             nc.gpsimd.tensor_tensor(rounded_view(place, width), flat, gain_runs[:, b, 0 : width * PACK], MULT)
 
-        def h_views(b, first, width):
-            half = first // HALF
-            if (b, half) not in h_tiles:
-                words = keep.tile([P, HALF], U32, name=f"h_words{b}{half}", align_bytes=64)
-                scales = keep.tile([P, HALF], U8, name=f"h_scales{b}{half}", align_bytes=64)
-                h_tiles[b, half] = (words, scales)
-            words, scales = h_tiles[b, half]
-            cols = slice(first % HALF, first % HALF + width)
+        def h_views(b, chunk, width):
+            tile, half = divmod(H_ORDER.index((b, chunk)), 2)
+            if tile not in h_tiles:
+                words = keep.tile([P, HALF], U32, name=f"h_words{tile}", align_bytes=64)
+                scales = keep.tile([P, HALF], U8, name=f"h_scales{tile}", align_bytes=64)
+                h_tiles[tile] = (words, scales)
+            words, scales = h_tiles[tile]
+            cols = slice(half * CHUNK, half * CHUNK + width)
             return words[:, cols].bitcast(E4M3X4), scales[:, cols]
 
-        def quantize_h(b, first, width, place):
-            words, scales = h_views(b, first, width)
+        def quantize_h(b, chunk, width, place):
+            words, scales = h_views(b, chunk, width)
             nc.vector.quantize_mx(out=words, scales=scales, in_=rounded_view(place, width))
 
-        high, low, top = HALF - OVERLAP, CHUNK, HALF + CHUNK
+        low, high, top = HALF, HALF + CHUNK - OVERLAP, S - OVERLAP
 
         def gain_part(apply, b, chunk, place, e0, e1):
             apply(b, tanh_of[b, chunk][:, e0:e1, :], place + e0, e1 - e0)
@@ -249,7 +251,7 @@ def tile_list_gated_edge_messages_kernel(
                     y_of[chunk, n] = psum.tile([P, pair, CHUNK], F32, name=f"bank{SECOND_BANKS[chunk][n]}")
                 for e in range(pair):
                     cols = slice(P * (n * pair + e), P * (n * pair + e + 1))
-                    words, scales = h_views(b, chunk * CHUNK, CHUNK)
+                    words, scales = h_views(b, chunk, CHUNK)
                     nc.tensor.matmul_mx(
                         out=y_of[chunk, n][:, e, :],
                         lhsT=w2[:, b, cols].bitcast(E4M3X4),
@@ -315,6 +317,7 @@ def tile_list_gated_edge_messages_kernel(
             first_layer_pass(1, n, 0)
         quantize_h(0, 0, HALF, 0)
         quantize_w1(1, 1)
+        rounded.append(keep.tile([P, (HALF + CHUNK) * PACK], BF16, name="second_tanh", align_bytes=64))
 
         gain_part(gain_on_gpsimd, 0, 2, high, 0, SHARES[0])
         gain_part(gain_on_vector, 0, 2, high, SHARES[0], CHUNK)
@@ -322,7 +325,7 @@ def tile_list_gated_edge_messages_kernel(
         for n in range(3):
             first_layer(1, n, [1])
         second_layer(0, 0)
-        quantize_h(0, 2 * CHUNK, CHUNK, high)
+        quantize_h(0, 2, CHUNK, high)
         first_layer(1, 3, [0, 1])
         gain_part(gain_on_vector, 1, 0, low, 0, CHUNK - SHARES[1])
         gain_part(gain_on_gpsimd, 1, 0, low, CHUNK - SHARES[1], CHUNK)
@@ -338,8 +341,7 @@ def tile_list_gated_edge_messages_kernel(
         gate_and_store(0, 0)
         gate_and_store(0, 1)
         first_layer(1, 6, [0, 1])
-        quantize_h(0, 3 * CHUNK, CHUNK, top)
-        quantize_h(1, CHUNK, CHUNK, high)
+        quantize_h(1, 1, HALF, high)
         second_layer(1, 1)
         first_layer(1, 7, [0, 1])
         second_layer(2, 0)
@@ -347,13 +349,13 @@ def tile_list_gated_edge_messages_kernel(
         gain_part(gain_on_gpsimd, 1, 2, low, CHUNK - SHARES[3], CHUNK)
         gate_and_store(1, 0)
         gate_and_store(1, 1)
-        quantize_h(1, 2 * CHUNK, CHUNK, low)
+        quantize_h(1, 2, CHUNK, low)
         second_layer(2, 1)
         second_layer(3, 0)
         gain_part(gain_on_gpsimd, 1, 3, high, 0, SHARES[4])
         gain_part(gain_on_vector, 1, 3, high, SHARES[4], CHUNK)
         gate_and_store(2, 0)
-        quantize_h(1, 3 * CHUNK, CHUNK, high)
+        quantize_h(1, 3, CHUNK, high)
         second_layer(3, 1)
         gate_and_store(2, 1)
         gate_and_store(3, 0)

@@ -29,11 +29,13 @@ PASS1_DROP = 16
 BIAS_ROW = 4
 RING = 4
 STORES = N // P * S // BANK
-LAST_PIECE_ON_VECTOR = 48
+LAST_PIECE_ON_VECTOR = 64
 GAIN_BANK = 7
-FIRST_BANKS = [[1, 2, 3, 4, 5, 6, 5, 6], [2, 3, 4, 2, 3, 4, 2, 3]]
-SECOND_BANKS = [(0, 1), (5, 6), (0, 1), (5, 6)]
+FIRST_BANKS = [[0, 1, 2, 3, 4, 5, 4, 5], [6, 2, 3, 6, 2, 3, 6, 2]]
+GATE_BANKS = [0, 1, 2, 3, 4, 5, 6, 4]
+SECOND_BANKS = [(0, 1), (4, 5), (0, 1), (4, 5)]
 SHARES = [128,64,160,128,80]
+FIRST_SHARE = 128
 LONGEST_SHARE = max(SHARES)
 H_ORDER = [(0, 0), (0, 1), (0, 2), (1, 0), (1, 1), (0, 3), (1, 2), (1, 3)]
 OVERLAP = 8
@@ -68,10 +70,10 @@ def tile_list_gated_edge_messages_kernel(
             nc.sync.dma_start(words[:], tab_words[a].rearrange("p t i -> p (t i)").bitcast(I32))
             return words
 
-        def load_weight_planes(scales):
+        def load_weight_planes(scales, drop):
             rows = scales.bitcast(I32).rearrange("a (q r) n -> r q a n", r=PLANE_ROWS)
             for r in range(PLANE_ROWS):
-                nc.sync.dma_start(weight_plane_words[r:P:32], rows[r])
+                nc.sync.dma_start(weight_plane_words[drop + r : P : 32], rows[r])
 
         tab_planes = slots.tile([P, T // 4], I32, name="slot_a", align_bytes=64)
         v_scales_lifted = keep.tile([P, S // 4], I32, name="v_scales_lifted", align_bytes=64)
@@ -95,7 +97,7 @@ def tile_list_gated_edge_messages_kernel(
             nc.sync.dma_start(tab_planes[r:P:PASS1_DROP, :], tab_rows[r])
         table = [load_table(0, "slot_c")]
         nc.sync.dma_start(vec_rows[0:PASSES, :], gain.rearrange("(b c) -> b c", b=PASSES))
-        load_weight_planes(wg_scales)
+        load_weight_planes(wg_scales, 0)
         table.append(load_table(1, "slot_b"))
 
         bias_turned = psum.tile([P, P], F32, name="bank6")
@@ -154,7 +156,7 @@ def tile_list_gated_edge_messages_kernel(
         def gate_pass(half, i, a):
             edges = slice(half * HALF, (half + 1) * HALF)
             if a == 0:
-                gate_acc[half, i] = psum.tile([P, HALF], F32, name=f"bank{(half * (N // P) + i) % GAIN_BANK}")
+                gate_acc[half, i] = psum.tile([P, HALF], F32, name=f"bank{GATE_BANKS[half * (N // P) + i]}")
             acc = gate_acc[half, i]
             nc.tensor.matmul_mx(
                 out=acc[:],
@@ -190,19 +192,15 @@ def tile_list_gated_edge_messages_kernel(
                 )
 
         def tanh(b, n):
-            if (b, n) == (0, 1):
-                th = keep.tile([P, P, PACK], F32, name="second_tanh", align_bytes=64)[:]
-            elif (b, n) == (0, 0):
-                th = keep.tile([P, P, PACK], F32, name="first_tanh", align_bytes=64)[:]
-            else:
-                if n % 2 == 0:
-                    if (b, n) == (0, 6):
-                        both = slots.tile([P, CHUNK, PACK], F32, name="slot_c", align_bytes=64)
-                    else:
-                        both = ring.tile([P, CHUNK, PACK], F32, name="th")
-                    tanh_of[b, n // 2] = both
-                th = tanh_of[b, n // 2][:, n % 2 * P : (n % 2 + 1) * P, :]
-            tanh_of[b, n, P] = th
+            if n % 2 == 0:
+                if (b, n) == (0, 0):
+                    both = keep.tile([P, CHUNK, PACK], F32, name="second_tanh", align_bytes=64)
+                elif (b, n) == (0, 6):
+                    both = slots.tile([P, CHUNK, PACK], F32, name="slot_c", align_bytes=64)
+                else:
+                    both = ring.tile([P, CHUNK, PACK], F32, name="th")
+                tanh_of[b, n // 2] = both
+            th = tanh_of[b, n // 2][:, n % 2 * P : (n % 2 + 1) * P, :]
             nc.scalar.activation(th, first_acc[b, n][:].rearrange("p t j -> p j t"), ACT.Tanh)
 
         def first_layer(b, n, passes):
@@ -210,7 +208,7 @@ def tile_list_gated_edge_messages_kernel(
                 first_layer_pass(b, n, a)
             tanh(b, n)
 
-        rounded = [keep.tile([P, HALF * PACK], BF16, name="rounded_first", align_bytes=64)]
+        rounded = []
 
         def rounded_view(place, width):
             tile, start = (rounded[0], place) if place < HALF else (rounded[1], place - HALF)
@@ -255,7 +253,7 @@ def tile_list_gated_edge_messages_kernel(
                     nc.tensor.matmul_mx(
                         out=y_of[chunk, n][:, e, :],
                         lhsT=w2[:, b, cols].bitcast(E4M3X4),
-                        lhsT_scale=weight_planes[:, b, cols],
+                        lhsT_scale=weight_planes[PLANE_ROWS:P, b, cols],
                         rhs=words,
                         rhs_scale=scales,
                         start=(b == 0 and e == 0),
@@ -281,8 +279,6 @@ def tile_list_gated_edge_messages_kernel(
             gate_pass(half, i, 0)
         for half, i in outputs[:GAIN_BANK]:
             gate_pass(half, i, 1)
-        for a in range(PASSES):
-            gate_pass(*outputs[GAIN_BANK], a)
 
         round_w1(nc.vector.tensor_copy, 0, 0, 0, P)
         quantize_w1(0, 0)
@@ -294,18 +290,19 @@ def tile_list_gated_edge_messages_kernel(
         nc.sync.dma_start(
             w2[:], w2_words.rearrange("a p n i -> a p (n i)").bitcast(I32).rearrange("a p n -> p a n")
         )
-        load_weight_planes(w2_scales)
+        load_weight_planes(w2_scales, PLANE_ROWS)
         quantize_w1(0, 1)
 
         for m0 in range(0, P, P // 2):
             round_w1(nc.vector.tensor_copy, 1, 0, m0, m0 + P // 2)
+        quantize_w1(1, 0)
         first_layer(0, 0, [1])
         first_layer(0, 1, [1])
-        gain_on_vector(0, tanh_of[0, 0, P], 0, P)
-        quantize_w1(1, 0)
+        rounded.append(keep.tile([P, HALF * PACK], BF16, name="grouped10", align_bytes=64))
+        gain_part(gain_on_gpsimd, 0, 0, 0, 0, FIRST_SHARE)
+        gain_part(gain_on_vector, 0, 0, 0, FIRST_SHARE, CHUNK)
         first_layer(0, 2, [1])
         first_layer(0, 3, [1])
-        gain_on_vector(0, tanh_of[0, 1, P], P, P)
         first_layer(0, 4, [1])
         first_layer(0, 5, [1])
         gain_on_vector(0, tanh_of[0, 1][:], CHUNK, CHUNK)
@@ -329,6 +326,8 @@ def tile_list_gated_edge_messages_kernel(
         first_layer(1, 3, [0, 1])
         gain_part(gain_on_vector, 1, 0, low, 0, CHUNK - SHARES[1])
         gain_part(gain_on_gpsimd, 1, 0, low, CHUNK - SHARES[1], CHUNK)
+        for a in range(PASSES):
+            gate_pass(*outputs[GAIN_BANK], a)
         first_layer(1, 4, [0, 1])
         quantize_h(1, 0, CHUNK, low)
         second_layer(0, 1)

@@ -87,15 +87,17 @@ def tile_list_gated_edge_messages_kernel(
         bias = keep.tile([P, N // P], F32, name="bias")
         vec_rows = keep.tile([P, PASS], F32, name="vec_rows")
         identity = keep.tile([P, P], F32, name="identity")
-        nc.gpsimd.memset(vec_rows[:], 0.0)
-        make_identity(nc, identity[:])
+        nc.vector.memset(vec_rows[:], 0.0)
+        nc.vector.memset(identity[:], 0.0)
+        make_identity(nc, identity[:], nomemset=True)
 
-        nc.sync.dma_start(wg[:], wg_words.bitcast(I32).rearrange("a p n -> p a n"))
-        nc.sync.dma_start(vec_rows[BIAS_ROW : BIAS_ROW + N // P, 0:P], bg.rearrange("(i p) -> i p", p=P))
+        for a in range(PASSES):
+            nc.sync.dma_start(wg[:, a, :], wg_words[a].bitcast(I32))
         tab_rows = tab_scales.bitcast(I32).rearrange("a (q r) n -> r q a n", r=PLANE_ROWS)
         for r in range(PLANE_ROWS):
             nc.sync.dma_start(tab_planes[r:P:PASS1_DROP, :], tab_rows[r])
         table = [load_table(0, "slot_c")]
+        nc.sync.dma_start(vec_rows[BIAS_ROW : BIAS_ROW + N // P, 0:P], bg.rearrange("(i p) -> i p", p=P))
         nc.sync.dma_start(vec_rows[0:PASSES, :], gain.rearrange("(b c) -> b c", b=PASSES))
         load_weight_planes(wg_scales, 0)
         table.append(load_table(1, "slot_b"))

@@ -284,7 +284,7 @@ def tile_list_gated_edge_messages_kernel(
 
         round_w1(nc.vector.tensor_copy, 0, 0, 0, P)
         quantize_w1(0, 0)
-        for n in range(6):
+        for n in range(4):
             first_layer_pass(0, n, 0)
         for m0 in range(0, P, P // 2):
             round_w1(nc.vector.tensor_copy, 0, 1, m0, m0 + P // 2)
@@ -305,8 +305,8 @@ def tile_list_gated_edge_messages_kernel(
         gain_part(gain_on_vector, 0, 0, 0, FIRST_SHARE, CHUNK)
         first_layer(0, 2, [1])
         first_layer(0, 3, [1])
-        first_layer(0, 4, [1])
-        first_layer(0, 5, [1])
+        first_layer(0, 4, [0, 1])
+        first_layer(0, 5, [0, 1])
         gain_on_vector(0, tanh_of[0, 1][:], CHUNK, CHUNK)
         round_w1(nc.scalar.copy, 1, 1, LAST_PIECE_ON_VECTOR, P)
         round_w1(nc.vector.tensor_copy, 1, 1, 0, LAST_PIECE_ON_VECTOR)

@@ -27,17 +27,14 @@ CHUNK = 256
 PLANE_ROWS = 4
 PASS1_DROP = 16
 BIAS_ROW = 4
-RING = 4
-STORES = N // P * S // BANK
-LAST_PIECE_ON_VECTOR = 64
 GAIN_BANK = 7
-FIRST_BANKS = [[0, 1, 2, 3, 4, 5, 4, 5], [6, 2, 3, 6, 2, 3, 6, 2]]
-GATE_BANKS = [0, 1, 2, 3, 4, 5, 6, 4]
-SECOND_BANKS = [(0, 1), (4, 5), (0, 1), (4, 5)]
-SHARES = [128,64,160,128,80]
-FIRST_SHARE = 128
-LONGEST_SHARE = max(SHARES)
-H_ORDER = [(0, 0), (0, 1), (0, 2), (1, 0), (1, 1), (0, 3), (1, 2), (1, 3)]
+FIRST_BANKS = [[1, 2, 3, 4, 5, 6, 0, 1], [2, 3, 4, 5, 6, 2, 3, 4]]
+GATE_BANKS = [0, 1, 2, 3, 4, 5, 6, 0]
+CHUNK_BANKS = [(0, 1), (5, 6), (2, 3), (4, 0)]
+ROUND_ON_SCALAR = 40
+SHARES = [320, 104, 120, 80]
+RUNS = [SHARES[0], max(SHARES[1:])]
+TH_LEAD = 5 * BANK - ROUND_ON_SCALAR * PACK
 OVERLAP = 8
 
 
@@ -47,7 +44,6 @@ def tile_list_gated_edge_messages_kernel(
     nc = tc.nc
     with ExitStack() as ctx:
         keep = ctx.enter_context(tc.tile_pool(name="keep", bufs=1))
-        ring = ctx.enter_context(tc.tile_pool(name="ring", bufs=RING))
         slots = ctx.enter_context(tc.tile_pool(name="slots", bufs=1))
         psum = ctx.enter_context(tc.psum_pool(name="psum", bufs=1))
 
@@ -56,14 +52,13 @@ def tile_list_gated_edge_messages_kernel(
 
         raw = {}
 
-        def load_w1(b, slot, pieces):
-            staged = slots.tile([P, PASSES * PACK * PASS], F32, name=slot, align_bytes=64)
+        def load_w1(b, staged, starts, cuts):
             for a in range(PASSES):
-                raw[b, a] = staged[:, a * PACK * PASS : (a + 1) * PACK * PASS].rearrange("p (j c) -> p j c", j=PACK)
+                raw[b, a] = staged[:, starts[a] : starts[a] + PACK * PASS].rearrange("p (j c) -> p j c", j=PACK)
                 rows = w1[a * PASS : (a + 1) * PASS, b * PASS : (b + 1) * PASS].rearrange("(p j) c -> p j c", j=PACK)
-                width = PASS // pieces[a]
-                for c0 in range(0, PASS, width):
-                    nc.sync.dma_start(raw[b, a][:, :, c0 : c0 + width], rows[:, :, c0 : c0 + width])
+                edges = [0] + cuts[a] + [PASS]
+                for c0, c1 in zip(edges, edges[1:]):
+                    nc.sync.dma_start(raw[b, a][:, :, c0:c1], rows[:, :, c0:c1])
 
         def load_table(a, slot):
             words = slots.tile([P, T], I32, name=slot, align_bytes=64)
@@ -109,32 +104,34 @@ def tile_list_gated_edge_messages_kernel(
             nc.tensor.transpose(gains_turned[:, t, :], vec_rows[:, t:PASS:PACK], identity[:])
         nc.scalar.copy(bias[:], bias_turned[:, BIAS_ROW : BIAS_ROW + N // P])
 
-        gain_runs = keep.tile([P, PASSES, LONGEST_SHARE * PACK], F32, name="gain_runs", align_bytes=64)
+        gain_runs = []
         for b in range(PASSES):
+            run = keep.tile([P, RUNS[b] * PACK], F32, name=f"gain_run{b}", align_bytes=64)
             nc.scalar.copy(
-                gain_runs[:, b, :].rearrange("p (j t) -> p j t", t=PACK),
-                gains_turned[:, :, b].unsqueeze(1).to_broadcast([P, LONGEST_SHARE, PACK]),
+                run[:].rearrange("p (j t) -> p j t", t=PACK),
+                gains_turned[:, :, b].unsqueeze(1).to_broadcast([P, RUNS[b], PACK]),
             )
+            gain_runs.append(run)
 
         w1_words = keep.tile([P, PASSES, H], U32, name="w1_words", align_bytes=64)
         w1_scales = keep.tile([P, PASSES, H], U8, name="w1_scales", align_bytes=64)
-        grouped = {}
+        early = keep.tile([P, PASSES * PACK * PASS], BF16, name="early", align_bytes=64)
+        rounded = keep.tile([P, (2 * S + HALF) * PACK], BF16, name="rounded", align_bytes=64)
+
+        def grouped(b, a):
+            start = a * PASS if b == 0 else a * S
+            return (early, rounded)[b][:, start * PACK : (start + PASS) * PACK]
 
         def round_w1(copy, b, a, m0, m1):
-            if (b, a) not in grouped:
-                tag = "second_tanh" if (b, a) == (1, 1) else f"grouped{b}{a}"
-                grouped[b, a] = keep.tile([P, PACK, P, PACK], BF16, name=tag, align_bytes=64)
             copy(
-                grouped[b, a][:, :, m0:m1, :].rearrange("p t m j -> p m j t"),
+                grouped(b, a).rearrange("p (t m j) -> p m j t", t=PACK, j=PACK)[:, m0:m1],
                 raw[b, a][:, :, PACK * m0 : PACK * m1].rearrange("p j (m t) -> p m j t", t=PACK),
             )
 
         def quantize_w1(b, a):
             cols = slice(b * PASS, (b + 1) * PASS)
             nc.vector.quantize_mx(
-                out=w1_words[:, a, cols].bitcast(E4M3X4),
-                scales=w1_scales[:, a, cols],
-                in_=grouped[b, a][:].rearrange("p t m j -> p (t m j)"),
+                out=w1_words[:, a, cols].bitcast(E4M3X4), scales=w1_scales[:, a, cols], in_=grouped(b, a)
             )
 
         v_words = keep.tile([P, PASSES, S], U32, name="v_words", align_bytes=64)
@@ -142,26 +139,28 @@ def tile_list_gated_edge_messages_kernel(
         nc.vector.tensor_copy(v_scales[:], tab_planes[:].bitcast(U8).indirect(offsets[:]))
         for r in range(PLANE_ROWS):
             nc.sync.dma_start(v_scales_lifted[r:P:32, :], v_scales[PASS1_DROP + r : P : 32, :].bitcast(I32))
-        load_w1(0, "slot_a", [1, 2])
+        staged = slots.tile([P, PASSES * PACK * PASS], F32, name="slot_a", align_bytes=64)
+        load_w1(0, staged, [0, PACK * PASS], [[], [PASS // 2]])
         nc.vector.tensor_copy(v_words[:, 0, :], table[0][:].bitcast(U32).indirect(offsets[:]))
         for half in range(2):
             nc.vector.tensor_copy(
                 v_words[:, 1, half * HALF : (half + 1) * HALF],
                 table[1][:].bitcast(U32).indirect(offsets[:, half * HALF // 16 : (half + 1) * HALF // 16]),
             )
-        load_w1(1, "slot_c", [2, 1])
+        late = slots.tile([P, TH_LEAD + PASSES * PACK * PASS], F32, name="slot_c", align_bytes=64)
+        load_w1(1, late, [TH_LEAD + PACK * PASS, TH_LEAD], [[PASS // 2], []])
         v_planes = [v_scales[:], v_scales_lifted[:].bitcast(U8)]
 
         gate = [keep.tile([P, N // P, HALF], F32, name=f"gate{half}", align_bytes=64) for half in range(2)]
         gate_acc = {}
 
-        def gate_pass(half, i, a):
+        def gate_pass(o, a):
+            half, i = divmod(o, N // P)
             edges = slice(half * HALF, (half + 1) * HALF)
             if a == 0:
-                gate_acc[half, i] = psum.tile([P, HALF], F32, name=f"bank{GATE_BANKS[half * (N // P) + i]}")
-            acc = gate_acc[half, i]
+                gate_acc[o] = psum.tile([P, HALF], F32, name=f"bank{GATE_BANKS[o]}")
             nc.tensor.matmul_mx(
-                out=acc[:],
+                out=gate_acc[o][:],
                 lhsT=wg[:, a, P * i // 2 : P * (i + 1) // 2].bitcast(E2M1X4),
                 lhsT_scale=weight_planes[:, a, P * i : P * (i + 1)],
                 rhs=v_words[:, a, edges].bitcast(E4M3X4),
@@ -169,195 +168,198 @@ def tile_list_gated_edge_messages_kernel(
                 start=(a == 0),
                 stop=(a == PASSES - 1),
             )
-            if a == PASSES - 1:
-                nc.scalar.activation(gate[half][:, i, :], acc[:], ACT.Sigmoid, bias=bias[:, i : i + 1])
+
+        def sigmoid(o):
+            half, i = divmod(o, N // P)
+            nc.scalar.activation(gate[half][:, i, :], gate_acc[o][:], ACT.Sigmoid, bias=bias[:, i : i + 1])
 
         first_acc = {}
-        tanh_of = {}
-        h_tiles = {}
-        y_of = {}
-
-        def first_layer_pass(b, n, a):
-            if a == 0:
-                first_acc[b, n] = psum.tile([P, PACK, P], F32, name=f"bank{FIRST_BANKS[b][n]}")
-            edges = slice(n * P, (n + 1) * P)
-            for t in range(PACK):
-                cols = slice(b * PASS + t * P, b * PASS + (t + 1) * P)
-                nc.tensor.matmul_mx(
-                    out=first_acc[b, n][:, t, :],
-                    lhsT=w1_words[:, a, cols].bitcast(E4M3X4),
-                    lhsT_scale=w1_scales[:, a, cols],
-                    rhs=v_words[:, a, edges].bitcast(E4M3X4),
-                    rhs_scale=v_planes[a][:, edges],
-                    start=(a == 0 and t == 0),
-                    stop=(a == PASSES - 1 and t == PACK - 1),
-                )
-
-        def tanh(b, n):
-            if n % 2 == 0:
-                if (b, n) == (0, 0):
-                    both = keep.tile([P, CHUNK, PACK], F32, name="second_tanh", align_bytes=64)
-                elif (b, n) == (0, 6):
-                    both = slots.tile([P, CHUNK, PACK], F32, name="slot_c", align_bytes=64)
-                else:
-                    both = ring.tile([P, CHUNK, PACK], F32, name="th")
-                tanh_of[b, n // 2] = both
-            th = tanh_of[b, n // 2][:, n % 2 * P : (n % 2 + 1) * P, :]
-            nc.scalar.activation(th, first_acc[b, n][:].rearrange("p t j -> p j t"), ACT.Tanh)
+        th = [late, keep.tile([P, S * PACK], F32, name="th1", align_bytes=64)]
 
         def first_layer(b, n, passes):
+            edges = slice(n * P, (n + 1) * P)
             for a in passes:
-                first_layer_pass(b, n, a)
-            tanh(b, n)
+                if a == 0:
+                    first_acc[b, n] = psum.tile([P, PACK, P], F32, name=f"bank{FIRST_BANKS[b][n]}")
+                for t in range(PACK):
+                    cols = slice(b * PASS + t * P, b * PASS + (t + 1) * P)
+                    nc.tensor.matmul_mx(
+                        out=first_acc[b, n][:, t, :],
+                        lhsT=w1_words[:, a, cols].bitcast(E4M3X4),
+                        lhsT_scale=w1_scales[:, a, cols],
+                        rhs=v_words[:, a, edges].bitcast(E4M3X4),
+                        rhs_scale=v_planes[a][:, edges],
+                        start=(a == 0 and t == 0),
+                        stop=(a == PASSES - 1 and t == PACK - 1),
+                    )
 
-        rounded = []
+        def tanh(b, n):
+            values = th[b][:, n * BANK : (n + 1) * BANK].rearrange("p (j t) -> p j t", t=PACK)
+            nc.scalar.activation(values, first_acc[b, n][:].rearrange("p t j -> p j t"), ACT.Tanh)
 
-        def rounded_view(place, width):
-            tile, start = (rounded[0], place) if place < HALF else (rounded[1], place - HALF)
-            return tile[:, start * PACK : (start + width) * PACK]
+        second = S + HALF - OVERLAP - CHUNK
+        places = {
+            (0, 0): HALF,
+            (1, 0): second, (0, 1): second + CHUNK, (0, 2): second + 2 * CHUNK, (0, 3): second + 3 * CHUNK,
+            (1, 1): second, (1, 2): second, (1, 3): second,
+        }
 
-        def gain_on_vector(b, values, place, width):
-            factor = gains_turned[:, :, b].unsqueeze(1).to_broadcast([P, width, PACK])
-            nc.vector.tensor_tensor(rounded_view(place, width).rearrange("p (j t) -> p j t", t=PACK), values, factor, MULT)
+        def rounded_view(b, e0, e1):
+            start = places[b, e0 // CHUNK] + e0 % CHUNK
+            return rounded[:, start * PACK : (start + e1 - e0) * PACK]
 
-        def gain_on_gpsimd(b, values, place, width):
-            flat = values.rearrange("p j t -> p (j t)")
-            nc.gpsimd.tensor_tensor(rounded_view(place, width), flat, gain_runs[:, b, 0 : width * PACK], MULT)
+        def gain_on_vector(b, e0, e1):
+            factor = gains_turned[:, :, b].unsqueeze(1).to_broadcast([P, e1 - e0, PACK])
+            nc.vector.tensor_tensor(
+                rounded_view(b, e0, e1).rearrange("p (j t) -> p j t", t=PACK),
+                th[b][:, e0 * PACK : e1 * PACK].rearrange("p (j t) -> p j t", t=PACK),
+                factor,
+                MULT,
+            )
 
-        def h_views(b, chunk, width):
-            tile, half = divmod(H_ORDER.index((b, chunk)), 2)
-            if tile not in h_tiles:
-                words = keep.tile([P, HALF], U32, name=f"h_words{tile}", align_bytes=64)
-                scales = keep.tile([P, HALF], U8, name=f"h_scales{tile}", align_bytes=64)
-                h_tiles[tile] = (words, scales)
-            words, scales = h_tiles[tile]
-            cols = slice(half * CHUNK, half * CHUNK + width)
-            return words[:, cols].bitcast(E4M3X4), scales[:, cols]
+        def gain_on_gpsimd(b, e0, e1):
+            nc.gpsimd.tensor_tensor(
+                rounded_view(b, e0, e1), th[b][:, e0 * PACK : e1 * PACK], gain_runs[b][:, 0 : (e1 - e0) * PACK], MULT
+            )
 
-        def quantize_h(b, chunk, width, place):
-            words, scales = h_views(b, chunk, width)
-            nc.vector.quantize_mx(out=words, scales=scales, in_=rounded_view(place, width))
+        h_of = {}
 
-        low, high, top = HALF, HALF + CHUNK - OVERLAP, S - OVERLAP
+        def quantize_h(*chunks):
+            width = CHUNK * len(chunks)
+            b, c = chunks[0]
+            words = keep.tile([P, width], U32, name=f"h_words{b}_{c}", align_bytes=64)
+            scales = keep.tile([P, width], U8, name=f"h_scales{b}_{c}", align_bytes=64)
+            for i, chunk in enumerate(chunks):
+                h_of[chunk] = (words[:, i * CHUNK : (i + 1) * CHUNK], scales[:, i * CHUNK : (i + 1) * CHUNK])
+            values = rounded[:, places[b, c] * PACK : (places[b, c] + width) * PACK]
+            nc.vector.quantize_mx(out=words[:].bitcast(E4M3X4), scales=scales[:], in_=values)
 
-        def gain_part(apply, b, chunk, place, e0, e1):
-            apply(b, tanh_of[b, chunk][:, e0:e1, :], place + e0, e1 - e0)
-
-        pair = BANK // CHUNK
+        y_of = {}
+        out_view = out.rearrange("(i p) j -> p i j", p=P)
 
         def second_layer(chunk, b, banks=(0, 1)):
+            words, scales = h_of[b, chunk]
             for n in banks:
                 if b == 0:
-                    y_of[chunk, n] = psum.tile([P, pair, CHUNK], F32, name=f"bank{SECOND_BANKS[chunk][n]}")
-                for e in range(pair):
-                    cols = slice(P * (n * pair + e), P * (n * pair + e + 1))
-                    words, scales = h_views(b, chunk, CHUNK)
+                    y_of[chunk, n] = psum.tile([P, 2, CHUNK], F32, name=f"bank{CHUNK_BANKS[chunk][n]}")
+                for e in range(2):
+                    cols = slice(P * (2 * n + e), P * (2 * n + e + 1))
                     nc.tensor.matmul_mx(
                         out=y_of[chunk, n][:, e, :],
                         lhsT=w2[:, b, cols].bitcast(E4M3X4),
                         lhsT_scale=weight_planes[PLANE_ROWS:P, b, cols],
-                        rhs=words,
+                        rhs=words.bitcast(E4M3X4),
                         rhs_scale=scales,
                         start=(b == 0 and e == 0),
-                        stop=(b == PASSES - 1 and e == pair - 1),
+                        stop=(b == 1 and e == 1),
                     )
 
-        out_view = out.rearrange("(i p) j -> p i j", p=P)
-        last_chunk = S // CHUNK - 1
+        results = {}
 
-        def gate_and_store(chunk, n):
-            first = chunk * CHUNK
-            result = ring.tile([P, pair, CHUNK], F32, name="result", bufs=STORES)
-            factor = gate[first // HALF][:, n * pair : (n + 1) * pair, first % HALF : first % HALF + CHUNK]
-            step = 1 if (chunk, n) == (last_chunk, 1) else pair
-            for e in range(0, pair, step):
-                part = slice(e, e + step)
-                nc.vector.tensor_tensor(result[:, part], y_of[chunk, n][:, part], factor[:, part], MULT)
-                channels = slice(n * pair + e, n * pair + e + step)
-                nc.sync.dma_start(out_view[:, channels, first : first + CHUNK], result[:, part])
+        def product(chunk, n, e0=0, e1=2, on=None):
+            half, first = divmod(chunk * CHUNK, HALF)
+            if e0 == 0:
+                if on is None:
+                    results[chunk, n] = keep.tile([P, BANK], F32, name=f"result{chunk}_{n}")[:]
+                else:
+                    results[chunk, n] = th[1][:, on * CHUNK * PACK : on * CHUNK * PACK + BANK]
+            result = results[chunk, n].rearrange("p (e j) -> p e j", e=2)
+            factor = gate[half][:, 2 * n + e0 : 2 * n + e1, first : first + CHUNK]
+            nc.vector.tensor_tensor(result[:, e0:e1], y_of[chunk, n][:, e0:e1], factor, MULT)
 
-        outputs = [(half, i) for half in range(2) for i in range(N // P)]
-        for half, i in outputs[:GAIN_BANK]:
-            gate_pass(half, i, 0)
-        for half, i in outputs[:GAIN_BANK]:
-            gate_pass(half, i, 1)
+        def store(chunk, n, e0=0, e1=2):
+            result = results[chunk, n].rearrange("p (e j) -> p e j", e=2)
+            nc.sync.dma_start(out_view[:, 2 * n + e0 : 2 * n + e1, chunk * CHUNK : (chunk + 1) * CHUNK], result[:, e0:e1])
+
+        for o in range(GAIN_BANK):
+            gate_pass(o, 0)
+        for o in range(GAIN_BANK):
+            gate_pass(o, 1)
+        sigmoid(0)
+        gate_pass(7, 0)
+        gate_pass(7, 1)
+        for o in range(1, 8):
+            sigmoid(o)
 
         round_w1(nc.vector.tensor_copy, 0, 0, 0, P)
+        round_w1(nc.vector.tensor_copy, 0, 1, 0, P // 2)
         quantize_w1(0, 0)
         for n in range(4):
-            first_layer_pass(0, n, 0)
-        for m0 in range(0, P, P // 2):
-            round_w1(nc.vector.tensor_copy, 0, 1, m0, m0 + P // 2)
+            first_layer(0, n, [0])
+        round_w1(nc.vector.tensor_copy, 0, 1, P // 2, P)
         w2 = slots.tile([P, PASSES, N], I32, name="slot_a", align_bytes=64)
         nc.sync.dma_start(
             w2[:], w2_words.rearrange("a p n i -> a p (n i)").bitcast(I32).rearrange("a p n -> p a n")
         )
         load_weight_planes(w2_scales, PLANE_ROWS)
         quantize_w1(0, 1)
-
-        for m0 in range(0, P, P // 2):
-            round_w1(nc.vector.tensor_copy, 1, 0, m0, m0 + P // 2)
+        round_w1(nc.vector.tensor_copy, 1, 0, 0, P // 2)
+        for n in range(4):
+            first_layer(0, n, [1])
+            tanh(0, n)
+        round_w1(nc.vector.tensor_copy, 1, 0, P // 2, P)
+        gain_on_vector(0, 0, P)
         quantize_w1(1, 0)
-        first_layer(0, 0, [1])
-        first_layer(0, 1, [1])
-        rounded.append(keep.tile([P, HALF * PACK], BF16, name="grouped10", align_bytes=64))
-        gain_part(gain_on_gpsimd, 0, 0, 0, 0, FIRST_SHARE)
-        gain_part(gain_on_vector, 0, 0, 0, FIRST_SHARE, CHUNK)
-        first_layer(0, 2, [1])
-        first_layer(0, 3, [1])
-        first_layer(0, 4, [0, 1])
-        first_layer(0, 5, [0, 1])
-        gain_on_vector(0, tanh_of[0, 1][:], CHUNK, CHUNK)
-        round_w1(nc.scalar.copy, 1, 1, LAST_PIECE_ON_VECTOR, P)
-        round_w1(nc.vector.tensor_copy, 1, 1, 0, LAST_PIECE_ON_VECTOR)
-        first_layer(0, 6, [0, 1])
-        first_layer(0, 7, [0, 1])
-        for n in range(3):
-            first_layer_pass(1, n, 0)
-        quantize_h(0, 0, HALF, 0)
+        for n in range(4, 8):
+            first_layer(0, n, [0, 1])
+        gain_on_vector(0, P, CHUNK)
+        round_w1(nc.scalar.copy, 1, 1, 0, ROUND_ON_SCALAR)
+        round_w1(nc.vector.tensor_copy, 1, 1, ROUND_ON_SCALAR, P)
+        for n in range(4, 8):
+            tanh(0, n)
+        for n in range(5):
+            first_layer(1, n, [0])
+        quantize_h((0, 0))
         quantize_w1(1, 1)
-        rounded.append(keep.tile([P, (HALF + CHUNK) * PACK], BF16, name="second_tanh", align_bytes=64))
 
-        gain_part(gain_on_gpsimd, 0, 2, high, 0, SHARES[0])
-        gain_part(gain_on_vector, 0, 2, high, SHARES[0], CHUNK)
-        gain_part(gain_on_vector, 0, 3, top, 0, P)
-        for n in range(3):
+        gain_on_gpsimd(0, CHUNK, CHUNK + SHARES[0])
+        gain_on_vector(0, CHUNK + SHARES[0], 6 * P)
+        gain_on_vector(0, 6 * P, 7 * P)
+        gain_on_vector(0, 7 * P, S)
+        for n in range(5):
             first_layer(1, n, [1])
+            tanh(1, n)
         second_layer(0, 0)
-        quantize_h(0, 2, CHUNK, high)
-        first_layer(1, 3, [0, 1])
-        gain_part(gain_on_vector, 1, 0, low, 0, CHUNK - SHARES[1])
-        gain_part(gain_on_gpsimd, 1, 0, low, CHUNK - SHARES[1], CHUNK)
-        for a in range(PASSES):
-            gate_pass(*outputs[GAIN_BANK], a)
-        first_layer(1, 4, [0, 1])
-        quantize_h(1, 0, CHUNK, low)
+        gain_on_vector(1, 0, P)
+        gain_on_vector(1, P, CHUNK)
+        for n in range(5, 7):
+            first_layer(1, n, [0, 1])
+            tanh(1, n)
+        quantize_h((1, 0), (0, 1), (0, 2), (0, 3))
         second_layer(0, 1)
-        second_layer(1, 0)
-        first_layer(1, 5, [0, 1])
-
-        gain_part(gain_on_gpsimd, 1, 1, high, 0, SHARES[2])
-        gain_part(gain_on_vector, 0, 3, top, P, CHUNK)
-        gain_part(gain_on_vector, 1, 1, high, SHARES[2], CHUNK)
-        gate_and_store(0, 0)
-        gate_and_store(0, 1)
-        first_layer(1, 6, [0, 1])
-        quantize_h(1, 1, HALF, high)
-        second_layer(1, 1)
         first_layer(1, 7, [0, 1])
+        tanh(1, 7)
+        second_layer(1, 0)
+
+        gain_on_gpsimd(1, CHUNK, CHUNK + SHARES[1])
+        gain_on_vector(1, CHUNK + SHARES[1], HALF)
+        product(0, 0)
+        store(0, 0)
+        quantize_h((1, 1))
         second_layer(2, 0)
-        gain_part(gain_on_vector, 1, 2, low, 0, CHUNK - SHARES[3])
-        gain_part(gain_on_gpsimd, 1, 2, low, CHUNK - SHARES[3], CHUNK)
-        gate_and_store(1, 0)
-        gate_and_store(1, 1)
-        quantize_h(1, 2, CHUNK, low)
-        second_layer(2, 1)
+        second_layer(1, 1)
+        gain_on_gpsimd(1, HALF, HALF + SHARES[2])
+        product(0, 1, on=1)
+        store(0, 1)
+        gain_on_vector(1, HALF + SHARES[2], HALF + CHUNK)
+        product(1, 0)
+        store(1, 0)
+        quantize_h((1, 2))
         second_layer(3, 0)
-        gain_part(gain_on_gpsimd, 1, 3, high, 0, SHARES[4])
-        gain_part(gain_on_vector, 1, 3, high, SHARES[4], CHUNK)
-        gate_and_store(2, 0)
-        quantize_h(1, 3, CHUNK, high)
+        second_layer(2, 1)
+        gain_on_gpsimd(1, 3 * CHUNK, 3 * CHUNK + SHARES[3])
+        product(1, 1, 0, 1, on=2)
+        gain_on_vector(1, 3 * CHUNK + SHARES[3], S)
+        product(1, 1, 1, 2)
+        store(1, 1)
+        quantize_h((1, 3))
         second_layer(3, 1)
-        gate_and_store(2, 1)
-        gate_and_store(3, 0)
-        gate_and_store(3, 1)
+        product(2, 0, on=3)
+        store(2, 0)
+        product(2, 1)
+        store(2, 1)
+        product(3, 0)
+        store(3, 0)
+        for e in range(2):
+            product(3, 1, e, e + 1)
+            store(3, 1, e, e + 1)

@@ -32,9 +32,9 @@ FIRST_BANKS = [[1, 2, 3, 4, 5, 6, 0, 1], [2, 3, 4, 5, 6, 2, 3, 4]]
 GATE_BANKS = [0, 1, 2, 3, 4, 5, 6, 0]
 CHUNK_BANKS = [(0, 1), (5, 6), (2, 3), (4, 0)]
 ROUND_ON_SCALAR = 40
-SHARES = [320, 104, 120, 80]
+SHARES = [320, 88, 120, 120]
 RUNS = [SHARES[0], max(SHARES[1:])]
-TH_LEAD = 5 * BANK - ROUND_ON_SCALAR * PACK
+TH_LEAD = 6 * BANK - ROUND_ON_SCALAR * PACK
 OVERLAP = 8
 
 
@@ -65,37 +65,35 @@ def tile_list_gated_edge_messages_kernel(
             nc.sync.dma_start(words[:], tab_words[a].rearrange("p t i -> p (t i)").bitcast(I32))
             return words
 
-        def load_weight_planes(scales, drop):
+        def load_weight_planes(scales, drop, which=range(PLANE_ROWS)):
             rows = scales.bitcast(I32).rearrange("a (q r) n -> r q a n", r=PLANE_ROWS)
-            for r in range(PLANE_ROWS):
+            for r in which:
                 nc.sync.dma_start(weight_plane_words[drop + r : P : 32], rows[r])
 
         tab_planes = slots.tile([P, T // 4], I32, name="slot_a", align_bytes=64)
-        v_scales_lifted = keep.tile([P, S // 4], I32, name="v_scales_lifted", align_bytes=64)
         nc.vector.memset(tab_planes[:], 0)
         wg = keep.tile([P, PASSES, N // 2], I32, name="wg", align_bytes=64)
         weight_plane_words = keep.tile([P, PASSES, N // 4], I32, name="weight_plane_words", align_bytes=64)
         weight_planes = weight_plane_words[:].bitcast(U8)
-        nc.vector.memset(weight_plane_words[:], 0)
-        nc.vector.memset(v_scales_lifted[:], 0)
 
         bias = keep.tile([P, N // P], F32, name="bias")
-        vec_rows = keep.tile([P, PASS], F32, name="vec_rows")
-        identity = keep.tile([P, P], F32, name="identity")
+        vec_rows = slots.tile([P, PASS], F32, name="slot_b", align_bytes=64)
+        identity = slots.tile([P, P], F32, name="slot_d", align_bytes=64)
         nc.vector.memset(vec_rows[:], 0.0)
+        nc.vector.memset(weight_plane_words[:], 0)
         nc.vector.memset(identity[:], 0.0)
+        lifted = [keep.tile([P, S // 4], I32, name="lifted0", align_bytes=64)]
+        nc.vector.memset(lifted[0][:], 0)
         make_identity(nc, identity[:], nomemset=True)
 
         for a in range(PASSES):
             nc.sync.dma_start(wg[:, a, :], wg_words[a].bitcast(I32))
-        tab_rows = tab_scales.bitcast(I32).rearrange("a (q r) n -> r q a n", r=PLANE_ROWS)
-        for r in range(PLANE_ROWS):
-            nc.sync.dma_start(tab_planes[r:P:PASS1_DROP, :], tab_rows[r])
-        table = [load_table(0, "slot_c")]
+        nc.sync.dma_start(tab_planes[0:P:PLANE_ROWS, :], tab_scales.bitcast(I32).rearrange("a q n -> (a q) n"))
         nc.sync.dma_start(vec_rows[BIAS_ROW : BIAS_ROW + N // P, 0:P], bg.rearrange("(i p) -> i p", p=P))
         nc.sync.dma_start(vec_rows[0:PASSES, :], gain.rearrange("(b c) -> b c", b=PASSES))
-        load_weight_planes(wg_scales, 0)
-        table.append(load_table(1, "slot_b"))
+        load_weight_planes(wg_scales, 0, range(2))
+        table = [load_table(0, "slot_c")]
+        load_weight_planes(wg_scales, 0, range(2, PLANE_ROWS))
 
         bias_turned = psum.tile([P, P], F32, name="bank6")
         nc.tensor.transpose(bias_turned[:], vec_rows[:, 0:P], identity[:])
@@ -137,19 +135,28 @@ def tile_list_gated_edge_messages_kernel(
         v_words = keep.tile([P, PASSES, S], U32, name="v_words", align_bytes=64)
         v_scales = keep.tile([P, S], U8, name="v_scales", align_bytes=64)
         nc.vector.tensor_copy(v_scales[:], tab_planes[:].bitcast(U8).indirect(offsets[:]))
-        for r in range(PLANE_ROWS):
-            nc.sync.dma_start(v_scales_lifted[r:P:32, :], v_scales[PASS1_DROP + r : P : 32, :].bitcast(I32))
-        staged = slots.tile([P, PASSES * PACK * PASS], F32, name="slot_a", align_bytes=64)
-        load_w1(0, staged, [0, PACK * PASS], [[], [PASS // 2]])
+
+        def lift(a):
+            for r in range(PLANE_ROWS):
+                rows = v_scales[64 * a + PLANE_ROWS * r : 64 * (a + 1) : 16, :]
+                nc.sync.dma_start(lifted[a][r:P:32, :], rows.bitcast(I32))
+
+        lift(0)
+        table.append(load_table(1, "slot_b"))
+        lifted.append(slots.tile([P, S // 4], I32, name="slot_d", align_bytes=64))
+        nc.vector.memset(lifted[1][:], 0)
+        lift(1)
         nc.vector.tensor_copy(v_words[:, 0, :], table[0][:].bitcast(U32).indirect(offsets[:]))
+        staged = slots.tile([P, PASSES * PACK * PASS], F32, name="slot_c", align_bytes=64)
+        load_w1(0, staged, [0, PACK * PASS], [[], [PASS // 2]])
         for half in range(2):
             nc.vector.tensor_copy(
                 v_words[:, 1, half * HALF : (half + 1) * HALF],
                 table[1][:].bitcast(U32).indirect(offsets[:, half * HALF // 16 : (half + 1) * HALF // 16]),
             )
-        late = slots.tile([P, TH_LEAD + PASSES * PACK * PASS], F32, name="slot_c", align_bytes=64)
+        late = slots.tile([P, TH_LEAD + PASSES * PACK * PASS], F32, name="slot_b", align_bytes=64)
         load_w1(1, late, [TH_LEAD + PACK * PASS, TH_LEAD], [[PASS // 2], []])
-        v_planes = [v_scales[:], v_scales_lifted[:].bitcast(U8)]
+        v_planes = [lifted[a][:].bitcast(U8) for a in range(PASSES)]
 
         gate = [keep.tile([P, N // P, HALF], F32, name=f"gate{half}", align_bytes=64) for half in range(2)]
         gate_acc = {}
@@ -197,11 +204,12 @@ def tile_list_gated_edge_messages_kernel(
             values = th[b][:, n * BANK : (n + 1) * BANK].rearrange("p (j t) -> p j t", t=PACK)
             nc.scalar.activation(values, first_acc[b, n][:].rearrange("p t j -> p j t"), ACT.Tanh)
 
-        second = S + HALF - OVERLAP - CHUNK
+        second = S + HALF - OVERLAP
+        third = second + 3 * CHUNK - OVERLAP
         places = {
             (0, 0): HALF,
-            (1, 0): second, (0, 1): second + CHUNK, (0, 2): second + 2 * CHUNK, (0, 3): second + 3 * CHUNK,
-            (1, 1): second, (1, 2): second, (1, 3): second,
+            (1, 0): second - CHUNK, (0, 1): second, (0, 2): second + CHUNK, (0, 3): second + HALF,
+            (1, 1): third, (1, 2): third, (1, 3): third,
         }
 
         def rounded_view(b, e0, e1):
@@ -287,7 +295,7 @@ def tile_list_gated_edge_messages_kernel(
         for n in range(4):
             first_layer(0, n, [0])
         round_w1(nc.vector.tensor_copy, 0, 1, P // 2, P)
-        w2 = slots.tile([P, PASSES, N], I32, name="slot_a", align_bytes=64)
+        w2 = slots.tile([P, PASSES, N], I32, name="slot_c", align_bytes=64)
         nc.sync.dma_start(
             w2[:], w2_words.rearrange("a p n i -> a p (n i)").bitcast(I32).rearrange("a p n -> p a n")
         )
@@ -302,10 +310,11 @@ def tile_list_gated_edge_messages_kernel(
         quantize_w1(1, 0)
         for n in range(4, 8):
             first_layer(0, n, [0, 1])
+        tanh(0, 4)
         gain_on_vector(0, P, CHUNK)
         round_w1(nc.scalar.copy, 1, 1, 0, ROUND_ON_SCALAR)
         round_w1(nc.vector.tensor_copy, 1, 1, ROUND_ON_SCALAR, P)
-        for n in range(4, 8):
+        for n in range(5, 8):
             tanh(0, n)
         for n in range(5):
             first_layer(1, n, [0])
@@ -325,7 +334,8 @@ def tile_list_gated_edge_messages_kernel(
         for n in range(5, 7):
             first_layer(1, n, [0, 1])
             tanh(1, n)
-        quantize_h((1, 0), (0, 1), (0, 2), (0, 3))
+        quantize_h((1, 0), (0, 1))
+        quantize_h((0, 2), (0, 3))
         second_layer(0, 1)
         first_layer(1, 7, [0, 1])
         tanh(1, 7)
@@ -336,8 +346,8 @@ def tile_list_gated_edge_messages_kernel(
         product(0, 0)
         store(0, 0)
         quantize_h((1, 1))
-        second_layer(2, 0)
         second_layer(1, 1)
+        second_layer(2, 0)
         gain_on_gpsimd(1, HALF, HALF + SHARES[2])
         product(0, 1, on=1)
         store(0, 1)
@@ -345,18 +355,17 @@ def tile_list_gated_edge_messages_kernel(
         product(1, 0)
         store(1, 0)
         quantize_h((1, 2))
-        second_layer(3, 0)
         second_layer(2, 1)
+        second_layer(3, 0)
         gain_on_gpsimd(1, 3 * CHUNK, 3 * CHUNK + SHARES[3])
-        product(1, 1, 0, 1, on=2)
-        gain_on_vector(1, 3 * CHUNK + SHARES[3], S)
-        product(1, 1, 1, 2)
+        product(1, 1, on=2)
         store(1, 1)
+        gain_on_vector(1, 3 * CHUNK + SHARES[3], S)
+        product(2, 0)
+        store(2, 0)
         quantize_h((1, 3))
         second_layer(3, 1)
-        product(2, 0, on=3)
-        store(2, 0)
-        product(2, 1)
+        product(2, 1, on=3)
         store(2, 1)
         product(3, 0)
         store(3, 0)

@@ -26,6 +26,7 @@ HALF = S // 2
 CHUNK = 256
 PLANE_ROWS = 4
 PASS1_DROP = 16
+ROWS_FROM = 96
 BIAS_ROW = 4
 GAIN_BANK = 7
 FIRST_BANKS = [[1, 2, 3, 4, 5, 6, 0, 1], [2, 3, 4, 5, 6, 2, 3, 4]]
@@ -71,7 +72,6 @@ def tile_list_gated_edge_messages_kernel(
                 nc.sync.dma_start(weight_plane_words[drop + r : P : 32], rows[r])
 
         tab_planes = slots.tile([P, T // 4], I32, name="slot_a", align_bytes=64)
-        nc.vector.memset(tab_planes[:], 0)
         wg = keep.tile([P, PASSES, N // 2], I32, name="wg", align_bytes=64)
         weight_plane_words = keep.tile([P, PASSES, N // 4], I32, name="weight_plane_words", align_bytes=64)
         weight_planes = weight_plane_words[:].bitcast(U8)
@@ -82,13 +82,13 @@ def tile_list_gated_edge_messages_kernel(
         nc.vector.memset(vec_rows[:], 0.0)
         nc.vector.memset(weight_plane_words[:], 0)
         nc.vector.memset(identity[:], 0.0)
+        nc.vector.memset(tab_planes[0:ROWS_FROM, :], 0)
         lifted = [keep.tile([P, S // 4], I32, name="lifted0", align_bytes=64)]
         nc.vector.memset(lifted[0][:], 0)
         make_identity(nc, identity[:], nomemset=True)
 
-        for a in range(PASSES):
-            nc.sync.dma_start(wg[:, a, :], wg_words[a].bitcast(I32))
-        nc.sync.dma_start(tab_planes[0:P:PLANE_ROWS, :], tab_scales.bitcast(I32).rearrange("a q n -> (a q) n"))
+        nc.sync.dma_start(tab_planes[ROWS_FROM:P, :], tab_scales.bitcast(I32).rearrange("a q n -> (a q) n"))
+        nc.sync.dma_start(wg[:], wg_words.bitcast(I32).rearrange("a p n -> p a n"))
         nc.sync.dma_start(vec_rows[BIAS_ROW : BIAS_ROW + N // P, 0:P], bg.rearrange("(i p) -> i p", p=P))
         nc.sync.dma_start(vec_rows[0:PASSES, :], gain.rearrange("(b c) -> b c", b=PASSES))
         load_weight_planes(wg_scales, 0, range(2))
@@ -138,7 +138,7 @@ def tile_list_gated_edge_messages_kernel(
 
         def lift(a):
             for r in range(PLANE_ROWS):
-                rows = v_scales[64 * a + PLANE_ROWS * r : 64 * (a + 1) : 16, :]
+                rows = v_scales[ROWS_FROM + 16 * a + r : ROWS_FROM + 16 * (a + 1) : PLANE_ROWS, :]
                 nc.sync.dma_start(lifted[a][r:P:32, :], rows.bitcast(I32))
 
         lift(0)

@@ -31,9 +31,10 @@ BIAS_ROW = 4
 GAIN_BANK = 7
 FIRST_BANKS = [[1, 2, 3, 4, 5, 6, 0, 1], [2, 3, 4, 5, 6, 2, 3, 4]]
 GATE_BANKS = [0, 1, 2, 3, 4, 5, 6, 0]
-CHUNK_BANKS = [(0, 1), (5, 6), (2, 3), (4, 0)]
+CHUNK_BANKS = [(0, 1), (5, 6), (2, 3)]
+LAST_BANKS = [4, 0, 1, 5]
 ROUND_ON_SCALAR = 40
-SHARES = [320, 88, 120, 120]
+SHARES = [320, 96, 136, 136]
 RUNS = [SHARES[0], max(SHARES[1:])]
 TH_LEAD = 6 * BANK - ROUND_ON_SCALAR * PACK
 OVERLAP = 8
@@ -158,7 +159,7 @@ def tile_list_gated_edge_messages_kernel(
         load_w1(1, late, [TH_LEAD + PACK * PASS, TH_LEAD], [[PASS // 2], []])
         v_planes = [lifted[a][:].bitcast(U8) for a in range(PASSES)]
 
-        gate = [keep.tile([P, N // P, HALF], F32, name=f"gate{half}", align_bytes=64) for half in range(2)]
+        gate = [keep.tile([P, 2, 2, BANK], F32, name=f"gate{half}", align_bytes=64) for half in range(2)]
         gate_acc = {}
 
         def gate_pass(o, a):
@@ -178,7 +179,13 @@ def tile_list_gated_edge_messages_kernel(
 
         def sigmoid(o):
             half, i = divmod(o, N // P)
-            nc.scalar.activation(gate[half][:, i, :], gate_acc[o][:], ACT.Sigmoid, bias=bias[:, i : i + 1])
+            n, e = divmod(i, 2)
+            nc.scalar.activation(
+                gate[half][:, :, n, e * CHUNK : (e + 1) * CHUNK],
+                gate_acc[o][:].rearrange("p (c j) -> p c j", c=2),
+                ACT.Sigmoid,
+                bias=bias[:, i : i + 1],
+            )
 
         first_acc = {}
         th = [late, keep.tile([P, S * PACK], F32, name="th1", align_bytes=64)]
@@ -205,16 +212,18 @@ def tile_list_gated_edge_messages_kernel(
             nc.scalar.activation(values, first_acc[b, n][:].rearrange("p t j -> p j t"), ACT.Tanh)
 
         second = S + HALF - OVERLAP
-        third = second + 3 * CHUNK - OVERLAP
         places = {
             (0, 0): HALF,
             (1, 0): second - CHUNK, (0, 1): second, (0, 2): second + CHUNK, (0, 3): second + HALF,
-            (1, 1): third, (1, 2): third, (1, 3): third,
+            (1, 1): second - CHUNK,
         }
 
         def rounded_view(b, e0, e1):
-            start = places[b, e0 // CHUNK] + e0 % CHUNK
-            return rounded[:, start * PACK : (start + e1 - e0) * PACK]
+            chunk, first = divmod(e0, CHUNK)
+            if (b, chunk) in places:
+                start = places[b, chunk] + first
+                return rounded[:, start * PACK : (start + e1 - e0) * PACK]
+            return gate[0][:, chunk - 2, 0, :].bitcast(BF16)[:, first * PACK : (first + e1 - e0) * PACK]
 
         def gain_on_vector(b, e0, e1):
             factor = gains_turned[:, :, b].unsqueeze(1).to_broadcast([P, e1 - e0, PACK])
@@ -239,45 +248,53 @@ def tile_list_gated_edge_messages_kernel(
             scales = keep.tile([P, width], U8, name=f"h_scales{b}_{c}", align_bytes=64)
             for i, chunk in enumerate(chunks):
                 h_of[chunk] = (words[:, i * CHUNK : (i + 1) * CHUNK], scales[:, i * CHUNK : (i + 1) * CHUNK])
-            values = rounded[:, places[b, c] * PACK : (places[b, c] + width) * PACK]
+            values = rounded_view(b, c * CHUNK, c * CHUNK + width)
             nc.vector.quantize_mx(out=words[:].bitcast(E4M3X4), scales=scales[:], in_=values)
 
         y_of = {}
         out_view = out.rearrange("(i p) j -> p i j", p=P)
 
-        def second_layer(chunk, b, banks=(0, 1)):
+        def second_layer(chunk, b):
             words, scales = h_of[b, chunk]
-            for n in banks:
-                if b == 0:
-                    y_of[chunk, n] = psum.tile([P, 2, CHUNK], F32, name=f"bank{CHUNK_BANKS[chunk][n]}")
+            last = chunk == 3
+            for n in range(2):
+                if b == 0 and not last:
+                    acc = psum.tile([P, 2, CHUNK], F32, name=f"bank{CHUNK_BANKS[chunk][n]}")
+                    y_of[chunk, n] = acc[:].rearrange("p e j -> p (e j)")
+                    for e in range(2):
+                        y_of[chunk, n, e] = acc[:, e, :]
                 for e in range(2):
+                    if b == 0 and last:
+                        y_of[chunk, n, e] = psum.tile([P, CHUNK], F32, name=f"bank{LAST_BANKS[2 * n + e]}")[:]
                     cols = slice(P * (2 * n + e), P * (2 * n + e + 1))
                     nc.tensor.matmul_mx(
-                        out=y_of[chunk, n][:, e, :],
+                        out=y_of[chunk, n, e],
                         lhsT=w2[:, b, cols].bitcast(E4M3X4),
                         lhsT_scale=weight_planes[PLANE_ROWS:P, b, cols],
                         rhs=words.bitcast(E4M3X4),
                         rhs_scale=scales,
-                        start=(b == 0 and e == 0),
-                        stop=(b == 1 and e == 1),
+                        start=(b == 0 and (e == 0 or last)),
+                        stop=(b == 1 and (e == 1 or last)),
                     )
 
         results = {}
 
-        def product(chunk, n, e0=0, e1=2, on=None):
-            half, first = divmod(chunk * CHUNK, HALF)
-            if e0 == 0:
+        def product(chunk, n, c0=0, c1=BANK, on=None):
+            if c0 == 0:
                 if on is None:
                     results[chunk, n] = keep.tile([P, BANK], F32, name=f"result{chunk}_{n}")[:]
                 else:
                     results[chunk, n] = th[1][:, on * CHUNK * PACK : on * CHUNK * PACK + BANK]
-            result = results[chunk, n].rearrange("p (e j) -> p e j", e=2)
-            factor = gate[half][:, 2 * n + e0 : 2 * n + e1, first : first + CHUNK]
-            nc.vector.tensor_tensor(result[:, e0:e1], y_of[chunk, n][:, e0:e1], factor, MULT)
+            sums = y_of[chunk, n] if c1 - c0 == BANK else y_of[chunk, n, c0 // CHUNK]
+            factor = gate[chunk // 2][:, chunk % 2, n, c0:c1]
+            nc.vector.tensor_tensor(results[chunk, n][:, c0:c1], sums, factor, MULT)
 
-        def store(chunk, n, e0=0, e1=2):
-            result = results[chunk, n].rearrange("p (e j) -> p e j", e=2)
-            nc.sync.dma_start(out_view[:, 2 * n + e0 : 2 * n + e1, chunk * CHUNK : (chunk + 1) * CHUNK], result[:, e0:e1])
+        def store(chunk, n, c0=0, c1=BANK):
+            e0, j0 = divmod(c0, CHUNK)
+            rows, width = max((c1 - c0) // CHUNK, 1), min(c1 - c0, CHUNK)
+            first = chunk * CHUNK + j0
+            result = results[chunk, n][:, c0:c1].rearrange("p (e j) -> p e j", e=rows)
+            nc.sync.dma_start(out_view[:, 2 * n + e0 : 2 * n + e0 + rows, first : first + width], result)
 
         for o in range(GAIN_BANK):
             gate_pass(o, 0)
@@ -367,8 +384,7 @@ def tile_list_gated_edge_messages_kernel(
         second_layer(3, 1)
         product(2, 1, on=3)
         store(2, 1)
-        product(3, 0)
-        store(3, 0)
-        for e in range(2):
-            product(3, 1, e, e + 1)
-            store(3, 1, e, e + 1)
+        for n in range(2):
+            for c0 in range(0, BANK, CHUNK):
+                product(3, n, c0, c0 + CHUNK)
+                store(3, n, c0, c0 + CHUNK)

@@ -29,10 +29,10 @@ PASS1_DROP = 16
 ROWS_FROM = 96
 BIAS_ROW = 4
 GAIN_BANK = 7
-FIRST_BANKS = [[1, 2, 3, 4, 5, 6, 0, 1], [2, 3, 4, 5, 6, 2, 3, 4]]
-GATE_BANKS = [0, 1, 2, 3, 4, 5, 6, 0]
-CHUNK_BANKS = [(0, 1), (5, 6), (2, 3)]
-LAST_BANKS = [4, 0, 1, 5]
+FIRST_BANKS = [[1, 2, 0, 4, 5, 6, 3, 1], [2, 0, 4, 5, 6, 2, 0, 4]]
+GATE_BANKS = [0, 1, 2, 3, 4, 5, 6, 3]
+CHUNK_BANKS = [(3, 1), (5, 6), (2, 0)]
+LAST_BANKS = [4, 3, 1, 5]
 ROUND_ON_SCALAR = 40
 SHARES = [320, 96, 136, 136]
 RUNS = [SHARES[0], max(SHARES[1:])]
@@ -300,10 +300,11 @@ def tile_list_gated_edge_messages_kernel(
             gate_pass(o, 0)
         for o in range(GAIN_BANK):
             gate_pass(o, 1)
-        sigmoid(0)
+        for o in range(4):
+            sigmoid(o)
         gate_pass(7, 0)
         gate_pass(7, 1)
-        for o in range(1, 8):
+        for o in range(4, 8):
             sigmoid(o)
 
         round_w1(nc.vector.tensor_copy, 0, 0, 0, P)

@@ -34,7 +34,7 @@ GATE_BANKS = [0, 1, 2, 3, 4, 5, 6, 3]
 CHUNK_BANKS = [(3, 1), (5, 6), (2, 0)]
 LAST_BANKS = [4, 3, 1, 5]
 ROUND_ON_SCALAR = 40
-SHARES = [320, 96, 136, 136]
+SHARES = [272, 80, 112, 112]
 RUNS = [SHARES[0], max(SHARES[1:])]
 TH_LEAD = 6 * BANK - ROUND_ON_SCALAR * PACK
 OVERLAP = 8

@@ -34,7 +34,7 @@ GATE_BANKS = [0, 1, 2, 3, 4, 5, 6, 3]
 CHUNK_BANKS = [(3, 1), (5, 6), (2, 0)]
 LAST_BANKS = [4, 3, 1, 5]
 ROUND_ON_SCALAR = 40
-SHARES = [272, 80, 112, 112]
+SHARES = [272, 96, 120, 120]
 RUNS = [SHARES[0], max(SHARES[1:])]
 TH_LEAD = 6 * BANK - ROUND_ON_SCALAR * PACK
 OVERLAP = 8
@@ -215,7 +215,7 @@ def tile_list_gated_edge_messages_kernel(
         places = {
             (0, 0): HALF,
             (1, 0): second - CHUNK, (0, 1): second, (0, 2): second + CHUNK, (0, 3): second + HALF,
-            (1, 1): second - CHUNK,
+            (1, 1): second + CHUNK,
         }
 
         def rounded_view(b, e0, e1):
@@ -352,8 +352,8 @@ def tile_list_gated_edge_messages_kernel(
         for n in range(5, 7):
             first_layer(1, n, [0, 1])
             tanh(1, n)
-        quantize_h((1, 0), (0, 1))
         quantize_h((0, 2), (0, 3))
+        quantize_h((1, 0), (0, 1))
         second_layer(0, 1)
         first_layer(1, 7, [0, 1])
         tanh(1, 7)

@@ -34,7 +34,7 @@ GATE_BANKS = [0, 1, 2, 3, 4, 5, 6, 3]
 CHUNK_BANKS = [(3, 1), (5, 6), (2, 0)]
 LAST_BANKS = [4, 3, 1, 5]
 ROUND_ON_SCALAR = 40
-SHARES = [272, 96, 120, 120]
+SHARES = [256, 72, 112, 112]
 RUNS = [SHARES[0], max(SHARES[1:])]
 TH_LEAD = 6 * BANK - ROUND_ON_SCALAR * PACK
 OVERLAP = 8

@@ -34,7 +34,8 @@ GATE_BANKS = [0, 1, 2, 3, 4, 5, 6, 3]
 CHUNK_BANKS = [(3, 1), (5, 6), (2, 0)]
 LAST_BANKS = [4, 3, 1, 5]
 ROUND_ON_SCALAR = 40
-SHARES = [256, 72, 112, 112]
+SHARES = [256, 72, 112, 80]
+ON_SCALAR = 6
 RUNS = [SHARES[0], max(SHARES[1:])]
 TH_LEAD = 6 * BANK - ROUND_ON_SCALAR * PACK
 OVERLAP = 8
@@ -47,6 +48,7 @@ def tile_list_gated_edge_messages_kernel(
     with ExitStack() as ctx:
         keep = ctx.enter_context(tc.tile_pool(name="keep", bufs=1))
         slots = ctx.enter_context(tc.tile_pool(name="slots", bufs=1))
+        top = ctx.enter_context(tc.tile_pool(name="top", bufs=1))
         psum = ctx.enter_context(tc.psum_pool(name="psum", bufs=1))
 
         offsets = keep.tile([P, S // 16], U16, name="offsets")
@@ -208,8 +210,27 @@ def tile_list_gated_edge_messages_kernel(
                     )
 
         def tanh(b, n):
-            values = th[b][:, n * BANK : (n + 1) * BANK].rearrange("p (j t) -> p j t", t=PACK)
-            nc.scalar.activation(values, first_acc[b, n][:].rearrange("p t j -> p j t"), ACT.Tanh)
+            values = th[b][:, n * BANK : (n + 1) * BANK]
+            if (b, n) == (1, ON_SCALAR):
+                nc.scalar.activation(values, first_acc[b, n][:].rearrange("p t j -> p (t j)"), ACT.Tanh)
+            else:
+                nc.scalar.activation(
+                    values.rearrange("p (j t) -> p j t", t=PACK), first_acc[b, n][:].rearrange("p t j -> p j t"), ACT.Tanh
+                )
+
+        scaled = {}
+
+        def gain_on_scalar(n):
+            scaled[n] = top.tile([P, PACK, P], BF16, name=f"scaled{n}", align_bytes=64)
+            for t in range(PACK):
+                values = th[1][:, n * BANK + t * P : n * BANK + (t + 1) * P]
+                nc.scalar.activation(scaled[n][:, t, :], values, ACT.Copy, scale=gain_runs[1][:, t : t + 1])
+
+        def weave_on_scalar(n):
+            nc.scalar.copy(
+                rounded_view(1, n * P, (n + 1) * P).rearrange("p (j t) -> p j t", t=PACK),
+                scaled[n][:].rearrange("p t j -> p j t"),
+            )
 
         second = S + HALF - OVERLAP
         places = {
@@ -223,7 +244,9 @@ def tile_list_gated_edge_messages_kernel(
             if (b, chunk) in places:
                 start = places[b, chunk] + first
                 return rounded[:, start * PACK : (start + e1 - e0) * PACK]
-            return gate[0][:, chunk - 2, 0, :].bitcast(BF16)[:, first * PACK : (first + e1 - e0) * PACK]
+            start = (chunk - 2) * (BANK + CHUNK)
+            place = gate[0][:].rearrange("p c n j -> p (c n j)")[:, start : start + BANK]
+            return place.bitcast(BF16)[:, first * PACK : (first + e1 - e0) * PACK]
 
         def gain_on_vector(b, e0, e1):
             factor = gains_turned[:, :, b].unsqueeze(1).to_broadcast([P, e1 - e0, PACK])
@@ -284,7 +307,7 @@ def tile_list_gated_edge_messages_kernel(
                 if on is None:
                     results[chunk, n] = keep.tile([P, BANK], F32, name=f"result{chunk}_{n}")[:]
                 else:
-                    results[chunk, n] = th[1][:, on * CHUNK * PACK : on * CHUNK * PACK + BANK]
+                    results[chunk, n] = th[1][:, on * BANK : (on + 1) * BANK]
             sums = y_of[chunk, n] if c1 - c0 == BANK else y_of[chunk, n, c0 // CHUNK]
             factor = gate[chunk // 2][:, chunk % 2, n, c0:c1]
             nc.vector.tensor_tensor(results[chunk, n][:, c0:c1], sums, factor, MULT)
@@ -357,6 +380,7 @@ def tile_list_gated_edge_messages_kernel(
         second_layer(0, 1)
         first_layer(1, 7, [0, 1])
         tanh(1, 7)
+        gain_on_scalar(ON_SCALAR)
         second_layer(1, 0)
 
         gain_on_gpsimd(1, CHUNK, CHUNK + SHARES[1])
@@ -367,23 +391,24 @@ def tile_list_gated_edge_messages_kernel(
         second_layer(1, 1)
         second_layer(2, 0)
         gain_on_gpsimd(1, HALF, HALF + SHARES[2])
-        product(0, 1, on=1)
+        product(0, 1, on=2)
         store(0, 1)
+        weave_on_scalar(ON_SCALAR)
         gain_on_vector(1, HALF + SHARES[2], HALF + CHUNK)
         product(1, 0)
         store(1, 0)
         quantize_h((1, 2))
         second_layer(2, 1)
         second_layer(3, 0)
-        gain_on_gpsimd(1, 3 * CHUNK, 3 * CHUNK + SHARES[3])
-        product(1, 1, on=2)
+        gain_on_gpsimd(1, 7 * P, 7 * P + SHARES[3])
+        product(1, 1, on=4)
         store(1, 1)
-        gain_on_vector(1, 3 * CHUNK + SHARES[3], S)
+        gain_on_vector(1, 7 * P + SHARES[3], S)
         product(2, 0)
         store(2, 0)
         quantize_h((1, 3))
         second_layer(3, 1)
-        product(2, 1, on=3)
+        product(2, 1, on=7)
         store(2, 1)
         for n in range(2):
             for c0 in range(0, BANK, CHUNK):

from contextlib import ExitStack

import concourse.mybir as mybir
from concourse.masks import make_identity

K, H, N, T, S = 1024, 1024, 512, 4096, 1024
FLOPS = 2 * S * (K * H + K * N + H * N)

F32 = mybir.dt.float32
BF16 = mybir.dt.bfloat16
I32 = mybir.dt.int32
U32 = mybir.dt.uint32
U16 = mybir.dt.uint16
U8 = mybir.dt.uint8
E4M3X4 = mybir.dt.float8_e4m3fn_x4
E2M1X4 = mybir.dt.float4_e2m1fn_x4
ACT = mybir.ActivationFunctionType
MULT = mybir.AluOpType.mult

P = 128
PACK = 4
PASS = P * PACK
PASSES = 2
BANK = 512
HALF = S // 2
CHUNK = 256
PLANE_ROWS = 4
PASS1_DROP = 16
ROWS_FROM = 96
BIAS_ROW = 4
GAIN_BANK = 7
FIRST_BANKS = [[1, 2, 0, 4, 5, 6, 3, 1], [2, 0, 4, 5, 6, 2, 0, 4]]
GATE_BANKS = [0, 1, 2, 3, 4, 5, 6, 3]
CHUNK_BANKS = [(3, 1), (5, 6), (2, 0)]
LAST_BANKS = [4, 3, 1, 5]
ROUND_ON_SCALAR = 40
SHARES = [256, 72, 112, 80]
ON_SCALAR = 6
RUNS = [SHARES[0], max(SHARES[1:])]
TH_LEAD = 6 * BANK - ROUND_ON_SCALAR * PACK
OVERLAP = 8


def tile_list_gated_edge_messages_kernel(
    tc, tab_words, tab_scales, offs, w1, gain, wg_words, wg_scales, bg, w2_words, w2_scales, out
):
    nc = tc.nc
    with ExitStack() as ctx:
        keep = ctx.enter_context(tc.tile_pool(name="keep", bufs=1))
        slots = ctx.enter_context(tc.tile_pool(name="slots", bufs=1))
        top = ctx.enter_context(tc.tile_pool(name="top", bufs=1))
        psum = ctx.enter_context(tc.psum_pool(name="psum", bufs=1))

        offsets = keep.tile([P, S // 16], U16, name="offsets")
        nc.sync.dma_start(offsets[:], offs)

        raw = {}

        def load_w1(b, staged, starts, cuts):
            for a in range(PASSES):
                raw[b, a] = staged[:, starts[a] : starts[a] + PACK * PASS].rearrange("p (j c) -> p j c", j=PACK)
                rows = w1[a * PASS : (a + 1) * PASS, b * PASS : (b + 1) * PASS].rearrange("(p j) c -> p j c", j=PACK)
                edges = [0] + cuts[a] + [PASS]
                for c0, c1 in zip(edges, edges[1:]):
                    nc.sync.dma_start(raw[b, a][:, :, c0:c1], rows[:, :, c0:c1])

        def load_table(a, slot):
            words = slots.tile([P, T], I32, name=slot, align_bytes=64)
            nc.sync.dma_start(words[:], tab_words[a].rearrange("p t i -> p (t i)").bitcast(I32))
            return words

        def load_weight_planes(scales, drop, which=range(PLANE_ROWS)):
            rows = scales.bitcast(I32).rearrange("a (q r) n -> r q a n", r=PLANE_ROWS)
            for r in which:
                nc.sync.dma_start(weight_plane_words[drop + r : P : 32], rows[r])

        tab_planes = slots.tile([P, T // 4], I32, name="slot_a", align_bytes=64)
        wg = keep.tile([P, PASSES, N // 2], I32, name="wg", align_bytes=64)
        weight_plane_words = keep.tile([P, PASSES, N // 4], I32, name="weight_plane_words", align_bytes=64)
        weight_planes = weight_plane_words[:].bitcast(U8)

        bias = keep.tile([P, N // P], F32, name="bias")
        vec_rows = slots.tile([P, PASS], F32, name="slot_b", align_bytes=64)
        identity = slots.tile([P, P], F32, name="slot_d", align_bytes=64)
        nc.vector.memset(vec_rows[:], 0.0)
        nc.vector.memset(weight_plane_words[:], 0)
        nc.vector.memset(identity[:], 0.0)
        nc.vector.memset(tab_planes[0:ROWS_FROM, :], 0)
        lifted = [keep.tile([P, S // 4], I32, name="lifted0", align_bytes=64)]
        nc.vector.memset(lifted[0][:], 0)
        make_identity(nc, identity[:], nomemset=True)

        nc.sync.dma_start(tab_planes[ROWS_FROM:P, :], tab_scales.bitcast(I32).rearrange("a q n -> (a q) n"))
        nc.sync.dma_start(wg[:], wg_words.bitcast(I32).rearrange("a p n -> p a n"))
        nc.sync.dma_start(vec_rows[BIAS_ROW : BIAS_ROW + N // P, 0:P], bg.rearrange("(i p) -> i p", p=P))
        nc.sync.dma_start(vec_rows[0:PASSES, :], gain.rearrange("(b c) -> b c", b=PASSES))
        load_weight_planes(wg_scales, 0, range(2))
        table = [load_table(0, "slot_c")]
        load_weight_planes(wg_scales, 0, range(2, PLANE_ROWS))

        bias_turned = psum.tile([P, P], F32, name="bank6")
        nc.tensor.transpose(bias_turned[:], vec_rows[:, 0:P], identity[:])
        gains_turned = psum.tile([P, PACK, P], F32, name=f"bank{GAIN_BANK}")
        for t in range(PACK):
            nc.tensor.transpose(gains_turned[:, t, :], vec_rows[:, t:PASS:PACK], identity[:])
        nc.scalar.copy(bias[:], bias_turned[:, BIAS_ROW : BIAS_ROW + N // P])

        gain_runs = []
        for b in range(PASSES):
            run = keep.tile([P, RUNS[b] * PACK], F32, name=f"gain_run{b}", align_bytes=64)
            nc.scalar.copy(
                run[:].rearrange("p (j t) -> p j t", t=PACK),
                gains_turned[:, :, b].unsqueeze(1).to_broadcast([P, RUNS[b], PACK]),
            )
            gain_runs.append(run)

        w1_words = keep.tile([P, PASSES, H], U32, name="w1_words", align_bytes=64)
        w1_scales = keep.tile([P, PASSES, H], U8, name="w1_scales", align_bytes=64)
        early = keep.tile([P, PASSES * PACK * PASS], BF16, name="early", align_bytes=64)
        rounded = keep.tile([P, (2 * S + HALF) * PACK], BF16, name="rounded", align_bytes=64)

        def grouped(b, a):
            start = a * PASS if b == 0 else a * S
            return (early, rounded)[b][:, start * PACK : (start + PASS) * PACK]

        def round_w1(copy, b, a, m0, m1):
            copy(
                grouped(b, a).rearrange("p (t m j) -> p m j t", t=PACK, j=PACK)[:, m0:m1],
                raw[b, a][:, :, PACK * m0 : PACK * m1].rearrange("p j (m t) -> p m j t", t=PACK),
            )

        def quantize_w1(b, a):
            cols = slice(b * PASS, (b + 1) * PASS)
            nc.vector.quantize_mx(
                out=w1_words[:, a, cols].bitcast(E4M3X4), scales=w1_scales[:, a, cols], in_=grouped(b, a)
            )

        v_words = keep.tile([P, PASSES, S], U32, name="v_words", align_bytes=64)
        v_scales = keep.tile([P, S], U8, name="v_scales", align_bytes=64)
        nc.vector.tensor_copy(v_scales[:], tab_planes[:].bitcast(U8).indirect(offsets[:]))

        def lift(a):
            for r in range(PLANE_ROWS):
                rows = v_scales[ROWS_FROM + 16 * a + r : ROWS_FROM + 16 * (a + 1) : PLANE_ROWS, :]
                nc.sync.dma_start(lifted[a][r:P:32, :], rows.bitcast(I32))

        lift(0)
        table.append(load_table(1, "slot_b"))
        lifted.append(slots.tile([P, S // 4], I32, name="slot_d", align_bytes=64))
        nc.vector.memset(lifted[1][:], 0)
        lift(1)
        nc.vector.tensor_copy(v_words[:, 0, :], table[0][:].bitcast(U32).indirect(offsets[:]))
        staged = slots.tile([P, PASSES * PACK * PASS], F32, name="slot_c", align_bytes=64)
        load_w1(0, staged, [0, PACK * PASS], [[], [PASS // 2]])
        for half in range(2):
            nc.vector.tensor_copy(
                v_words[:, 1, half * HALF : (half + 1) * HALF],
                table[1][:].bitcast(U32).indirect(offsets[:, half * HALF // 16 : (half + 1) * HALF // 16]),
            )
        late = slots.tile([P, TH_LEAD + PASSES * PACK * PASS], F32, name="slot_b", align_bytes=64)
        load_w1(1, late, [TH_LEAD + PACK * PASS, TH_LEAD], [[PASS // 2], []])
        v_planes = [lifted[a][:].bitcast(U8) for a in range(PASSES)]

        gate = [keep.tile([P, 2, 2, BANK], F32, name=f"gate{half}", align_bytes=64) for half in range(2)]
        gate_acc = {}

        def gate_pass(o, a):
            half, i = divmod(o, N // P)
            edges = slice(half * HALF, (half + 1) * HALF)
            if a == 0:
                gate_acc[o] = psum.tile([P, HALF], F32, name=f"bank{GATE_BANKS[o]}")
            nc.tensor.matmul_mx(
                out=gate_acc[o][:],
                lhsT=wg[:, a, P * i // 2 : P * (i + 1) // 2].bitcast(E2M1X4),
                lhsT_scale=weight_planes[:, a, P * i : P * (i + 1)],
                rhs=v_words[:, a, edges].bitcast(E4M3X4),
                rhs_scale=v_planes[a][:, edges],
                start=(a == 0),
                stop=(a == PASSES - 1),
            )

        def sigmoid(o):
            half, i = divmod(o, N // P)
            n, e = divmod(i, 2)
            nc.scalar.activation(
                gate[half][:, :, n, e * CHUNK : (e + 1) * CHUNK],
                gate_acc[o][:].rearrange("p (c j) -> p c j", c=2),
                ACT.Sigmoid,
                bias=bias[:, i : i + 1],
            )

        first_acc = {}
        th = [late, keep.tile([P, S * PACK], F32, name="th1", align_bytes=64)]

        def first_layer(b, n, passes):
            edges = slice(n * P, (n + 1) * P)
            for a in passes:
                if a == 0:
                    first_acc[b, n] = psum.tile([P, PACK, P], F32, name=f"bank{FIRST_BANKS[b][n]}")
                for t in range(PACK):
                    cols = slice(b * PASS + t * P, b * PASS + (t + 1) * P)
                    nc.tensor.matmul_mx(
                        out=first_acc[b, n][:, t, :],
                        lhsT=w1_words[:, a, cols].bitcast(E4M3X4),
                        lhsT_scale=w1_scales[:, a, cols],
                        rhs=v_words[:, a, edges].bitcast(E4M3X4),
                        rhs_scale=v_planes[a][:, edges],
                        start=(a == 0 and t == 0),
                        stop=(a == PASSES - 1 and t == PACK - 1),
                    )

        def tanh(b, n):
            values = th[b][:, n * BANK : (n + 1) * BANK]
            if (b, n) == (1, ON_SCALAR):
                nc.scalar.activation(values, first_acc[b, n][:].rearrange("p t j -> p (t j)"), ACT.Tanh)
            else:
                nc.scalar.activation(
                    values.rearrange("p (j t) -> p j t", t=PACK), first_acc[b, n][:].rearrange("p t j -> p j t"), ACT.Tanh
                )

        scaled = {}

        def gain_on_scalar(n):
            scaled[n] = top.tile([P, PACK, P], BF16, name=f"scaled{n}", align_bytes=64)
            for t in range(PACK):
                values = th[1][:, n * BANK + t * P : n * BANK + (t + 1) * P]
                nc.scalar.activation(scaled[n][:, t, :], values, ACT.Copy, scale=gain_runs[1][:, t : t + 1])

        def weave_on_scalar(n):
            nc.scalar.copy(
                rounded_view(1, n * P, (n + 1) * P).rearrange("p (j t) -> p j t", t=PACK),
                scaled[n][:].rearrange("p t j -> p j t"),
            )

        second = S + HALF - OVERLAP
        places = {
            (0, 0): HALF,
            (1, 0): second - CHUNK, (0, 1): second, (0, 2): second + CHUNK, (0, 3): second + HALF,
            (1, 1): second + CHUNK,
        }

        def rounded_view(b, e0, e1):
            chunk, first = divmod(e0, CHUNK)
            if (b, chunk) in places:
                start = places[b, chunk] + first
                return rounded[:, start * PACK : (start + e1 - e0) * PACK]
            start = (chunk - 2) * (BANK + CHUNK)
            place = gate[0][:].rearrange("p c n j -> p (c n j)")[:, start : start + BANK]
            return place.bitcast(BF16)[:, first * PACK : (first + e1 - e0) * PACK]

        def gain_on_vector(b, e0, e1):
            factor = gains_turned[:, :, b].unsqueeze(1).to_broadcast([P, e1 - e0, PACK])
            nc.vector.tensor_tensor(
                rounded_view(b, e0, e1).rearrange("p (j t) -> p j t", t=PACK),
                th[b][:, e0 * PACK : e1 * PACK].rearrange("p (j t) -> p j t", t=PACK),
                factor,
                MULT,
            )

        def gain_on_gpsimd(b, e0, e1):
            nc.gpsimd.tensor_tensor(
                rounded_view(b, e0, e1), th[b][:, e0 * PACK : e1 * PACK], gain_runs[b][:, 0 : (e1 - e0) * PACK], MULT
            )

        h_of = {}

        def quantize_h(*chunks):
            width = CHUNK * len(chunks)
            b, c = chunks[0]
            words = keep.tile([P, width], U32, name=f"h_words{b}_{c}", align_bytes=64)
            scales = keep.tile([P, width], U8, name=f"h_scales{b}_{c}", align_bytes=64)
            for i, chunk in enumerate(chunks):
                h_of[chunk] = (words[:, i * CHUNK : (i + 1) * CHUNK], scales[:, i * CHUNK : (i + 1) * CHUNK])
            values = rounded_view(b, c * CHUNK, c * CHUNK + width)
            nc.vector.quantize_mx(out=words[:].bitcast(E4M3X4), scales=scales[:], in_=values)

        y_of = {}
        out_view = out.rearrange("(i p) j -> p i j", p=P)

        def second_layer(chunk, b):
            words, scales = h_of[b, chunk]
            last = chunk == 3
            for n in range(2):
                if b == 0 and not last:
                    acc = psum.tile([P, 2, CHUNK], F32, name=f"bank{CHUNK_BANKS[chunk][n]}")
                    y_of[chunk, n] = acc[:].rearrange("p e j -> p (e j)")
                    for e in range(2):
                        y_of[chunk, n, e] = acc[:, e, :]
                for e in range(2):
                    if b == 0 and last:
                        y_of[chunk, n, e] = psum.tile([P, CHUNK], F32, name=f"bank{LAST_BANKS[2 * n + e]}")[:]
                    cols = slice(P * (2 * n + e), P * (2 * n + e + 1))
                    nc.tensor.matmul_mx(
                        out=y_of[chunk, n, e],
                        lhsT=w2[:, b, cols].bitcast(E4M3X4),
                        lhsT_scale=weight_planes[PLANE_ROWS:P, b, cols],
                        rhs=words.bitcast(E4M3X4),
                        rhs_scale=scales,
                        start=(b == 0 and (e == 0 or last)),
                        stop=(b == 1 and (e == 1 or last)),
                    )

        results = {}

        def product(chunk, n, c0=0, c1=BANK, on=None):
            if c0 == 0:
                if on is None:
                    results[chunk, n] = keep.tile([P, BANK], F32, name=f"result{chunk}_{n}")[:]
                else:
                    results[chunk, n] = th[1][:, on * BANK : (on + 1) * BANK]
            sums = y_of[chunk, n] if c1 - c0 == BANK else y_of[chunk, n, c0 // CHUNK]
            factor = gate[chunk // 2][:, chunk % 2, n, c0:c1]
            nc.vector.tensor_tensor(results[chunk, n][:, c0:c1], sums, factor, MULT)

        def store(chunk, n, c0=0, c1=BANK):
            e0, j0 = divmod(c0, CHUNK)
            rows, width = max((c1 - c0) // CHUNK, 1), min(c1 - c0, CHUNK)
            first = chunk * CHUNK + j0
            result = results[chunk, n][:, c0:c1].rearrange("p (e j) -> p e j", e=rows)
            nc.sync.dma_start(out_view[:, 2 * n + e0 : 2 * n + e0 + rows, first : first + width], result)

        for o in range(GAIN_BANK):
            gate_pass(o, 0)
        for o in range(GAIN_BANK):
            gate_pass(o, 1)
        for o in range(4):
            sigmoid(o)
        gate_pass(7, 0)
        gate_pass(7, 1)
        for o in range(4, 8):
            sigmoid(o)

        round_w1(nc.vector.tensor_copy, 0, 0, 0, P)
        round_w1(nc.vector.tensor_copy, 0, 1, 0, P // 2)
        quantize_w1(0, 0)
        for n in range(4):
            first_layer(0, n, [0])
        round_w1(nc.vector.tensor_copy, 0, 1, P // 2, P)
        w2 = slots.tile([P, PASSES, N], I32, name="slot_c", align_bytes=64)
        nc.sync.dma_start(
            w2[:], w2_words.rearrange("a p n i -> a p (n i)").bitcast(I32).rearrange("a p n -> p a n")
        )
        load_weight_planes(w2_scales, PLANE_ROWS)
        quantize_w1(0, 1)
        round_w1(nc.vector.tensor_copy, 1, 0, 0, P // 2)
        for n in range(4):
            first_layer(0, n, [1])
            tanh(0, n)
        round_w1(nc.vector.tensor_copy, 1, 0, P // 2, P)
        gain_on_vector(0, 0, P)
        quantize_w1(1, 0)
        for n in range(4, 8):
            first_layer(0, n, [0, 1])
        tanh(0, 4)
        gain_on_vector(0, P, CHUNK)
        round_w1(nc.scalar.copy, 1, 1, 0, ROUND_ON_SCALAR)
        round_w1(nc.vector.tensor_copy, 1, 1, ROUND_ON_SCALAR, P)
        for n in range(5, 8):
            tanh(0, n)
        for n in range(5):
            first_layer(1, n, [0])
        quantize_h((0, 0))
        quantize_w1(1, 1)

        gain_on_gpsimd(0, CHUNK, CHUNK + SHARES[0])
        gain_on_vector(0, CHUNK + SHARES[0], 6 * P)
        gain_on_vector(0, 6 * P, 7 * P)
        gain_on_vector(0, 7 * P, S)
        for n in range(5):
            first_layer(1, n, [1])
            tanh(1, n)
        second_layer(0, 0)
        gain_on_vector(1, 0, P)
        gain_on_vector(1, P, CHUNK)
        for n in range(5, 7):
            first_layer(1, n, [0, 1])
            tanh(1, n)
        quantize_h((0, 2), (0, 3))
        quantize_h((1, 0), (0, 1))
        second_layer(0, 1)
        first_layer(1, 7, [0, 1])
        tanh(1, 7)
        gain_on_scalar(ON_SCALAR)
        second_layer(1, 0)

        gain_on_gpsimd(1, CHUNK, CHUNK + SHARES[1])
        gain_on_vector(1, CHUNK + SHARES[1], HALF)
        product(0, 0)
        store(0, 0)
        quantize_h((1, 1))
        second_layer(1, 1)
        second_layer(2, 0)
        gain_on_gpsimd(1, HALF, HALF + SHARES[2])
        product(0, 1, on=2)
        store(0, 1)
        weave_on_scalar(ON_SCALAR)
        gain_on_vector(1, HALF + SHARES[2], HALF + CHUNK)
        product(1, 0)
        store(1, 0)
        quantize_h((1, 2))
        second_layer(2, 1)
        second_layer(3, 0)
        gain_on_gpsimd(1, 7 * P, 7 * P + SHARES[3])
        product(1, 1, on=4)
        store(1, 1)
        gain_on_vector(1, 7 * P + SHARES[3], S)
        product(2, 0)
        store(2, 0)
        quantize_h((1, 3))
        second_layer(3, 1)
        product(2, 1, on=7)
        store(2, 1)
        for n in range(2):
            for c0 in range(0, BANK, CHUNK):
                product(3, n, c0, c0 + CHUNK)
                store(3, n, c0, c0 + CHUNK)
